import numpy as np, ml_dtypes
CORES = [24,25,26,27,28,29,30,31]
N = 8
BF = ml_dtypes.bfloat16
V, M, W, TR, RO, CAP = 320, 160, 4096, 4, 3, 28
def spot(a, b, p, q):
    return ((a * (2 * b + 1) >> 4) + a + p * (2 * b + 613) + q * (2 * a + 37)) & (W - 1)
def look(X, a, b, p, q):
    return np.take_along_axis(X, spot(a, b, p, q).reshape(N, 8, 1, 16 * M), 3).reshape(N, 8, 16, 16, M)
def excess(R, z):
    return np.add.reduce(np.maximum(R - z[:, :, :, None, :], 0), axis=2)
def scan(X, G, B, d, z, t):
    ra = np.arange(N)[:, None, None, None]; ga = np.arange(8)[None, :, None, None]; z = z.astype(np.int32)
    n = np.add.reduce((G >= 0).astype(np.int64), axis=2)
    s = np.where((G >= 0) & ((G & 1) == (t & 1)), n[ra, ga, np.maximum(G, 0)], -1)
    e = np.take_along_axis(G, np.argmax(s, axis=2)[:, :, None, :], 2)[:, :, 0]
    e = np.where(np.max(s, axis=2) >= 0, e, -1)
    v = 2 * np.arange(M) + (t & 1); L = G[..., v]; on = L >= 0; a = np.maximum(L, 0)
    old = d[ra, ga, a]; mine = on & (e[ra, ga, a] == v); dv = d[:, :, v][:, :, None, :]
    new = old; pick = look(X, a, v, old, dv); low = excess(pick, z)
    for j in range(1, TR):
        p = (old + j) & 15; R = look(X, a, v, p, dv); x = excess(R, z); w = mine & (x < low)
        low = np.where(w, x, low); new = np.where(w, p, new); pick = np.where(w[:, :, None], R, pick)
    up = np.max(np.where(on[:, :, None], pick, 0), axis=3)
    o = np.take_along_axis(B, a, 3); both = np.concatenate([d, np.roll(d, -1, axis=0)], axis=2); do = both[ra, ga, o]
    dmg = np.where(on, excess(look(X, o, a, do, new), z) - excess(look(X, o, a, do, old), z), -99999)
    k = np.argmax(dmg, axis=2)[:, :, None, :]
    return n[:, :, v], v, L, a, mine, new, up, np.take_along_axis(dmg, k, 2)[:, :, 0], np.take_along_axis(o, k, 2)[:, :, 0]
def graph(rng, S, share):
    m = np.argsort(rng.random((S, V)), axis=1); i = np.arange(S)[:, None]; mate = np.zeros((S, V), np.int64)
    mate[i, m[:, :M]] = m[:, M:]; mate[i, m[:, M:]] = m[:, :M]
    act = 0.3 + 0.7 * rng.random(V); act[rng.random(V) < 0.04] = 0.0
    r = rng.random((S, V))[i, np.minimum(mate, np.arange(V))]
    return np.where(r < share * act * act[mate], mate, -1)
def tidy(tab):
    tab = np.array(tab, np.int64)
    for k in range(1, len(tab)): tab[k] = np.where(np.any(tab[:k] == tab[k], axis=0), -1, tab[k])
    tab = np.take_along_axis(tab, np.argsort(tab < 0, axis=0, kind="stable"), 0)[:16]
    return np.concatenate([tab, np.full((16 - len(tab), V), -1, np.int64)])
def plain(rng, share):
    return tidy(np.concatenate([np.where(rng.random((1, V)) < 0.15, np.arange(V), -1), graph(rng, 16, share)]))
def blocks(rng, own):
    p = rng.permutation(V).reshape(-1, 16); tab = np.zeros((16, V), np.int64)
    o = np.argsort(rng.random((len(p), 16, 16)), axis=2)
    tab[:, p.reshape(-1)] = p[np.arange(len(p))[:, None, None], o].reshape(-1, 16).T
    return tab if own else tidy(np.where(tab == np.arange(V), -1, tab))
def edges():
    return np.concatenate([np.arange(8), np.arange(V - 8, V)])
def corner(rng):
    c = edges(); tab = c[np.argsort(rng.random((16, V)), axis=0)]
    size = rng.choice(np.array([16, 16, 15, 14, 2, 0]), V); size[c] = rng.choice(np.array([16, 16, 15, 14]), 16)
    tab[:2, size == 2] = np.array([[0], [V - 1]])
    for u in (0, V - 1): tab[:, u] = np.concatenate([[V - 2], rng.permutation(c[c != V - 2])])
    tab[:, V - 2] = np.concatenate([[0], rng.permutation(c[1:15]), [V - 1]]); size[[0, V - 2, V - 1]] = 16
    return np.where(np.arange(16)[:, None] < size, tab, -1)
def lift(rng, rec, z, a, v, dv, o, do):
    def ex(x): return np.add.reduce(np.maximum(rec[:, x] - z.reshape((16,) + (1,) * (x.ndim - 1) + (-1,)), 0), axis=0)
    p = np.arange(16)[:, None]; E = ex(spot(a, v, p, dv))
    new = (p + np.argmin(np.stack([np.roll(E, -j, axis=0) for j in range(TR)]), axis=0)) & 15
    F = ex(spot(o[:, None], a, do[:, None], p))
    D = np.take_along_axis(F, np.broadcast_to(new, F.shape), 1) - F
    s = np.where(D > 0, 1 + rng.random(D.shape) + 2 * (np.arange(len(o))[:, None, None] == 0), 0)
    b = np.argmax(s.reshape(-1, s.shape[-1]), axis=0)
    return b & 15, b >> 4
def parts(rng):
    gl = np.stack([np.stack([plain(rng, float(rng.choice(np.array([0.7, 1.0, 1.5, 2.5])))) for g in range(8)]) for r in range(N)])
    rec = (256 * rng.random((N, 8, 16, W)) * (0.4 + 0.6 * rng.random((N, 8, 1, W)))).astype(np.int64)
    val = rng.integers(0, 16, (N, 8, V)); zl = (256 * rng.random((N, 8, 16, M)) ** 1.5).astype(np.int64)
    th = (rng.choice(np.array([4, 40, 200, 1000]), (N, 8, M)) * rng.random((N, 8, M))).astype(np.int64)
    gs = rng.choice(np.array([0.3, 0.5, 0.8]), (N, 8, 1, 1)); full = rng.integers(0, 8, N); gs[np.arange(N), full] = 1.0; th[np.arange(N), full] = rng.integers(0, 8, (N, M))
    nb = rng.integers(0, V, (N, 8, 16, V)) + V * (rng.random((N, 8, 16, V)) < gs)
    return rec, gl, nb, val, zl, th
def pack(rec, gl, nb, val, zl, th):
    return {"rec": rec.reshape(N, 128, W).astype(np.float32).astype(BF), "gl": np.ascontiguousarray(gl.reshape(N, 128, V)).astype(np.int32), "nb": np.ascontiguousarray(nb.reshape(N, 128, V)).astype(np.int32),
            "val": val.astype(np.int32), "zl": zl.reshape(N, 128, M).astype(np.float32).astype(BF), "th": th.astype(np.int32)}
def largest(rec, gl, nb, val, zl):
    return scan(rec.astype(np.int32), gl, nb, val, zl, 0)[7]
def tune(rng, top, want):
    pos = np.argsort(np.argsort(np.where(top > 0, rng.random(top.shape), 2.0), axis=2), axis=2); sel = (pos < want) & (top > 0); coin = rng.random(top.shape)
    low = np.where(coin < 0.5, top - 1, (rng.random(top.shape) * top).astype(np.int64))
    return np.where(sel, low, np.where(coin < 0.1, 4080, np.maximum(top, 0)))
def setup_inputs(rng):
    return pack(*parts(rng))
def setup_inputs_spread(rng):
    rec, gl, nb, val, zl, th = parts(rng)
    rec = (np.exp2(8 * rng.random((N, 8, 1, W))) * rng.random((N, 8, 16, W))).astype(np.int64)
    zl = (np.exp2(8 * rng.random((N, 8, 1, M))) * rng.random((N, 8, 16, M))).astype(np.int64)
    th = np.minimum((np.exp2(12 * rng.random((N, 8, M)) ** 1.5) - 1).astype(np.int64), 4080)
    nb = (2 * V * rng.random((N, 8, 16, V)) ** 1.5).astype(np.int64); val = (16 * rng.random((N, 8, V)) ** 2).astype(np.int64)
    return pack(rec, gl, nb, val, zl, th)
def setup_inputs_ends(rng):
    rec, gl, nb, val, zl, th = parts(rng)
    rec = 255 * np.where(rng.random((N, 8, 1, W)) < 0.8, rng.integers(0, 2, (N, 8, 1, W)), rng.integers(0, 2, (N, 8, 16, W)))
    val = 15 * rng.integers(0, 2, (N, 8, V)); th = 4080 * (rng.random((N, 8, M)) < 0.4).astype(np.int64)
    zl = 255 * np.where(rng.random((N, 8, 1, M)) < 0.6, rng.random((N, 8, 1, M)) < 0.35, rng.random((N, 8, 16, M)) < 0.35).astype(np.int64)
    e = rng.random((N, 8, 16, V)); nb = np.where(e < 0.4, 0, np.where(e < 0.85, 2 * V - 1, nb))
    for r in range(N):
        few = [6, 7] + [int(g) for g in rng.permutation(6)[:2]]
        for g in range(8):
            gl[r, g] = corner(rng) if g in few else tidy(np.concatenate([graph(rng, 14, 1.5), np.zeros((1, V), np.int64), np.full((1, V), V - 1, np.int64)]))
    for g in (6, 7):
        val[:, g, 0] = 15; val[:, g, V - 2] = 0; val[:, g, V - 1] = 0; zl[:, g, :, M - 1] = 0
        th[:, g, M - 1] = np.where(np.arange(N) % 2 == 1, 0, 4080)
        nb[:, g, 15, V - 1] = 2 * V - 1; nb[:, g, 0, 0] = 0 if g == 7 else 2 * V - 1
        hi = [spot(0, V - 2, 15, 0), spot(V - 1, V - 2, 0, 0), spot(2 * V - 1, V - 1, 0, 1), spot(0, 0, 15, 0) if g == 7 else spot(2 * V - 1, 0, 0, 15)]
        lo = [spot(0, V - 2, 0, 0), spot(V - 1, V - 2, 1, 0), spot(2 * V - 1, V - 1, 0, 0), spot(0, 0, 15, 15) if g == 7 else spot(2 * V - 1, 0, 0, 0)]
        for x in lo: rec[:, g, :, x] = 0
        for x in hi: rec[:, g, :, x] = 255
    return pack(rec, gl, nb, val, zl, th)
def setup_inputs_corners(rng):
    rec, gl, nb, val, zl, th = parts(rng); c = edges(); late = []
    for r in range(N):
        for g, k in enumerate(rng.permutation(8)):
            if k == 0:
                ev = np.concatenate([[V - 2], 2 * rng.permutation(M - 1)]); od = 2 * rng.permutation(M) + 1; h = M // 2
                tab = np.full((16, V), -1, np.int64)
                tab[0, ev[:h]] = od[:h]; tab[0, od[:h]] = ev[:h]; tab[0, od[h:]] = ev[:h]; tab[1, od[h:]] = ev[h:]; tab[0, ev[h:]] = od[h:]
                late.append((r, g, ev[:h], od[:h], od[h:]))
            elif k == 1: tab = blocks(rng, True)
            elif k == 2: tab = blocks(rng, False)
            elif k == 3:
                tab = graph(rng, 16, 2.0); tab = tidy(np.where((tab & 1 == 1) & (np.arange(V) & 1 == 1), tab, -1))
            elif k == 4:
                tab = graph(rng, 16, 2.0); off = rng.random(V) < 0.5; tab = tidy(np.where(off | off[tab], -1, tab))
            elif k == 5:
                tab = np.argsort(rng.random((V, V)), axis=1)[:, :16].T; tab = np.where(np.arange(16)[:, None] < rng.integers(0, 17, V), tab, -1)
            elif k == 6:
                tab = c[np.argsort(rng.random((16, V)), axis=0)]; tab[:, c] = np.argsort(rng.random((16, V)), axis=1)[:, :16].T
            else: tab = plain(rng, 1.5)
            gl[r, g] = tab
    m = np.arange(V); e = rng.integers(0, 10, (N, 8, 16, V))
    for k, x in enumerate((0, V - 1, V, 2 * V - 1, m, m + V)): nb = np.where(e == k, x, nb)
    e = rng.integers(0, 4, (N, 8, V)); val = np.where(e == 0, 0, np.where(e == 1, 15, val))
    e = rng.integers(0, 6, (N, 8, 1, M)); zl = np.where(e == 0, 0, np.where(e == 1, 255, zl >> 1))
    want = rng.choice(np.array([0, 1, CAP - 1, CAP, CAP + 1, M]), (N, 8, 1))
    for r, g, v, a, o in late:
        zl[r, g, :, M - 1] = 0; dv = val[r, g, v]; do = val[r, g, o]; q = (np.arange(16) + 1) & 15
        x = spot(a[0], v[0], np.arange(16), dv[0]); y = spot(o[0], a[0], do[0], np.arange(16))
        s = int(np.argmax((x != y) & (x[q] != y[q]))); u = int(q[s])
        rec[r, g, :, int(x[s])] = 255; rec[r, g, :, int(y[u])] = 255; rec[r, g, :, int(x[u])] = 0; rec[r, g, :, int(y[s])] = 0
        p = lift(rng, rec[r, g], zl[r, g][:, v >> 1], a, v, dv, o[None], do[None])[0]
        val[r, g, a] = p; val[r, g, a[0]] = s; nb[r, g][:, a] = o; want[r, g, 0] = M
    th = tune(rng, largest(rec, gl, nb, val, zl), want)
    for r, g, v, a, o in late: th[r, g, M - 1] = 4079
    return pack(rec, gl, nb, val, zl, th)
def setup_inputs_crowd(rng):
    rec, gl, nb, val, zl, th = parts(rng); zl = zl >> 1; ev = 2 * np.arange(M)
    spots = np.array([V, 2 * V - 1, V + M]); cnt = np.array([CAP, CAP + 1, CAP - 1, M, CAP + 1]); want = np.zeros((N, 8, 1), np.int64)
    for r in range(N):
        most = ((2, 3), (4, 5), (3, 2), (5, 4))[r % 4]
        left = [g for g in range(1, 8) if g not in most]
        want[r, left, 0] = cnt if r == 0 else rng.permutation(cnt)
        want[r, most[0], 0] = M; want[r, most[1], 0] = M - 1
        for g in range(8):
            gl[r, g] = plain(rng, 1.5); s = int(rng.choice(spots))
            if g in most:
                od = 2 * rng.permutation(M) + 1; tab = np.full((16, V), -1, np.int64); tab[0, ev] = od; tab[0, od] = ev; gl[r, g] = tab
                o = np.tile(rng.permutation(spots)[:, None], (1, M))
                p, k = lift(rng, rec[r, g], zl[r, g], od, ev, val[r, g, ev], o, val[(r + 1) % N, g][o - V])
                val[r, g, od] = p; nb[r, g] = o[0, 0]; nb[r, g][:, od] = o[k, np.arange(M)]
            elif g == 0: nb[r, g] = (0, V - 1)[r % 2]
            elif g < 5: nb[r, g] = s
            elif g == 5: nb[r, g] = rng.choice(spots, (16, V))
            else: nb[r, g] = np.where(rng.random((16, V)) * CAP < 1, 2 * V - 1 if s == V else V, s)
    top = largest(rec, gl, nb, val, zl); got = np.minimum(np.add.reduce((top > 0).astype(np.int64), axis=2), want[:, :, 0])
    for r in range(N): want[r, 0, 0] = ((31, 0)[r % 2] - int(np.add.reduce(got[r, 1:]))) & 31
    return pack(rec, gl, nb, val, zl, tune(rng, top, want))
def check_inputs(d):
    bad = []
    for k, lo, hi in (("rec", 0, 255), ("gl", -1, V - 1), ("nb", 0, 2 * V - 1), ("val", 0, 15), ("zl", 0, 255), ("th", 0, 4080)):
        x = np.asarray(d[k]).astype(np.float64)
        if not (np.min(x) >= lo and np.max(x) <= hi): bad.append("range of " + k)
        if np.any(x != np.floor(x)): bad.append("whole numbers in " + k)
    g = np.asarray(d["gl"]).reshape(N, 8, 16, V); on = g >= 0; s = np.sort(g, axis=2)
    if np.any(on[:, :, 1:] & ~on[:, :, :-1]): bad.append("gl: a name after an empty slot")
    if np.any((s[:, :, 1:] == s[:, :, :-1]) & (s[:, :, 1:] >= 0)): bad.append("gl: a name twice in one list")
    return bad
def reference(rec, gl, nb, val, zl, th):
    X = rec.astype(np.float32).astype(np.int32).reshape(N, 8, 16, W); G = gl.astype(np.int64).reshape(N, 8, 16, V); B = nb.astype(np.int64).reshape(N, 8, 16, V)
    d = val.astype(np.int64); z = zl.astype(np.float32).astype(np.int32).reshape(N, 8, 16, M); h = th.astype(np.int64); c = np.zeros((N, 1, 1), np.int64)
    for t in range(RO):
        n, v, L, a, mine, new, up, top, who = scan(X, G, B, d, z, t)
        hurt = top > h + (c & 31)
        c = np.add.reduce(hurt.astype(np.int64).reshape(N, 8 * M), axis=1).reshape(N, 1, 1)
        z = np.roll((z + up) >> 1, 1 + t, axis=0)
        w = np.nonzero(mine); d = d + 0; d[w[0], w[1], a[w]] = new[w]
        gh = (hurt & (who >= V)).astype(np.int64); told = (gh == 1) & (np.add.accumulate(gh, axis=2) - gh < CAP)
        w = np.nonzero(told); np.add.at(d, ((w[0] + 1) % N, w[1], who[w] - V), 1); d = d & 15
        w = np.nonzero(hurt & (who < V) & (n < 16) & ~np.any(L == who[:, :, None, :], axis=2))
        G[w[0], w[1], n[w], v[w[2]]] = who[w]
    return {"yl": G.reshape(N, 128, V).astype(np.float32), "yd": d.astype(np.float32), "yz": z.reshape(N, 128, M).astype(np.float32).astype(BF)}

@@ -1,0 +1,737 @@
+from concourse.mybir import AluOpType as A, AxisListType, ActivationFunctionType as F
+
+N, RO, CAP = 8, 3, 28
+BIG = 524288.0
+
+SCRATCH = {}
+VIEW = {}
+_TYPES = {"f": "float32", "i": "int32", "b": "bfloat16", "u": "uint16"}
+_fill = {}
+
+
+def _own(name, width, kind):
+    SCRATCH[name] = ("sbuf", [128, width], _TYPES[kind])
+    VIEW[name] = (name, 0, width)
+
+
+def _put(name, width, kind):
+    tag = "ar" + kind
+    o = _fill.get(tag, 0)
+    VIEW[name] = (tag, o, width)
+    _fill[tag] = o + (width + 15) // 16 * 16
+    SCRATCH[tag] = ("sbuf", [128, _fill[tag]], _TYPES[kind])
+
+
+for _n, _w in (("BLP", 128), ("CM1", 128), ("B1", 128), ("BLC", 128), ("ALL1", 128), ("MIN1", 128), ("NTRI", 128), ("EVW", 128), ("ODW", 128), ("ID", 128),
+               ("VAL", 320), ("NT", 320), ("NH", 320), ("R8", 640), ("SEL8", 128), ("THL", 320), ("SEL0", 128), ("K15", 160), ("K10", 160)):
+    _put(_n, _w, "b")
+for _n, _w in (("ONF", 128), ("LN", 1), ("LN2", 1), ("LNB", 1), ("LNC", 1), ("LNN", 1), ("ON1", 1), ("LK1", 1), ("LC0", 1), ("LC1", 1),
+               ("AC", 20), ("DMP", 20), ("A21", 20), ("CM40", 40),
+               ("MA1", 320), ("M1V", 320), ("V21", 320), ("KC", 320), ("FL", 320), ("IOT", 208),
+               ("AO", 320), ("HA", 320), ("M2A", 320), ("BU", 320), ("INV", 320), ("CT", 320), ("CK", 640), ("NS", 320), ("KB", 40),
+               ("NCF", 320), ("V8F", 160), ("TH2", 20), ("th64", 10), ("YL", 320), ("EMP", 320)):
+    _put(_n, _w, "f")
+for _n, _w in (("LI", 1), ("TI", 20), ("TJ", 20), ("CJ", 14), ("NA", 320), ("PB", 320), ("BUI", 320)):
+    _put(_n, _w, "i")
+for _n, _w in (("AOU", 320), ("COFF", 14)):
+    _put(_n, _w, "u")
+LOCAL = set()
+for _k, _l in (("f", (("T1", 320), ("KL", 320), ("R1", 320), ("A3", 60), ("X1", 20), ("X3", 20), ("X4", 20), ("X5", 20),
+                      ("X6", 20), ("X7", 20), ("X8", 20), ("OF", 20), ("NM", 20), ("DN", 20), ("PX", 40), ("MM2", 40), ("BB2", 40), ("JC", 80), ("J2", 80), ("TP", 100),
+                      ("U", 40), ("B40", 40), ("PQ", 40), ("UC", 160), ("S1", 160), ("QE", 160), ("QY", 160), ("S2", 160), ("HF", 16),
+                      ("CC", 2), ("JA", 160), ("J3", 30), ("NKA", 160), ("p10", 10), ("p16", 10),
+                      ("thr", 10), ("gh", 10), ("xh", 10), ("cs", 10), ("pre", 10), ("prf", 10), ("w", 10), ("cd", 10), ("op", 10),
+                      ("ng", 10), ("n15", 10), ("cc", 10), ("k1", 10), ("k2", 10), ("k4", 10), ("k6", 10), ("k7", 10), ("k8", 10), ("k9", 10))),
+                ("i", (("E1", 20), ("EI", 20), ("E2", 20), ("E3", 20), ("E4", 20), ("X2", 20), ("XS", 20), ("Y2", 20), ("YS", 20), ("CI", 20), ("CS1", 20), ("SI", 20),
+                       ("PJ", 80), ("PJM", 80), ("SGI", 20), ("SGJ", 20), ("T6", 100), ("IX", 100), ("KI", 80), ("KJ", 40), ("KK", 20), ("PN", 20), ("IN", 40), ("IM", 40),
+                       ("UE", 160), ("UF", 160), ("UG", 160), ("y", 10), ("code", 10), ("wi", 10), ("pb", 10), ("h5", 10), ("o2", 10), ("hh", 10),
+                       ("xi", 10), ("jh", 10), ("jl", 10), ("CCI", 1), ("CCJ", 1), ("ZA", 160), ("ZB", 160))),
+                ("b", (("EQ", 320), ("W3", 960), ("OEB", 320), ("SO", 20), ("SGH", 20), ("QD", 640), ("ZE", 320), ("X", 1280), ("XO", 320), ("NXO", 320),
+                       ("XN", 320), ("RN", 320), ("DG", 2560), ("RH", 208), ("LH", 1280), ("JHL", 20), ("JQ", 160), ("NK", 160), ("JB", 480),
+                       ("inj", 10), ("xb", 10))),
+                ("u", (("EU", 20), ("OU", 20), ("PU", 40), ("IXU", 100), ("IXN", 40), ("UI", 160), ("CU", 10)))):
+    for _n, _w in _l:
+        LOCAL.add(_n)
+        for _i in (0, 1):
+            _put(_n + "#%d" % _i, _w, _k)
+for _i in (0, 1):
+    _own("DWa%d" % _i, 832, "b")
+    _own("Ga%d" % _i, 2880, "b")
+    _own("OWa%d" % _i, 2880, "b")
+for _n, _w, _k in (("GLI", 320, "i"), ("NBI", 320, "i"), ("V8I", 640, "i"), ("RW", 4112, "b"), ("SS", 2048, "b"), ("EX", 2048, "b"), ("EH", 512, "f"),
+                   ("FLB", 2560, "b"), ("SG", 5120, "b"), ("GS", 2560, "b"), ("GL1", 336, "f"), ("YD", 320, "f"), ("GDI", 20, "b")):
+    _own(_n, _w, _k)
+for _t in range(RO):
+    _own("DX%d" % _t, 2880, "b")
+    for _n in ("CN", "CL", "GD", "GH"):
+        _own("%s%d" % (_n, _t), 20, "b")
+    _own("ZS%d" % _t, 160, "b")
+for _t in range(RO + 1):
+    _own("Z%d" % _t, 176, "b")
+for _t in range(8):
+    SCRATCH["P%d" % _t] = ("psum", [128, 512], "float32")
+    VIEW["P%d" % _t] = ("P%d" % _t, 0, 512)
+SEMAPHORES = ["sV", "sS", "sT", "sG", "loc", "ac0", "ac1", "ac2", "ag0", "ag1", "ag2", "az1", "az2", "az3",
+              "d_gl", "d_val", "d_th", "d_nb", "d_zl", "d_rec", "d_x1", "d_x2", "d_o0", "d_o1", "d_yl", "d_yd", "d_yz"]
+
+
+def rank_program(g, core, T, topo):
+    rank = T.rank_of(core)
+    if rank is None:
+        return
+    cores = list(T.cores)
+    queue = {"V": g.vector, "S": g.scalar, "T": g.tensor, "G": g, "Y": g.sync}
+    cur = [0]
+    ops = []
+    acc = {}
+
+    def c(name, lo=0, hi=None, step=1, np=128):
+        buf, o, w = VIEW[name + "#%d" % cur[0] if name in LOCAL else name]
+        return (buf, o + lo, o + (w if hi is None else hi), step, np)
+
+    def meet(a, lo, hi, step):
+        if a[1] <= lo or hi <= a[0]:
+            return False
+        return not (a[2] == step and step > 1 and a[0] % step != lo % step)
+
+    def node(q, calls, outs, ins, cost, lat=0.0, **kw):
+        r, w = [], []
+        for v in ins:
+            if isinstance(v, tuple):
+                r += [v[1], v[2]] if v[0] == "@" else [v]
+        for v in outs:
+            if v[0] == "@":
+                w.append(v[1])
+                r.append(v[2])
+            else:
+                w.append(v)
+        k, preds = len(ops), {}
+        for kind, views in ((0, r), (1, w)):
+            for (name, lo, hi, step, np) in views:
+                psum = SCRATCH[name][0] == "psum"
+                for a in acc.get(name, []):
+                    oq = ops[a[4]]["q"]
+                    if psum and oq != q:
+                        preds[a[4]] = True
+                        continue
+                    if not meet(a, lo, hi, step) or (a[3] == 0 and kind == 0):
+                        continue
+                    soft = oq == q and q == "T"
+                    preds[a[4]] = preds.get(a[4], False) or not soft
+        for (name, lo, hi, step, np) in w:
+            acc[name] = [a for a in acc.get(name, []) if not (lo <= a[0] and a[1] <= hi and step == 1 and np == 128)]
+            acc[name].append([lo, hi, step, 1, k])
+        for (name, lo, hi, step, np) in r:
+            acc.setdefault(name, []).append([lo, hi, step, 0, k])
+        d = {"q": q, "calls": calls, "preds": preds, "cost": cost, "lat": lat}
+        d.update(kw)
+        ops.append(d)
+        return k
+
+    def ap(v):
+        name, lo, hi, step, np = v
+        return T[name][0:np, lo:hi:step] if np != 128 else T[name][:, lo:hi:step]
+
+    def opnd(v):
+        if isinstance(v, tuple):
+            return ap(v[1]).indirect(ap(v[2])) if v[0] == "@" else ap(v)
+        return v
+
+    def at(win, off):
+        return ("@", win, off)
+
+    def width(v):
+        return 16 * (v[2][2] - v[2][1]) if v[0] == "@" else -(-(v[2] - v[1]) // v[3])
+
+    def size2(v):
+        return SCRATCH[(v[1] if v[0] == "@" else v)[0]][2] in ("bfloat16", "uint16")
+
+    def cyc(out, ins, two=False):
+        n = width(out)
+        if out[0] == "@":
+            return 60 + 3.0 * n
+        if any(v[0] == "@" for v in ins):
+            return 60 + 1.56 * n
+        if two:
+            return n * (1 if any(SCRATCH[v[0]][0] == "psum" for v in ins) else 2)
+        return n * (0.5 if all(size2(v) for v in [out] + ins) else 1)
+
+    def vec(call, out, ins, cy):
+        node("V", [call], [out], ins, max(64.0, cy) * 0.00104)
+
+    def tt(out, a, b, op):
+        vec(lambda: g.vector.tensor_tensor(opnd(out), opnd(a), opnd(b), op), out, [a, b], cyc(out, [a, b], True))
+
+    def ts(out, a, s1, op0, s2=None, op1=None):
+        if op1 is None:
+            vec(lambda: g.vector.tensor_scalar(opnd(out), opnd(a), opnd(s1), None, op0), out, [a, s1], cyc(out, [a]))
+        else:
+            vec(lambda: g.vector.tensor_scalar(opnd(out), opnd(a), opnd(s1), opnd(s2), op0, op1), out, [a, s1, s2], cyc(out, [a]))
+
+    def cp(out, a):
+        vec(lambda: g.vector.tensor_copy(opnd(out), opnd(a)), out, [a], cyc(out, [a]))
+
+    def act(out, a, scale=1.0, bias=0.0, func=F.Copy):
+        n = width(out)
+        cost = (78 + 1.56 * n if a[0] == "@" else 60 + n) * 0.00104
+        node("S", [lambda: g.scalar.activation(opnd(out), opnd(a), func, bias=opnd(bias), scale=opnd(scale))], [out], [a, bias, scale], cost)
+
+    def scan(out, d0, d1, op0, op1):
+        vec(lambda: g.vector.tensor_tensor_scan(ap(out), ap(d0), ap(d1), 0.0, op0, op1), out, [d0, d1], cyc(out, [d0, d1]))
+
+    def mms(lst):
+        calls = [lambda o=o, l=l, r=r, s=s, e=e: g.tensor.matmul(ap(o), ap(l), ap(r), s, e) for o, l, r, s, e in lst]
+        cost = sum(max(64, width(r)) * (1 if size2(r) else 4) for o, l, r, s, e in lst) * 0.0006
+        node("T", calls, [x[0] for x in lst], [x[1] for x in lst] + [x[2] for x in lst], cost)
+
+    def gps(call, out, ins, base):
+        node("G", [call], [out], ins, base + width(out) * 0.002)
+
+    def iota(v, pattern, base, cm):
+        if SCRATCH[v[0]][2] != "int32":
+            gps(lambda: g.iota(ap(v), pattern, base, cm, allow_small_or_imprecise_dtypes=True), v, [], 0.14)
+        else:
+            gps(lambda: g.iota(ap(v), pattern, base, cm), v, [], 0.14)
+
+    def const(v, x):
+        for lo in range(v[1], v[2], 720 * v[3]):
+            p = (v[0], lo, min(v[2], lo + 720 * v[3]), v[3], v[4])
+            iota(p, [[0, width(p)]], x, 0)
+
+    def select(out, a, pattern, op, base, cm):
+        gps(lambda: g.affine_select(ap(out), ap(a), pattern, op, 0.0, base, cm), out, [a], 0.18)
+
+    def dma(q, out_ap, in_ap, sem, reads, writes, lat):
+        node(q, [lambda: queue[q].dma_start(out_ap, in_ap)], writes, reads, 0.1, lat, sem=sem)
+
+    def send(dst_rank, src_rank, out_v, in_v, sem):
+        dst = cores[dst_rank % N]
+        m = topo.mask(core, dst)
+        rid, pid, _ = topo.addr(dst)
+        k = node("G", [lambda: g.remote_dma(ap(out_v), ap(in_v), T.sem[sem], T.sem.loc, pid, rid, m)], [], [in_v], 0.3,
+                 sent=len(topo.engines(core, dst)))
+        n = len(topo.engines(cores[src_rank % N], core))
+        ops.append({"q": "A", "calls": [], "preds": {k: False}, "cost": 0.0, "lat": 1.8, "sem": sem, "amount": n})
+        acc[out_v[0]] = [a for a in acc.get(out_v[0], []) if not meet(a, out_v[1], out_v[2], 1)]
+        acc[out_v[0]].append([out_v[1], out_v[2], 1, 1, len(ops) - 1])
+
+    SS = lambda b: c("SS", 128 * b, 128 * b + 128)
+    EX = lambda b: c("EX", 128 * b, 128 * b + 128)
+
+    def gather_lanes(out, src, lo, n):
+        mms([(out, SS(b), c(src, lo + b, lo + 16 * n, 16), b == 0, b == 15) for b in range(16)])
+
+    def spread(bank, src, n):
+        mms([(c(bank, b, 16 * n, 16), EX(b), src, True, True) for b in range(16)])
+
+    def half(n, par, d=0):
+        return c(n, d + 160 * par, d + 160 * par + 160)
+
+    def lists(par):
+        return c("GL1", 168 * par, 168 * par + 160)
+
+    dma("Y", ap(c("GLI")), T.gl[:, :], "d_gl", [], [c("GLI")], 2.2)
+    dma("S", ap(c("V8I", 0, 320, 1, 8)), T.val[:, :], "d_val", [], [c("V8I", 0, 320)], 1.9)
+    dma("Y", ap(c("NBI")), T.nb[:, :], "d_nb", [], [c("NBI")], 2.4)
+    dma("S", ap(c("V8I", 320, 480, 1, 8)), T.th[:, :], "d_th", [], [c("V8I", 320, 480)], 1.9)
+    dma("Y", ap(c("Z0", 0, 160)), T.zl[:, :], "d_zl", [], [c("Z0", 0, 160)], 2.5)
+    dma("Y", ap(c("RW", 0, 4096)), T.rec[:, :], "d_rec", [], [c("RW", 0, 4096)], 6.0)
+
+    ingroup = [[-16, 8], [0, 16]]
+    const(c("ALL1"), 1)
+    select(c("BLP"), c("ALL1"), ingroup, A.is_ge, 0, 1)
+    select(c("B1"), c("BLP"), [[16, 8], [0, 16]], A.is_ge, 15, -1)
+    iota(c("CM1"), [[0, 8], [1, 16]], 1, 0)
+    iota(c("LI"), [[0, 1]], 0, 1)
+    iota(c("SEL0", 0, 128, 1, 8), [[-1, 8], [0, 16]], 0, 1)
+    const(c("ONF"), 1)
+    for h in (0, 1):
+        for w in (0, 1):
+            e = 128 * (2 * h + w)
+            select(c("EH", e, e + 128), c("ONF"), [[-32, 4], [1000, 2], [-1, 16]], A.is_equal, -1000 * h - 16 * w, 1)
+    for b in range(16):
+        select(EX(b), c("ALL1"), ingroup, A.is_equal, -b, 1)
+    iota(c("TI"), [[1, 2], [32, 10]], 0, 0)
+    iota(c("TJ"), [[160, 2], [16, 10]], 2560, 0)
+    iota(c("MA1"), [[1, 2], [2, 160]], 1, 0)
+    iota(c("M1V"), [[2, 2], [4, 160]], 613, 0)
+    iota(c("V21"), [[2, 2], [4, 160]], 1, 0)
+    for i in (0, 1):
+        const(c("DWa%d" % i, 320, 512), 0)
+    for t in range(RO + 1):
+        const(c("Z%d" % t, 160, 176), 0)
+    iota(c("KC"), [[0, 20], [1, 16]], 0, 0)
+    const(c("RW", 4096, 4112), 0)
+    zero = c("DX0")
+    vec(lambda: g.vector.memset(ap(zero), 0.0), zero, [], 1440)
+    const(c("MIN1"), -1)
+    select(c("ID"), c("ALL1"), [[-1, 128]], A.is_equal, 0, 1)
+    select(c("NTRI"), c("MIN1"), [[-16, 8], [-1, 16]], A.is_gt, 0, 1)
+    select(c("NTRI"), c("NTRI"), [[16, 8], [0, 16]], A.is_ge, 15, -1)
+    const(c("FLB"), 1)
+    const(c("FLB", 0, 2560, 16), 0)
+    iota(c("IOT", 0, 200), [[0, 10], [1, 20]], 10, 0)
+    const(c("IOT", 200, 208), 0)
+    iota(c("CJ"), [[16, 14]], 0, 0)
+    for i in (1, 0):
+        cur[0] = i
+        const(c("HF"), 0)
+        const(c("JC", 0, 20), 0)
+    for n, s in (("OWa0", "d_o0"), ("OWa1", "d_o1"), ("DX1", "d_x1"), ("DX2", "d_x2")):
+        dma("Y", ap(c(n)), ap(c("DX0")), s, [c("DX0")], [c(n)], 4.0)
+    const(c("GL1", 160, 168), -5)
+    const(c("GL1", 328, 336), -5)
+    for n in ("EVW", "ODW"):
+        const(c(n), 0)
+
+    tt(c("BLC"), c("CM1"), c("B1"), A.mult)
+    ts(c("LI"), c("LI"), 15, A.bitwise_and)
+    cp(c("LN"), c("LI"))
+    ts(c("LN2"), c("LN"), 2.0, A.mult)
+    const(c("LNB"), 4096)
+    const(c("LNC"), int(BIG))
+    const(c("ON1"), 1)
+    ts(c("LNN"), c("LN"), -1.0, A.mult)
+    ts(c("LK1"), c("LN"), 1.0, A.add)
+    ts(c("LC0"), c("LN"), -256.0, A.mult, 3680.0, A.add)
+    ts(c("LC1"), c("LC0"), BIG, A.subtract)
+    for b in range(16):
+        ts(SS(b), c("BLC"), float(b + 1), A.is_equal, 64.0, A.mult)
+
+    def names(par):
+        ts(half("NA", par), lists(par), -1.0, A.add)
+        ts(half("PB", par), half("NA", par), 1, A.bitwise_and)
+        act(half("HA", par), lists(par), 0.5, -0.5)
+        ts(half("AO", par), half("PB", par), 159.5, A.mult)
+        tt(half("AO", par), half("AO", par), half("HA", par), A.add)
+        cp(half("AOU", par), half("AO", par))
+
+    def keys(par, q):
+        if q == 0:
+            ts(half("CT", par), half("PB", par), -BIG - 0.5, A.mult, c("LC0"), A.add)
+            tt(half("CK", par), half("CT", par), half("HA", par), A.add)
+        else:
+            act(half("EMP", par), lists(par), -BIG, c("LNC"), F.Relu)
+            ts(half("CT", par), half("PB", par), BIG - 0.5, A.mult, c("LC1"), A.add)
+            tt(half("CT", par), half("CT", par), half("EMP", par), A.subtract)
+            tt(half("CK", par, 320), half("CT", par), half("HA", par), A.add)
+
+    def places(par):
+        act(half("M2A", par), lists(par), 2.0, 35.0)
+        tt(half("BUI", par), half("NA", par), half("V21", par), A.mult)
+        ts(half("BUI", par), half("BUI", par), 4, A.arith_shift_right)
+        tt(half("BU", par), half("BUI", par), half("NA", par), A.add)
+        act(half("INV", par), lists(par), -4096.0, c("LNB"), F.Relu)
+
+    for par in (0, 1):
+        ts(lists(par), c("GLI", par, 320, 2), 1.0, A.add)
+        act(half("VAL", par), lists(par), 1.0, 0.0, F.Sign)
+    mms([(c("P7", 0, 320), c("B1"), c("VAL"), True, True)])
+    ts(c("NT"), c("P7", 0, 320), 4.0, A.mult, 4.0, A.add)
+    act(c("NS"), c("P7", 0, 320))
+    for par in (0, 1):
+        names(par)
+
+    def sizes_at_entries(split):
+        for lo, hi in ((split, 160), (160, 240), (240, 320)):
+            act(c("SG", 16 * lo, 16 * hi), at(c("NT"), c("AOU", lo, hi)))
+        if split:
+            cp(c("SG", 0, 16 * split), at(c("NT"), c("AOU", 0, split)))
+        for o in (0, 160):
+            mms([(c("P7", o, o + 160), SS(k), c("SG", 16 * o + k, 16 * o + 2560, 16), k == 0, k == 15) for k in range(16)])
+
+    def elect(q):
+        tt(c("KL"), c("P7", 0, 320), c("CK", 320 * q, 320 * q + 320), A.add)
+        v, o = c("T1"), c("KL")
+        vec(lambda: g.vector.transpose(ap(v), ap(o)), v, [o], 320)
+        scan(c("R1"), c("FL"), c("T1"), A.mult, A.max)
+        mms([(c("P2", 64 + w, 84, 2), c("EH", 128 * (2 * h + w), 128 * (2 * h + w) + 128), c("R1", 16 * h + 15, 320, 32), h == 0, h == 1)
+             for w in (0, 1) for h in (0, 1)])
+        cp(c("KB", 20 * q, 20 * q + 20), c("P2", 64, 84))
+
+    NHP, NLP = c("P4", 192, 512), c("P2", 192, 512)
+    for par in (0, 1):
+        cp(half("NCF", par), c("NBI", par, 320, 2))
+    act(c("NH"), c("NCF"))
+    act(NHP, c("NH"))
+    tt(NLP, c("NCF"), NHP, A.subtract)
+    ts(c("SEL8", 0, 128, 1, 8), c("SEL0", 0, 128, 1, 8), 0.0, A.is_equal)
+    cp(c("R8", 0, 320, 1, 8), c("V8I", 0, 320, 1, 8))
+    ts(c("V8F", 0, 160, 1, 8), c("V8I", 320, 480, 1, 8), 1.0 / 16, A.mult)
+    cp(c("R8", 320, 480, 1, 8), c("V8F", 0, 160, 1, 8))
+    tt(c("R8", 480, 640, 1, 8), c("V8F", 0, 160, 1, 8), c("R8", 320, 480, 1, 8), A.subtract)
+    mms([(c("P0", 0, 320), c("SEL8", 0, 128, 1, 8), c("R8", 0, 320, 1, 8), True, True)])
+    mms([(c("P1", 0, 320), c("SEL8", 0, 128, 1, 8), c("R8", 320, 640, 1, 8), True, True)])
+    for par in (0, 1):
+        act(c("DWa0", 160 * par, 160 * par + 160), c("P0", par, 320, 2), 1.0 / 1024)
+    act(c("THL"), c("P1", 0, 320))
+    gather_lanes(c("P2", 0, 20), "DWa0", 0, 20)
+    cp(c("GDI"), c("P2", 0, 20))
+    cp(c("SO"), c("P2", 0, 20))
+    cp(c("PJM", 0, 20), c("P2", 0, 20))
+    send(rank - 1, rank + 1, c("GH0"), c("GDI"), "ag0")
+    gather_lanes(c("P2", 32, 52), "THL", 0, 20)
+    act(c("TH2"), c("P2", 32, 52))
+    tt(c("th64"), c("TH2", 0, 10), c("TH2", 10, 20), A.add)
+    ts(c("thr"), c("th64"), 15.0, A.add)
+    ts(c("AC"), c("TI"), c("LN2"), A.add)
+    ts(c("DMP"), c("TJ"), c("LN"), A.add)
+    ts(c("A21"), c("AC"), 2.0, A.mult, 1.0, A.add)
+    ts(c("CM40", 0, 20), c("AC"), 2.0, A.mult, 37.0, A.add)
+    ts(c("CM40", 20, 40), c("AC"), 2.0, A.mult, 613.0, A.add)
+    ts(c("EVW", 0, 128, 2), c("B1", 0, 128, 2), 1.0 / 512, A.mult)
+    ts(c("ODW", 1, 128, 2), c("B1", 1, 128, 2), 1.0 / 512, A.mult)
+    ts(c("FL"), c("KC"), 0.5, A.is_ge)
+    ts(c("K15"), c("KC", 0, 160), -1.0, A.mult, 15.0, A.add)
+    ts(c("K10"), c("KC", 0, 160), 1024.0, A.mult)
+    ts(c("CJ"), c("CJ"), c("LN"), A.add)
+    ts(c("CJ"), c("CJ"), 3277.0, A.mult)
+    ts(c("CJ"), c("CJ"), 16, A.arith_shift_right)
+    cp(c("COFF"), c("CJ"))
+
+    sizes_at_entries(60)
+    for par in (0, 1):
+        keys(par, 0)
+    elect(0)
+
+    def prep(t):
+        par = t & 1
+        cur[0] = par
+        ts(c("E1"), c("KB", 20 * par, 20 * par + 20), 160.0, A.add)
+        ts(c("EI"), c("E1"), 255, A.bitwise_and)
+        cp(c("EU"), c("EI"))
+        tt(c("EQ"), at(c("GL1", 168 * par, 168 * par + 168), c("EU")), c("MA1"), A.is_equal)
+        tt(c("W3", 0, 320), c("EQ"), NHP, A.mult)
+        tt(c("W3", 320, 640), c("EQ"), NLP, A.mult)
+        act(c("W3", 640, 960), c("EQ"), c("LK1"))
+        gather_lanes(c("P6", 0, 60), "W3", 0, 60)
+        ts(c("X1"), c("EI"), 4.0, A.mult, 2.0 * par + 1.0, A.add)
+        tt(c("X2"), c("AC"), c("X1"), A.mult)
+        ts(c("XS"), c("X2"), 4, A.arith_shift_right)
+        ts(c("MM2", 0, 20), c("EI"), 4.0, A.mult, 2.0 * par + 613.0, A.add)
+        tt(c("BB2", 0, 20), c("XS"), c("AC"), A.add)
+        ts(c("X6"), c("EI"), 16.0, A.mult, -1.0, A.add)
+        ts(c("E3"), c("EI"), 15, A.bitwise_and)
+        ts(c("E4"), c("EI"), 4, A.arith_shift_right)
+        ts(c("X7"), c("E3"), 160.0, A.mult, -1.0, A.add)
+        ts(c("X4"), c("E4"), 16.0, A.mult)
+        tt(c("X7"), c("X7"), c("X4"), A.add)
+        ts(c("A3"), c("P6", 0, 60), 1.0 / 64, A.mult)
+        tt(c("OF"), c("A3", 0, 20), c("A3", 20, 40), A.add)
+        cp(c("CI"), c("OF"))
+        ts(c("X3"), c("OF"), 320.0, A.is_ge, 352.0, A.mult)
+        ts(c("E2"), c("CI"), 1, A.bitwise_and)
+        ts(c("CS1"), c("CI"), 1, A.arith_shift_right)
+        ts(c("X5"), c("E2"), 160.0, A.mult)
+        tt(c("X8"), c("X3"), c("CS1"), A.add)
+        tt(c("X8"), c("X8"), c("X5"), A.add)
+        cp(c("OU"), c("X8"))
+        tt(c("Y2"), c("OF"), c("A21"), A.mult)
+        ts(c("MM2", 20, 40), c("OF"), 2.0, A.mult, 37.0, A.add)
+        ts(c("YS"), c("Y2"), 4, A.arith_shift_right)
+        tt(c("BB2", 20, 40), c("YS"), c("OF"), A.add)
+        ts(c("NM"), c("A3", 40, 60), 0.5, A.is_lt)
+        tt(c("DN"), c("NM"), c("DMP"), A.mult)
+        for j in (1, 2, 3):
+            act(c("JC", 20 * j, 20 * j + 20), c("NM"), BIG, 16.0 * j)
+        for j, x in ((0, "X6"), (20, "X7")):
+            tt(c(x), c(x), c("A3", 40, 60), A.add)
+            tt(c("PX", j, j + 20), c(x), c("DN"), A.max)
+        cp(c("PU"), c("PX"))
+        ow = "OWa%d" % par
+        mms([(c("P6", 128, 448), c("EVW"), c("W3", 0, 320), True, False), (c("P6", 128, 448), c("ODW"), c("W3", 320, 640), False, True)])
+        act(c("OEB"), c("P6", 128, 448))
+        cp(at(c(ow), c("PU", 20, 40)), c("OEB"))
+        mms([(c("P7", 320, 480), SS(b), c(ow, 160 * b, 160 * b + 160), b == 0, False) for b in range(16)]
+            + [(c("P7", 320, 480), c("ID"), c("K10"), False, True)])
+        cur[0] = 1 - par
+
+    prep(0)
+    for par in (0, 1):
+        keys(par, 1)
+    elect(1)
+    cur[0] = 0
+    places(0)
+    places(1)
+
+    for t in range(RO):
+        par = t & 1
+        po = 160 * par
+        cur[0] = par
+        zw = "Z%d" % t
+        dw = "DWa%d" % par
+        if t:
+            cur[0] = 1 - par
+            pn = c("PN")
+            cur[0] = par
+            tt(c("SGI"), c("GH%d" % t), c("P6", 64, 84), A.add)
+            ts(c("SGJ"), c("SGI"), 15, A.bitwise_and)
+            cp(c("SGH"), c("SGJ"))
+            spread("P1", c("SGH"), 20)
+            act(c(dw, 512, 832), c("P1", 0, 320), 1.0 / 1024)
+            tt(c("SI"), pn, c("CL%d" % (t - 1)), A.add)
+            ts(c("PJM", 0, 20), c("SI"), 15, A.bitwise_and)
+            cp(c("SO"), c("PJM", 0, 20))
+            spread("P0", c("SO"), 20)
+            ts(c(dw, 0, 320), c("P0", 0, 320), 1.0 / 1024, A.mult)
+        else:
+            spread("P1", c("GH0"), 20)
+            act(c(dw, 512, 832), c("P1", 0, 320), 1.0 / 1024)
+            spread("P0", c("SO"), 20)
+        cp(c("QD", 0, 320), at(c(dw, po, po + 176), c("EU")))
+        act(c("QD", 320, 640), at(c(dw), c("OU")))
+        gather_lanes(c("P2", 0, 40), "QD", 0, 40)
+        for j in (1, 2, 3):
+            ts(c("PJ", 20 * j, 20 * j + 20), c("PJM", 0, 20), float(j), A.add)
+        ts(c("PJM", 20, 80), c("PJ", 20, 80), 15, A.bitwise_and)
+        for j in range(4):
+            tt(c("TP", 20 * j, 20 * j + 20), c("PJM", 20 * j, 20 * j + 20), c("MM2", 0, 20), A.mult)
+        tt(c("TP", 80, 100), c("PJM", 0, 20), c("MM2", 20, 40), A.mult)
+        tt(c("J2"), c("JC"), c("PJM"), A.add)
+        tt(c("U"), c("P2", 0, 40), c("CM40"), A.mult)
+        tt(c("B40"), c("BB2"), c("U"), A.add)
+        for j in range(5):
+            tt(c("T6", 20 * j, 20 * j + 20), c("TP", 20 * j, 20 * j + 20), c("B40", j // 4 * 20, j // 4 * 20 + 20), A.add)
+        ts(c("IX"), c("T6"), 4095, A.bitwise_and)
+        cp(c("IXU"), c("IX"))
+        act(c("ZE"), at(c(zw), c("EU")))
+        for j in range(4):
+            tt(c("X", 320 * j, 320 * j + 320), at(c("RW", 0, 4096), c("IXU", 20 * j, 20 * j + 20)), c("ZE"), A.max)
+        gather_lanes(c("P3", 0, 80), "X", 0, 80)
+        for hf in (0, 40, 80, 120):
+            act(c("DG", 16 * hf, 16 * hf + 640), at(c(dw, 0, 320), c("AOU", po + hf, po + hf + 40)))
+        mms([(c("P4", 0, 160), SS(k), c("DG", k, 2560, 16), k == 0, k == 15) for k in range(16)])
+        tt(c("P0", 320, 480), half("M2A", par), c("P0", po, po + 160), A.mult)
+        tt(c("UC"), half("BU", par), c("P0", 320, 480), A.add)
+        tt(c("P3", 320, 480), half("M1V", par), c("P4", 0, 160), A.mult)
+        tt(c("UE"), c("UC"), c("P3", 320, 480), A.add)
+        ts(c("UF"), c("UE"), 4095, A.bitwise_and)
+        tt(c("UG"), c("UF"), half("INV", par), A.max)
+        cp(c("UI"), c("UG"))
+        gw = "Ga%d" % par
+        tt(c("XO"), at(c("RW", 0, 4096), c("IXU", 80, 100)), c("ZE"), A.max)
+        act(c("NXO"), c("XO"), -1.0)
+        tt(c("KI"), c("P3", 0, 80), c("J2"), A.add)
+        tt(c("KJ"), c("KI", 0, 40), c("KI", 40, 80), A.min)
+        tt(c("KK"), c("KJ", 0, 20), c("KJ", 20, 40), A.min)
+        ts(c("PN"), c("KK"), 15, A.bitwise_and)
+        tt(c("PQ", 20, 40), c("PN"), c("MM2", 20, 40), A.mult)
+        tt(c("PQ", 0, 20), c("PN"), c("MM2", 0, 20), A.mult)
+        tt(c("IN"), c("PQ"), c("B40"), A.add)
+        ts(c("IM"), c("IN"), 4095, A.bitwise_and)
+        cp(c("IXN"), c("IM"))
+        if t < RO - 1:
+            cp(c("GD%d" % t), c("PN"))
+            send(rank - 1, rank + 1, c("GH%d" % (t + 1)), c("GD%d" % t), "ag%d" % (t + 1))
+        tt(c("XN"), at(c("RW", 0, 4096), c("IXN", 20, 40)), c("ZE"), A.max)
+        tt(at(c("DX%d" % t), c("PU", 20, 40)), c("XN"), c("NXO"), A.add)
+        mms([(c("P5", 0, 160), SS(b), c("DX%d" % t, 160 * b, 160 * b + 160), b == 0, False) for b in range(16)]
+            + [(c("P5", 0, 160), c("ID"), c("K15"), False, True)])
+        act(c("RN"), at(c("RW", 0, 4096), c("IXN", 0, 20)))
+        for hf in (0, 80):
+            act(c(gw, 16 * hf, 16 * hf + 1280), at(c("RW"), c("UI", hf, hf + 80)))
+        scan(c("S1"), c("FL", 0, 160), c("P5", 0, 160), A.mult, A.max)
+        tt(c("QE"), c("S1"), c("P5", 0, 160), A.is_equal)
+        tt(c("QY"), c("QE"), c("P7", 320, 480), A.mult)
+        scan(c("S2"), c("FL", 0, 160), c("QY"), A.mult, A.max)
+        tt(c("inj"), c("S1", 15, 160, 16), c("thr"), A.is_gt)
+        cp(c("y"), c("S2", 15, 160, 16))
+        ts(c("code"), c("y"), 1023, A.bitwise_and)
+        ts(c("gh"), c("code"), 320.0, A.is_ge)
+        if t == 1:
+            names(0)
+            keys(0, 0)
+            places(0)
+            sizes_at_entries(0)
+            elect(0)
+        tt(c("xb"), c("inj"), c("gh"), A.mult)
+        mms([(c("P5", 192, 202), c("B1"), c("xb"), True, True), (c("P5", 208, 218), c("NTRI"), c("xb"), True, True)])
+        ts(c("wi"), c("code"), 1, A.arith_shift_right, 15, A.bitwise_and)
+        ts(c("pb"), c("code"), 1, A.bitwise_and)
+        ts(c("p10"), c("pb"), 10.0, A.mult)
+        ts(c("w"), c("wi"), 1.0, A.add)
+        ts(c("h5"), c("code"), 5, A.arith_shift_right)
+        tt(c("hh"), c("h5"), c("p10"), A.add)
+        for x in range(10):
+            ts(c("LH", 128 * x, 128 * x + 128), c("BLC"), c("w", x, x + 1), A.is_equal)
+        tt(c("xh"), c("xb"), c("hh"), A.mult)
+        scan(c("cs"), c("ONF", 0, 10), c("P5", 192, 202), A.mult, A.add)
+        tt(c("pre"), c("cs"), c("P5", 208, 218), A.add)
+        ts(c("prf"), c("pre"), float(CAP), A.is_le)
+        tt(c("HF", 0, 10), c("prf"), c("xh"), A.mult)
+        tt(c("RH"), at(c("HF"), c("COFF", 0, 13)), c("IOT"), A.is_equal)
+        mms([(c("P6", 64, 84), c("LH", 128 * x, 128 * x + 128), c("RH", 20 * x, 20 * x + 20), x == 0, x == 9) for x in range(10)])
+        cp(c("CN%d" % t), c("P6", 64, 84))
+        send(rank + 1, rank - 1, c("CL%d" % t), c("CN%d" % t), "ac%d" % t)
+        cp(at(c(gw), c("PU", 0, 20)), c("RN"))
+        scan(c("GS"), c("FLB"), c(gw, 0, 2560), A.mult, A.max)
+        tt(c("ZA"), c(zw, 0, 160), c("GS", 15, 2560, 16), A.add)
+        ts(c("ZB"), c("ZA"), 1, A.arith_shift_right)
+        cp(c("ZS%d" % t), c("ZB"))
+        send(rank + 1 + t, rank - 1 - t, c("Z%d" % (t + 1), 0, 160), c("ZS%d" % t), "az%d" % (t + 1))
+        l1, ns, last = lists(par), half("NS", par), t == RO - 1
+        act(c("NKA"), ns, 1.0, c("LNN"), F.Abs)
+        act(c("NK"), c("NKA"), -1.0, c("ON1"), F.Relu)
+        act(c("JB", 160, 320), ns)
+        gather_lanes(c("P2", 144, 154), "JB", 160, 10)
+        ts(c("n15"), c("P2", 144, 154), 15.5 * 1024, A.is_le)
+        ts(c("ng"), c("gh"), 0.5, A.is_lt)
+        tt(c("cc"), c("inj"), c("n15"), A.mult)
+        tt(c("cd"), c("cc"), c("ng"), A.mult)
+        ts(c("op"), c("code"), 1.0, A.add)
+        ts(c("o2"), c("code"), 1, A.arith_shift_right)
+        tt(c("xi"), c("op"), c("cd"), A.mult)
+        ts(c("jh"), c("xi"), 496, A.bitwise_and)
+        ts(c("jl"), c("xi"), 15, A.bitwise_and)
+        cp(c("JHL", 0, 10), c("jh"))
+        cp(c("JHL", 10, 20), c("jl"))
+        mms([(c("P1", b, 160, 16), EX(b), c("JHL", 10 * h, 10 * h + 10), h == 0, h == 1) for b in range(16) for h in (0, 1)])
+        tt(c("JQ"), l1, c("P1", 0, 160), A.is_equal)
+        mms([(c("P3", 128, 288), c("B1"), c("JQ"), True, True)])
+        if not last:
+            ts(c("p16"), c("pb"), 160.0, A.mult)
+            tt(c("k1"), c("p16"), c("o2"), A.add)
+            ts(c("k1"), c("k1"), 319.0, A.min)
+            cp(c("CU"), c("k1"))
+            act(c("JB", 0, 160), at(c("NT"), c("CU")))
+        ts(c("JA"), c("P3", 128, 288), 0.5, A.is_lt)
+        jv, jw = c("P1", 160, 320), c("P1", 320, 480)
+        tt(jv, c("JA"), c("P1", 0, 160), A.mult)
+        if not last:
+            act(c("JB", 320, 480), jv, 1.0, 0.0, F.Sign)
+            gather_lanes(c("P2", 96, 126), "JB", 0, 30)
+        tt(jw, c("NK"), jv, A.mult)
+        tt(l1, l1, jw, A.add)
+        act(c("YL", par, 320, 2), l1, 1.0, -1.0)
+        if not last:
+            if t == 0:
+                tt(ns, ns, c("JB", 320, 480), A.add)
+            act(c("J3"), c("P2", 96, 126))
+            ts(c("k2"), c("J3", 10, 20), -0.25, A.mult, 3680.0, A.add)
+            ts(c("k4"), c("pb"), float(1 - par), A.is_equal, 1.0 / 1024, A.mult)
+            tt(c("k6"), c("k2"), c("J3", 0, 10), A.add)
+            tt(c("k7"), c("k6"), c("o2"), A.add)
+            tt(c("k8"), c("k4"), c("J3", 20, 30), A.mult)
+            tt(c("k9"), c("k7"), c("k8"), A.mult)
+            kb = c("KB", 20 * (1 - par) + 10 * par, 20 * (1 - par) + 10 * par + 10)
+            tt(kb, kb, c("k9"), A.max)
+            mms([(c("P5", 224, 234), c("ALL1"), c("inj"), True, True)])
+            o, i = c("CC", 0, 1), c("P5", 224, 234)
+            vec(lambda o=o, i=i: g.vector.tensor_reduce(ap(o), ap(i), AxisListType.X, A.add), o, [i], 10)
+            cp(c("CCI"), o)
+            ts(c("CCJ"), c("CCI"), 31, A.bitwise_and)
+            ts(c("CC", 1, 2), c("CCJ"), 64.0, A.mult, 15.0, A.add)
+            inc = c("CC", 1, 2)
+            cur[0] = 1 - par
+            ts(c("thr"), c("th64"), inc, A.add)
+            prep(t + 1)
+            if t == 0:
+                cur[0] = 0
+                ts(c("NT", 0, 160), c("NS", 0, 160), 4.0, A.mult, 4.0, A.add)
+
+    cur[0] = (RO - 1) & 1
+    pn = c("PN")
+    dma("Y", T.yl[:, :], ap(c("YL")), "d_yl", [c("YL")], [], 2.2)
+    cur[0] = RO & 1
+    tt(c("SI"), pn, c("CL%d" % (RO - 1)), A.add)
+    ts(c("PJM", 0, 20), c("SI"), 15, A.bitwise_and)
+    cp(c("SO"), c("PJM", 0, 20))
+    spread("P0", c("SO"), 20)
+    for par in (0, 1):
+        cp(c("YD", par, 320, 2), c("P0", 160 * par, 160 * par + 160))
+    dma("S", T.yd[:, :], T["YD"][0:128:16, :], "d_yd", [c("YD")], [], 2.0)
+    dma("Y", T.yz[:, :], ap(c("Z%d" % RO, 0, 160)), "d_yz", [c("Z%d" % RO, 0, 160)], [], 2.2)
+
+    succ = [[] for _ in ops]
+    for k, d in enumerate(ops):
+        for p in d["preds"]:
+            succ[p].append(k)
+    prio = [0.0] * len(ops)
+    for k in range(len(ops) - 1, -1, -1):
+        d = ops[k]
+        prio[k] = d["cost"] + d["lat"] + max([prio[s] + 0.06 for s in succ[k]], default=0.0)
+    left = [len(d["preds"]) for d in ops]
+    ready = [0.0] * len(ops)
+    pool = {q: [] for q in "VSTGYA"}
+    for k, d in enumerate(ops):
+        if not left[k]:
+            pool[d["q"]].append(k)
+    free = {q: 0.0 for q in pool}
+    order = []
+    while len(order) < len(ops):
+        best = None
+        for q in pool:
+            if not pool[q]:
+                continue
+            start = lambda k: ready[k] if q == "A" else max(free[q], ready[k])
+            k = min(pool[q], key=lambda k: (start(k), -prio[k], k))
+            for _ in range(6):
+                s = start(k)
+                up = [j for j in pool[q] if prio[j] > prio[k] and s < start(j) < s + 0.6 * ops[k]["cost"]]
+                if q == "A" or not up:
+                    break
+                j = max(up, key=lambda j: (prio[j], -j))
+                fit = [i for i in pool[q] if i != k and start(i) + ops[i]["cost"] <= start(j)]
+                k = max(fit, key=lambda i: (prio[i], -i)) if fit else j
+            key = (start(k), -prio[k], k)
+            if best is None or key < best[0]:
+                best = (key, q, k)
+        (s, _, k), q, _ = best
+        pool[q].remove(k)
+        d = ops[k]
+        free[q] = s + d["cost"] + 0.012
+        end = s + d["cost"] + d["lat"]
+        order.append(k)
+        for x in succ[k]:
+            gap = 0.06 if ops[x]["preds"][k] else 0.0
+            ready[x] = max(ready[x], end + gap)
+            left[x] -= 1
+            if not left[x]:
+                pool[ops[x]["q"]].append(x)
+
+    count = {q: 0 for q in "VSTG"}
+    clock = {q: {} for q in "VSTGY"}
+    token = [None] * len(ops)
+    sent = 0
+    for k in order:
+        d = ops[k]
+        q = d["q"]
+        if q == "A":
+            token[k] = (d["sem"], d["amount"], {d["sem"]: d["amount"]})
+            continue
+        ck, best = clock[q], {}
+        for p, hard in d["preds"].items():
+            if hard:
+                s, v, kk = token[p]
+                if ck.get(s, 0) < v and best.get(s, (0, None))[0] < v:
+                    best[s] = (v, kk)
+        for s in list(best):
+            v = best[s][0]
+            if any(s2 != s and k2.get(s, 0) >= v for s2, (v2, k2) in best.items()):
+                del best[s]
+        for s, (v, kk) in best.items():
+            queue[q].wait_ge(T.sem[s], v)
+            for s2, v2 in kk.items():
+                ck[s2] = max(ck.get(s2, 0), v2)
+        for call in d["calls"]:
+            if "sem" in d:
+                call().then_inc(T.sem[d["sem"]], 16)
+            elif "sent" in d:
+                call()
+                sent += d["sent"]
+            else:
+                count[q] += 1
+                call().then_inc(T.sem["s" + q], 1)
+        kk = dict(ck)
+        if "sem" in d:
+            kk[d["sem"]] = 16
+            token[k] = (d["sem"], 16, kk)
+        elif "sent" not in d:
+            kk["s" + q] = count[q]
+            token[k] = ("s" + q, count[q], kk)
+    g.wait_ge(T.sem.loc, sent)
+    for s in ("d_yl", "d_yd", "d_yz"):
+        g.wait_ge(T.sem[s], 16)
+    for q in "VSTG":
+        if clock["G"].get("s" + q, 0) < count[q]:
+            g.wait_ge(T.sem["s" + q], count[q])

@@ -1,11 +1,12 @@
 from concourse.mybir import AluOpType as A, AxisListType, ActivationFunctionType as F
 
 N, RO, CAP = 8, 3, 28
-BIG = 524288.0
+OFF = 32
+ROUND = 12582912.0
 
 SCRATCH = {}
 VIEW = {}
-_TYPES = {"f": "float32", "i": "int32", "b": "bfloat16", "u": "uint16"}
+_TYPES = {"f": "float32", "i": "int32", "b": "bfloat16", "u": "uint16", "h": "float16"}
 _fill = {}
 
 
@@ -22,57 +23,54 @@ def _put(name, width, kind):
     SCRATCH[tag] = ("sbuf", [128, _fill[tag]], _TYPES[kind])
 
 
-for _n, _w in (("BLP", 128), ("CM1", 128), ("B1", 128), ("BLC", 128), ("ALL1", 128), ("MIN1", 128), ("NTRI", 128), ("EVW", 128), ("ODW", 128), ("ID", 128),
-               ("VAL", 320), ("NT", 320), ("NH", 320), ("R8", 640), ("SEL8", 128), ("THL", 320), ("SEL0", 128), ("K15", 160), ("K10", 160)):
-    _put(_n, _w, "b")
-for _n, _w in (("ONF", 128), ("LN", 1), ("LN2", 1), ("LNB", 1), ("LNC", 1), ("LNN", 1), ("ON1", 1), ("LK1", 1), ("LC0", 1), ("LC1", 1),
-               ("AC", 20), ("DMP", 20), ("A21", 20), ("CM40", 40),
-               ("MA1", 320), ("M1V", 320), ("V21", 320), ("KC", 320), ("FL", 320), ("IOT", 208),
-               ("AO", 320), ("HA", 320), ("M2A", 320), ("BU", 320), ("INV", 320), ("CT", 320), ("CK", 640), ("NS", 320), ("KB", 40),
-               ("NCF", 320), ("V8F", 160), ("TH2", 20), ("th64", 10), ("YL", 320), ("EMP", 320)):
-    _put(_n, _w, "f")
-for _n, _w in (("LI", 1), ("TI", 20), ("TJ", 20), ("CJ", 14), ("NA", 320), ("PB", 320), ("BUI", 320)):
-    _put(_n, _w, "i")
-for _n, _w in (("AOU", 320), ("COFF", 14)):
-    _put(_n, _w, "u")
+_CONST = (("b", (("SS", 144), ("IDW", 144), ("WM", 144), ("WP", 144), ("WD", 144), ("WN", 144), ("B1", 128), ("B1N", 128), ("OD", 128), ("DPM", 128), ("ID8", 128),
+                 ("SHB", 128), ("BLC", 128), ("TRA", 128), ("TRI", 128), ("ALL1", 512), ("HI", 320), ("LO", 320), ("PI", 320), ("C16", 320), ("DUM", 32), ("D256", 32),
+                 ("R16", 320), ("VALN", 320), ("FL", 160), ("DR", 160), ("K512", 160), ("K15", 160), ("C185", 160), ("ST", 352))),
+          ("f", (("WI", 144), ("BI", 128), ("ID32", 128), ("PF", 1), ("LN", 1), ("LG", 1), ("LG20", 1), ("cu", 1), ("c3", 1), ("c4", 1), ("cd", 1), ("cn", 1), ("cs", 1),
+                 ("ck", 1), ("cj", 1), ("cp", 1), ("TI", 20), ("AC", 20), ("A17", 20), ("CM40", 40), ("MAJ", 320), ("M1V", 320), ("IOT", 208), ("CJF", 14), ("APR", 320),
+                 ("R1", 320), ("AB", 320), ("R2", 320), ("BASE", 20), ("th64", 10), ("ON10", 10), ("YL", 320))),
+          ("i", (("PI32", 1), ("LI", 1), ("LGI", 1), ("CJ", 14), ("KB0", 20), ("KB1", 20), ("KB2", 20))),
+          ("u", (("AOU", 320), ("COFF", 14))),
+          ("h", (("NBH", 320), ("K10", 160), ("VY", 320))))
+for _k, _l in _CONST:
+    for _n, _w in _l:
+        _put(_n, _w, _k)
 LOCAL = set()
-for _k, _l in (("f", (("T1", 320), ("KL", 320), ("R1", 320), ("A3", 60), ("X1", 20), ("X3", 20), ("X4", 20), ("X5", 20),
-                      ("X6", 20), ("X7", 20), ("X8", 20), ("OF", 20), ("NM", 20), ("DN", 20), ("PX", 40), ("MM2", 40), ("BB2", 40), ("JC", 80), ("J2", 80), ("TP", 100),
-                      ("U", 40), ("B40", 40), ("PQ", 40), ("UC", 160), ("S1", 160), ("QE", 160), ("QY", 160), ("S2", 160), ("HF", 16),
-                      ("CC", 2), ("JA", 160), ("J3", 30), ("NKA", 160), ("p10", 10), ("p16", 10),
-                      ("thr", 10), ("gh", 10), ("xh", 10), ("cs", 10), ("pre", 10), ("prf", 10), ("w", 10), ("cd", 10), ("op", 10),
-                      ("ng", 10), ("n15", 10), ("cc", 10), ("k1", 10), ("k2", 10), ("k4", 10), ("k6", 10), ("k7", 10), ("k8", 10), ("k9", 10))),
-                ("i", (("E1", 20), ("EI", 20), ("E2", 20), ("E3", 20), ("E4", 20), ("X2", 20), ("XS", 20), ("Y2", 20), ("YS", 20), ("CI", 20), ("CS1", 20), ("SI", 20),
-                       ("PJ", 80), ("PJM", 80), ("SGI", 20), ("SGJ", 20), ("T6", 100), ("IX", 100), ("KI", 80), ("KJ", 40), ("KK", 20), ("PN", 20), ("IN", 40), ("IM", 40),
-                       ("UE", 160), ("UF", 160), ("UG", 160), ("y", 10), ("code", 10), ("wi", 10), ("pb", 10), ("h5", 10), ("o2", 10), ("hh", 10),
-                       ("xi", 10), ("jh", 10), ("jl", 10), ("CCI", 1), ("CCJ", 1), ("ZA", 160), ("ZB", 160))),
-                ("b", (("EQ", 320), ("W3", 960), ("OEB", 320), ("SO", 20), ("SGH", 20), ("QD", 640), ("ZE", 320), ("X", 1280), ("XO", 320), ("NXO", 320),
-                       ("XN", 320), ("RN", 320), ("DG", 2560), ("RH", 208), ("LH", 1280), ("JHL", 20), ("JQ", 160), ("NK", 160), ("JB", 480),
-                       ("inj", 10), ("xb", 10))),
-                ("u", (("EU", 20), ("OU", 20), ("PU", 40), ("IXU", 100), ("IXN", 40), ("UI", 160), ("CU", 10)))):
+for _k, _l in (("f", (("EF", 20), ("V613", 20), ("V17", 20), ("X6", 20), ("MM", 100), ("BB", 40), ("pt", 20), ("pu", 20), ("PX", 20), ("U", 40), ("B60", 60), ("KIB", 40),
+                      ("PQ", 40), ("T1", 160), ("UE", 160), ("S1", 160), ("QE", 160), ("QY", 160), ("S2", 160), ("ZF", 160), ("P1C", 160), ("HF", 16), ("thr", 10),
+                      ("xi", 10), ("w", 10), ("t20", 10), ("h", 10), ("prf", 10), ("jk", 10), ("CC", 2))),
+                ("i", (("EI", 20), ("SI", 20), ("PJ", 20), ("SGI", 20), ("SGJ", 20), ("T6", 100), ("IX", 100), ("KJ", 40), ("KK", 20), ("PN", 20), ("IN", 40), ("IM", 40),
+                       ("UQ", 160), ("UF", 160), ("y", 10), ("code", 10), ("wi", 10), ("CCI", 1), ("CCJ", 1))),
+                ("b", (("XB", 100), ("SGN", 60), ("SGH", 20), ("QD", 640), ("ZE", 320), ("X", 1280), ("XO", 320), ("NXO", 320), ("XN", 320), ("RN", 320), ("OH", 320),
+                       ("OEB", 320), ("RH", 208), ("LH", 1280), ("JQ", 160), ("JB", 160), ("inj", 10), ("xb", 10), ("cs10", 10))),
+                ("h", (("W3", 960), ("xj", 10))),
+                ("u", (("EOU", 40), ("PU", 20), ("IXU", 100), ("IXN", 40), ("UI", 160), ("CU", 10)))):
     for _n, _w in _l:
         LOCAL.add(_n)
         for _i in (0, 1):
             _put(_n + "#%d" % _i, _w, _k)
 for _i in (0, 1):
-    _own("DWa%d" % _i, 832, "b")
-    _own("Ga%d" % _i, 2880, "b")
-    _own("OWa%d" % _i, 2880, "b")
-for _n, _w, _k in (("GLI", 320, "i"), ("NBI", 320, "i"), ("V8I", 640, "i"), ("RW", 4112, "b"), ("SS", 2048, "b"), ("EX", 2048, "b"), ("EH", 512, "f"),
-                   ("FLB", 2560, "b"), ("SG", 5120, "b"), ("GS", 2560, "b"), ("GL1", 336, "f"), ("YD", 320, "f"), ("GDI", 20, "b")):
+    _own("DW%d" % _i, 672, "b")
+    _own("GL%d" % _i, 352, "f")
+    _own("GW%d" % _i, 2880, "b")
+    _own("OW%d" % _i, 2880, "b")
+    _own("ZS%d" % _i, 352, "b")
+for _n, _w, _k in (("GLI", 320, "i"), ("NBI", 320, "i"), ("V5", 320, "i"), ("VAI", 20, "i"), ("THI", 10, "i"), ("ZL", 160, "b"), ("RW", 4112, "b"), ("EX", 2048, "b"),
+                   ("FLB", 2560, "b"), ("SG", 5120, "b"), ("GS", 2560, "b"), ("YD", 20, "f"), ("GDI", 20, "b"), ("ZS2", 160, "b"), ("Z3", 160, "b")):
     _own(_n, _w, _k)
 for _t in range(RO):
     _own("DX%d" % _t, 2880, "b")
+    _own("Z%d" % _t, 352, "b")
     for _n in ("CN", "CL", "GD", "GH"):
         _own("%s%d" % (_n, _t), 20, "b")
-    _own("ZS%d" % _t, 160, "b")
-for _t in range(RO + 1):
-    _own("Z%d" % _t, 176, "b")
 for _t in range(8):
     SCRATCH["P%d" % _t] = ("psum", [128, 512], "float32")
     VIEW["P%d" % _t] = ("P%d" % _t, 0, 512)
 SEMAPHORES = ["sV", "sS", "sT", "sG", "loc", "ac0", "ac1", "ac2", "ag0", "ag1", "ag2", "az1", "az2", "az3",
-              "d_gl", "d_val", "d_th", "d_nb", "d_zl", "d_rec", "d_x1", "d_x2", "d_o0", "d_o1", "d_yl", "d_yd", "d_yz"]
+              "d_gl", "d_v5", "d_va", "d_th", "d_nb", "d_zl", "d_rec", "d_a", "d_b", "d_x1", "d_x2", "d_o0", "d_o1", "d_yl", "d_yd", "d_yz"]
+
+CYC, PE, GAP, HOP = 0.00095, 0.00065, 0.09, 1.5
+FIRST = "VSSVSVSS"
 
 
 def rank_program(g, core, T, topo):
@@ -85,9 +83,9 @@ def rank_program(g, core, T, topo):
     ops = []
     acc = {}
 
-    def c(name, lo=0, hi=None, step=1, np=128):
+    def c(name, lo=0, hi=None, step=1):
         buf, o, w = VIEW[name + "#%d" % cur[0] if name in LOCAL else name]
-        return (buf, o + lo, o + (w if hi is None else hi), step, np)
+        return (buf, o + lo, o + (w if hi is None else hi), step)
 
     def meet(a, lo, hi, step):
         if a[1] <= lo or hi <= a[0]:
@@ -107,21 +105,23 @@ def rank_program(g, core, T, topo):
                 w.append(v)
         k, preds = len(ops), {}
         for kind, views in ((0, r), (1, w)):
-            for (name, lo, hi, step, np) in views:
+            for (name, lo, hi, step) in views:
                 psum = SCRATCH[name][0] == "psum"
                 for a in acc.get(name, []):
                     oq = ops[a[4]]["q"]
                     if psum and oq != q:
                         preds[a[4]] = True
                         continue
+                    if psum and q == "T":
+                        preds[a[4]] = preds.get(a[4], False)
+                        continue
                     if not meet(a, lo, hi, step) or (a[3] == 0 and kind == 0):
                         continue
-                    soft = oq == q and q == "T"
-                    preds[a[4]] = preds.get(a[4], False) or not soft
-        for (name, lo, hi, step, np) in w:
-            acc[name] = [a for a in acc.get(name, []) if not (lo <= a[0] and a[1] <= hi and step == 1 and np == 128)]
+                    preds[a[4]] = True
+        for (name, lo, hi, step) in w:
+            acc[name] = [a for a in acc.get(name, []) if not (lo <= a[0] and a[1] <= hi and step == 1)]
             acc[name].append([lo, hi, step, 1, k])
-        for (name, lo, hi, step, np) in r:
+        for (name, lo, hi, step) in r:
             acc.setdefault(name, []).append([lo, hi, step, 0, k])
         d = {"q": q, "calls": calls, "preds": preds, "cost": cost, "lat": lat}
         d.update(kw)
@@ -129,8 +129,8 @@ def rank_program(g, core, T, topo):
         return k
 
     def ap(v):
-        name, lo, hi, step, np = v
-        return T[name][0:np, lo:hi:step] if np != 128 else T[name][:, lo:hi:step]
+        name, lo, hi, step = v
+        return T[name][:, lo:hi:step]
 
     def opnd(v):
         if isinstance(v, tuple):
@@ -144,7 +144,7 @@ def rank_program(g, core, T, topo):
         return 16 * (v[2][2] - v[2][1]) if v[0] == "@" else -(-(v[2] - v[1]) // v[3])
 
     def size2(v):
-        return SCRATCH[(v[1] if v[0] == "@" else v)[0]][2] in ("bfloat16", "uint16")
+        return SCRATCH[(v[1] if v[0] == "@" else v)[0]][2] in ("bfloat16", "uint16", "float16")
 
     def cyc(out, ins, two=False):
         n = width(out)
@@ -157,7 +157,7 @@ def rank_program(g, core, T, topo):
         return n * (0.5 if all(size2(v) for v in [out] + ins) else 1)
 
     def vec(call, out, ins, cy):
-        node("V", [call], [out], ins, max(64.0, cy) * 0.00104)
+        node("V", [call], [out], ins, max(64.0, cy) * CYC)
 
     def tt(out, a, b, op):
         vec(lambda: g.vector.tensor_tensor(opnd(out), opnd(a), opnd(b), op), out, [a, b], cyc(out, [a, b], True))
@@ -171,35 +171,47 @@ def rank_program(g, core, T, topo):
     def cp(out, a):
         vec(lambda: g.vector.tensor_copy(opnd(out), opnd(a)), out, [a], cyc(out, [a]))
 
-    def act(out, a, scale=1.0, bias=0.0, func=F.Copy):
+    def fill(out, x):
+        vec(lambda: g.vector.memset(ap(out), x), out, [], cyc(out, []))
+
+    def act(out, a, scale=1.0, bias=0.0, func=F.Copy, total=None):
         n = width(out)
-        cost = (78 + 1.56 * n if a[0] == "@" else 60 + n) * 0.00104
-        node("S", [lambda: g.scalar.activation(opnd(out), opnd(a), func, bias=opnd(bias), scale=opnd(scale))], [out], [a, bias, scale], cost)
+        cost = (78 + 1.56 * n if a[0] == "@" else max(64, n)) * CYC
+        if total is None:
+            node("S", [lambda: g.scalar.activation(opnd(out), opnd(a), func, bias=opnd(bias), scale=opnd(scale))], [out], [a, bias, scale], cost)
+        else:
+            node("S", [lambda: g.scalar.activation(opnd(out), opnd(a), func, bias=bias, scale=scale, accum_out=ap(total))], [out, total], [a], cost + 0.02)
+
+    def fetch(q, out, win, off):
+        (cp if q == "V" else act)(out, at(win, off))
 
     def scan(out, d0, d1, op0, op1):
         vec(lambda: g.vector.tensor_tensor_scan(ap(out), ap(d0), ap(d1), 0.0, op0, op1), out, [d0, d1], cyc(out, [d0, d1]))
 
     def mms(lst):
         calls = [lambda o=o, l=l, r=r, s=s, e=e: g.tensor.matmul(ap(o), ap(l), ap(r), s, e) for o, l, r, s, e in lst]
-        cost = sum(max(64, width(r)) * (1 if size2(r) else 4) for o, l, r, s, e in lst) * 0.0006
+        cost = sum(max(64, width(r)) * (1 if size2(r) else 4) for o, l, r, s, e in lst) * PE
         node("T", calls, [x[0] for x in lst], [x[1] for x in lst] + [x[2] for x in lst], cost)
 
+    def total(out, terms, start=True, stop=True):
+        mms([(out, l, r, start and j == 0, stop and j == len(terms) - 1) for j, (l, r) in enumerate(terms)])
+
     def gps(call, out, ins, base):
-        node("G", [call], [out], ins, base + width(out) * 0.002)
+        node("G", [call], [out], ins, base + width(out) * 2 * CYC)
 
     def iota(v, pattern, base, cm):
         if SCRATCH[v[0]][2] != "int32":
-            gps(lambda: g.iota(ap(v), pattern, base, cm, allow_small_or_imprecise_dtypes=True), v, [], 0.14)
+            gps(lambda: g.iota(ap(v), pattern, base, cm, allow_small_or_imprecise_dtypes=True), v, [], 0.15)
         else:
-            gps(lambda: g.iota(ap(v), pattern, base, cm), v, [], 0.14)
+            gps(lambda: g.iota(ap(v), pattern, base, cm), v, [], 0.15)
 
     def const(v, x):
-        for lo in range(v[1], v[2], 720 * v[3]):
-            p = (v[0], lo, min(v[2], lo + 720 * v[3]), v[3], v[4])
+        for lo in range(v[1], v[2], 480 * v[3]):
+            p = (v[0], lo, min(v[2], lo + 480 * v[3]), v[3])
             iota(p, [[0, width(p)]], x, 0)
 
     def select(out, a, pattern, op, base, cm):
-        gps(lambda: g.affine_select(ap(out), ap(a), pattern, op, 0.0, base, cm), out, [a], 0.18)
+        gps(lambda: g.affine_select(ap(out), ap(a), pattern, op, 0.0, base, cm), out, [a], 0.2)
 
     def dma(q, out_ap, in_ap, sem, reads, writes, lat):
         node(q, [lambda: queue[q].dma_start(out_ap, in_ap)], writes, reads, 0.1, lat, sem=sem)
@@ -211,436 +223,363 @@ def rank_program(g, core, T, topo):
         k = node("G", [lambda: g.remote_dma(ap(out_v), ap(in_v), T.sem[sem], T.sem.loc, pid, rid, m)], [], [in_v], 0.3,
                  sent=len(topo.engines(core, dst)))
         n = len(topo.engines(cores[src_rank % N], core))
-        ops.append({"q": "A", "calls": [], "preds": {k: False}, "cost": 0.0, "lat": 1.8, "sem": sem, "amount": n})
-        acc[out_v[0]] = [a for a in acc.get(out_v[0], []) if not meet(a, out_v[1], out_v[2], 1)]
-        acc[out_v[0]].append([out_v[1], out_v[2], 1, 1, len(ops) - 1])
+        ops.append({"q": "A", "calls": [], "preds": {k: False}, "cost": 0.0, "lat": HOP, "sem": sem, "amount": n})
+        acc[out_v[0]] = [[out_v[1], out_v[2], 1, 1, len(ops) - 1]]
 
-    SS = lambda b: c("SS", 128 * b, 128 * b + 128)
+    def lane(w, b):
+        return c(w, 15 - b, 143 - b)
+
     EX = lambda b: c("EX", 128 * b, 128 * b + 128)
+    ID = c("IDW", 15, 143)
 
-    def gather_lanes(out, src, lo, n):
-        mms([(out, SS(b), c(src, lo + b, lo + 16 * n, 16), b == 0, b == 15) for b in range(16)])
+    def lanes16(w, src, lo, n):
+        return [(lane(w, b), c(src, lo + b, lo + 16 * n, 16)) for b in range(16)]
 
-    def spread(bank, src, n):
-        mms([(c(bank, b, 16 * n, 16), EX(b), src, True, True) for b in range(16)])
+    def blocks(w, src, lo, n, bs=range(16)):
+        return [(lane(w, b), c(src, lo + n * b, lo + n * b + n)) for b in bs]
 
-    def half(n, par, d=0):
-        return c(n, d + 160 * par, d + 160 * par + 160)
+    def spread(bank, lo, src, n):
+        mms([(c(bank, lo + n * b, lo + n * b + n), EX(b), src, True, True) for b in range(16)])
+
+    def half(n, par):
+        return c(n, 160 * par, 160 * par + 160)
 
     def lists(par):
-        return c("GL1", 168 * par, 168 * par + 160)
+        return c("GL%d" % par, OFF + par, OFF + 320, 2)
 
-    dma("Y", ap(c("GLI")), T.gl[:, :], "d_gl", [], [c("GLI")], 2.2)
-    dma("S", ap(c("V8I", 0, 320, 1, 8)), T.val[:, :], "d_val", [], [c("V8I", 0, 320)], 1.9)
-    dma("Y", ap(c("NBI")), T.nb[:, :], "d_nb", [], [c("NBI")], 2.4)
-    dma("S", ap(c("V8I", 320, 480, 1, 8)), T.th[:, :], "d_th", [], [c("V8I", 320, 480)], 1.9)
-    dma("Y", ap(c("Z0", 0, 160)), T.zl[:, :], "d_zl", [], [c("Z0", 0, 160)], 2.5)
+    dma("Y", ap(c("GLI")), T.gl[:, :], "d_gl", [], [c("GLI")], 1.8)
+    fill(c("V5"), 0)
+    dma("S", T["V5"][5:128:16, :], T.val[:, :], "d_v5", [], [c("V5")], 1.6)
+    dma("S", ap(c("VAI")), T.val[:, :], "d_va", [], [c("VAI")], 1.6)
+    dma("Y", ap(c("NBI")), T.nb[:, :], "d_nb", [], [c("NBI")], 2.0)
+    dma("Y", ap(c("THI")), T.th[:, :], "d_th", [], [c("THI")], 1.8)
+    dma("Y", ap(c("ZL")), T.zl[:, :], "d_zl", [], [c("ZL")], 2.0)
     dma("Y", ap(c("RW", 0, 4096)), T.rec[:, :], "d_rec", [], [c("RW", 0, 4096)], 6.0)
 
-    ingroup = [[-16, 8], [0, 16]]
+    iota(c("PI32"), [[0, 1]], 0, 1)
+    iota(c("WI"), [[1, 144]], -15, 0)
+    iota(c("HI"), [[-16, 20], [0, 16]], -OFF, 0)
+    iota(c("LO"), [[0, 20], [-1, 16]], 0, 0)
+    iota(c("K512"), [[0, 10], [-512, 16]], 7680, 0)
+    iota(c("TI"), [[1, 20]], 0, 20)
+    iota(c("BI"), [[16, 8], [0, 16]], 0, 0)
+    iota(c("MAJ"), [[1, 20], [20, 16]], OFF, 0)
+    iota(c("M1V"), [[2, 320]], 613, 0)
+    iota(c("K15"), [[0, 10], [-1, 16]], 15, 0)
+    iota(c("IOT", 0, 200), [[0, 10], [1, 20]], 1, 0)
+    const(c("IOT", 200, 208), -1)
+    iota(c("CJF"), [[16, 14]], 0, 0)
     const(c("ALL1"), 1)
-    select(c("BLP"), c("ALL1"), ingroup, A.is_ge, 0, 1)
-    select(c("B1"), c("BLP"), [[16, 8], [0, 16]], A.is_ge, 15, -1)
-    iota(c("CM1"), [[0, 8], [1, 16]], 1, 0)
-    iota(c("LI"), [[0, 1]], 0, 1)
-    iota(c("SEL0", 0, 128, 1, 8), [[-1, 8], [0, 16]], 0, 1)
-    const(c("ONF"), 1)
-    for h in (0, 1):
-        for w in (0, 1):
-            e = 128 * (2 * h + w)
-            select(c("EH", e, e + 128), c("ONF"), [[-32, 4], [1000, 2], [-1, 16]], A.is_equal, -1000 * h - 16 * w, 1)
-    for b in range(16):
-        select(EX(b), c("ALL1"), ingroup, A.is_equal, -b, 1)
-    iota(c("TI"), [[1, 2], [32, 10]], 0, 0)
-    iota(c("TJ"), [[160, 2], [16, 10]], 2560, 0)
-    iota(c("MA1"), [[1, 2], [2, 160]], 1, 0)
-    iota(c("M1V"), [[2, 2], [4, 160]], 613, 0)
-    iota(c("V21"), [[2, 2], [4, 160]], 1, 0)
+    for b in range(0, 16, 4):
+        select(c("EX", 128 * b, 128 * b + 512), c("ALL1"), [[-1, 4], [-16, 8], [0, 16]], A.is_equal, -b, 1)
     for i in (0, 1):
-        const(c("DWa%d" % i, 320, 512), 0)
-    for t in range(RO + 1):
-        const(c("Z%d" % t, 160, 176), 0)
-    iota(c("KC"), [[0, 20], [1, 16]], 0, 0)
+        const(c("GL%d" % i, 0, OFF), -5)
     const(c("RW", 4096, 4112), 0)
-    zero = c("DX0")
-    vec(lambda: g.vector.memset(ap(zero), 0.0), zero, [], 1440)
-    const(c("MIN1"), -1)
-    select(c("ID"), c("ALL1"), [[-1, 128]], A.is_equal, 0, 1)
-    select(c("NTRI"), c("MIN1"), [[-16, 8], [-1, 16]], A.is_gt, 0, 1)
-    select(c("NTRI"), c("NTRI"), [[16, 8], [0, 16]], A.is_ge, 15, -1)
+    const(c("DX0", 0, 960), 0)
+    for j, s in ((1, "d_a"), (2, "d_b")):
+        dma("Y", ap(c("DX0", 960 * j, 960 * j + 960)), ap(c("DX0", 0, 960)), s, [c("DX0", 0, 960)], [c("DX0", 960 * j, 960 * j + 960)], 2.2)
+    for n, s in (("OW0", "d_o0"), ("OW1", "d_o1"), ("DX1", "d_x1"), ("DX2", "d_x2")):
+        dma("Y", ap(c(n)), ap(c("DX0")), s, [c("DX0")], [c(n)], 4.0)
+    for n in ("Z0", "ZS0", "ZS1", "OD"):
+        const(c(n), 0)
+    const(c("ON10"), 1)
+    const(c("C16"), 16)
     const(c("FLB"), 1)
     const(c("FLB", 0, 2560, 16), 0)
-    iota(c("IOT", 0, 200), [[0, 10], [1, 20]], 10, 0)
-    const(c("IOT", 200, 208), 0)
-    iota(c("CJ"), [[16, 14]], 0, 0)
     for i in (1, 0):
         cur[0] = i
         const(c("HF"), 0)
-        const(c("JC", 0, 20), 0)
-    for n, s in (("OWa0", "d_o0"), ("OWa1", "d_o1"), ("DX1", "d_x1"), ("DX2", "d_x2")):
-        dma("Y", ap(c(n)), ap(c("DX0")), s, [c("DX0")], [c(n)], 4.0)
-    const(c("GL1", 160, 168), -5)
-    const(c("GL1", 328, 336), -5)
-    for n in ("EVW", "ODW"):
-        const(c(n), 0)
 
-    tt(c("BLC"), c("CM1"), c("B1"), A.mult)
-    ts(c("LI"), c("LI"), 15, A.bitwise_and)
+    ts(c("LI"), c("PI32"), 15, A.bitwise_and)
+    ts(c("LGI"), c("PI32"), 112, A.bitwise_and)
+    cp(c("LG"), c("LGI"))
     cp(c("LN"), c("LI"))
-    ts(c("LN2"), c("LN"), 2.0, A.mult)
-    const(c("LNB"), 4096)
-    const(c("LNC"), int(BIG))
-    const(c("ON1"), 1)
-    ts(c("LNN"), c("LN"), -1.0, A.mult)
-    ts(c("LK1"), c("LN"), 1.0, A.add)
-    ts(c("LC0"), c("LN"), -256.0, A.mult, 3680.0, A.add)
-    ts(c("LC1"), c("LC0"), BIG, A.subtract)
-    for b in range(16):
-        ts(SS(b), c("BLC"), float(b + 1), A.is_equal, 64.0, A.mult)
-
-    def names(par):
-        ts(half("NA", par), lists(par), -1.0, A.add)
-        ts(half("PB", par), half("NA", par), 1, A.bitwise_and)
-        act(half("HA", par), lists(par), 0.5, -0.5)
-        ts(half("AO", par), half("PB", par), 159.5, A.mult)
-        tt(half("AO", par), half("AO", par), half("HA", par), A.add)
-        cp(half("AOU", par), half("AO", par))
-
-    def keys(par, q):
-        if q == 0:
-            ts(half("CT", par), half("PB", par), -BIG - 0.5, A.mult, c("LC0"), A.add)
-            tt(half("CK", par), half("CT", par), half("HA", par), A.add)
-        else:
-            act(half("EMP", par), lists(par), -BIG, c("LNC"), F.Relu)
-            ts(half("CT", par), half("PB", par), BIG - 0.5, A.mult, c("LC1"), A.add)
-            tt(half("CT", par), half("CT", par), half("EMP", par), A.subtract)
-            tt(half("CK", par, 320), half("CT", par), half("HA", par), A.add)
-
-    def places(par):
-        act(half("M2A", par), lists(par), 2.0, 35.0)
-        tt(half("BUI", par), half("NA", par), half("V21", par), A.mult)
-        ts(half("BUI", par), half("BUI", par), 4, A.arith_shift_right)
-        tt(half("BU", par), half("BUI", par), half("NA", par), A.add)
-        act(half("INV", par), lists(par), -4096.0, c("LNB"), F.Relu)
-
-    for par in (0, 1):
-        ts(lists(par), c("GLI", par, 320, 2), 1.0, A.add)
-        act(half("VAL", par), lists(par), 1.0, 0.0, F.Sign)
-    mms([(c("P7", 0, 320), c("B1"), c("VAL"), True, True)])
-    ts(c("NT"), c("P7", 0, 320), 4.0, A.mult, 4.0, A.add)
-    act(c("NS"), c("P7", 0, 320))
-    for par in (0, 1):
-        names(par)
-
-    def sizes_at_entries(split):
-        for lo, hi in ((split, 160), (160, 240), (240, 320)):
-            act(c("SG", 16 * lo, 16 * hi), at(c("NT"), c("AOU", lo, hi)))
-        if split:
-            cp(c("SG", 0, 16 * split), at(c("NT"), c("AOU", 0, split)))
-        for o in (0, 160):
-            mms([(c("P7", o, o + 160), SS(k), c("SG", 16 * o + k, 16 * o + 2560, 16), k == 0, k == 15) for k in range(16)])
-
-    def elect(q):
-        tt(c("KL"), c("P7", 0, 320), c("CK", 320 * q, 320 * q + 320), A.add)
-        v, o = c("T1"), c("KL")
-        vec(lambda: g.vector.transpose(ap(v), ap(o)), v, [o], 320)
-        scan(c("R1"), c("FL"), c("T1"), A.mult, A.max)
-        mms([(c("P2", 64 + w, 84, 2), c("EH", 128 * (2 * h + w), 128 * (2 * h + w) + 128), c("R1", 16 * h + 15, 320, 32), h == 0, h == 1)
-             for w in (0, 1) for h in (0, 1)])
-        cp(c("KB", 20 * q, 20 * q + 20), c("P2", 64, 84))
-
-    NHP, NLP = c("P4", 192, 512), c("P2", 192, 512)
-    for par in (0, 1):
-        cp(half("NCF", par), c("NBI", par, 320, 2))
-    act(c("NH"), c("NCF"))
-    act(NHP, c("NH"))
-    tt(NLP, c("NCF"), NHP, A.subtract)
-    ts(c("SEL8", 0, 128, 1, 8), c("SEL0", 0, 128, 1, 8), 0.0, A.is_equal)
-    cp(c("R8", 0, 320, 1, 8), c("V8I", 0, 320, 1, 8))
-    ts(c("V8F", 0, 160, 1, 8), c("V8I", 320, 480, 1, 8), 1.0 / 16, A.mult)
-    cp(c("R8", 320, 480, 1, 8), c("V8F", 0, 160, 1, 8))
-    tt(c("R8", 480, 640, 1, 8), c("V8F", 0, 160, 1, 8), c("R8", 320, 480, 1, 8), A.subtract)
-    mms([(c("P0", 0, 320), c("SEL8", 0, 128, 1, 8), c("R8", 0, 320, 1, 8), True, True)])
-    mms([(c("P1", 0, 320), c("SEL8", 0, 128, 1, 8), c("R8", 320, 640, 1, 8), True, True)])
-    for par in (0, 1):
-        act(c("DWa0", 160 * par, 160 * par + 160), c("P0", par, 320, 2), 1.0 / 1024)
-    act(c("THL"), c("P1", 0, 320))
-    gather_lanes(c("P2", 0, 20), "DWa0", 0, 20)
-    cp(c("GDI"), c("P2", 0, 20))
-    cp(c("SO"), c("P2", 0, 20))
-    cp(c("PJM", 0, 20), c("P2", 0, 20))
-    send(rank - 1, rank + 1, c("GH0"), c("GDI"), "ag0")
-    gather_lanes(c("P2", 32, 52), "THL", 0, 20)
-    act(c("TH2"), c("P2", 32, 52))
-    tt(c("th64"), c("TH2", 0, 10), c("TH2", 10, 20), A.add)
-    ts(c("thr"), c("th64"), 15.0, A.add)
-    ts(c("AC"), c("TI"), c("LN2"), A.add)
-    ts(c("DMP"), c("TJ"), c("LN"), A.add)
-    ts(c("A21"), c("AC"), 2.0, A.mult, 1.0, A.add)
-    ts(c("CM40", 0, 20), c("AC"), 2.0, A.mult, 37.0, A.add)
-    ts(c("CM40", 20, 40), c("AC"), 2.0, A.mult, 613.0, A.add)
-    ts(c("EVW", 0, 128, 2), c("B1", 0, 128, 2), 1.0 / 512, A.mult)
-    ts(c("ODW", 1, 128, 2), c("B1", 1, 128, 2), 1.0 / 512, A.mult)
-    ts(c("FL"), c("KC"), 0.5, A.is_ge)
-    ts(c("K15"), c("KC", 0, 160), -1.0, A.mult, 15.0, A.add)
-    ts(c("K10"), c("KC", 0, 160), 1024.0, A.mult)
-    ts(c("CJ"), c("CJ"), c("LN"), A.add)
-    ts(c("CJ"), c("CJ"), 3277.0, A.mult)
-    ts(c("CJ"), c("CJ"), 16, A.arith_shift_right)
+    cp(c("PF"), c("PI32"))
+    ts(c("SS"), c("WI"), c("LG"), A.is_equal, 64.0, A.mult)
+    ts(c("IDW"), c("WI"), c("PF"), A.is_equal)
+    fill(c("PI", 0, 320, 2), 0.0)
+    fill(c("PI", 1, 320, 2), -524288.0)
+    fill(c("DUM"), -1048576.0)
+    fill(c("D256", 0, 31), 0.0)
+    fill(c("D256", 31, 32), 256.0)
+    fill(c("FL"), 1.0)
+    fill(c("FL", 0, 160, 16), 0.0)
+    fill(c("C185"), -18.5)
+    ts(c("cu"), c("LN"), 4.5, A.is_le, 1.0 / 32, A.mult)
+    for n, col, lim in (("WM", "c3", 2.5), ("WP", "c4", 3.5)):
+        ts(c(col), c("LN"), lim, A.is_ge, 0.5, A.subtract)
+        ts(c(n), c("SS"), c(col), A.mult, c("cu"), A.mult)
+    ts(c("cd"), c("LN"), 5.0, A.is_equal, 0.25, A.mult)
+    act(c("WD"), c("SS"), c("cd"))
+    ts(c("cn"), c("LN"), 15.0, A.is_equal, 1.0 / 32, A.mult)
+    ts(c("cn"), c("cn"), 1.0 / 16384, A.max)
+    act(c("WN"), c("SS"), c("cn"))
+    ts(c("B1"), c("BI"), c("LG"), A.is_equal)
+    ts(c("BLC"), c("WI", 15, 143), c("LG"), A.subtract)
+    ts(c("TRA"), c("BLC"), c("LN"), A.is_gt)
+    tt(c("TRI"), c("TRA"), c("B1"), A.mult)
+    act(c("B1N"), c("B1"), -1024.0)
+    act(c("OD", 1, 128, 2), c("B1", 1, 128, 2))
+    act(c("DPM", 0, 128, 2), c("IDW", 15, 143, 2))
+    act(c("DPM", 1, 128, 2), c("IDW", 16, 143, 2), -1.0)
+    act(c("ID8"), ID, -8.0)
+    act(c("ID32"), ID)
+    ts(c("cs"), c("LN"), 15.0, A.not_equal, -1.0, A.mult)
+    act(c("SHB"), c("IDW", 14, 142), c("cs"))
+    ts(c("cp"), c("LN"), 0.5, A.is_ge, -131072.0, A.mult)
+    ts(c("ck"), c("LN"), 1.0, A.add, 1.0 / 64, A.mult)
+    act(c("DR"), c("FL"), -262144.0, 262144.0)
+    ts(c("LG20"), c("LG"), -20.0, A.mult)
+    ts(c("AC"), c("TI"), c("LG20"), A.add)
+    act(c("A17"), c("AC"), 2.0 / 64, 17.0 / 64)
+    act(c("CM40", 0, 20), c("AC"), 2.0, 37.0)
+    act(c("CM40", 20, 40), c("AC"), 2.0, 613.0)
+    ts(c("K10"), c("LO", 0, 160), -1024.0, A.mult, float(OFF), A.add)
+    ts(c("VY"), c("M1V"), -596.0, A.add, 1.0 / 32, A.mult)
+    ts(c("cj"), c("LN"), -9.5, A.add)
+    ts(c("CJ"), c("CJF"), c("cj"), A.add, 0.05, A.mult)
     cp(c("COFF"), c("CJ"))
 
-    sizes_at_entries(60)
+    ts(c("VALN"), c("GLI"), 0.0, A.is_ge, -131072.0, A.mult)
     for par in (0, 1):
-        keys(par, 0)
-    elect(0)
+        ts(half("AOU", par), c("GLI", par, 320, 2), float(OFF), A.add)
+    ts(c("R16"), c("V5"), 16.0, A.mult)
+    statics = [(lane("SS", 1), c("HI")), (lane("SS", 2), c("LO")), (lane("SS", 3), c("PI"))]
+    total(c("P0", 0, OFF), [(lane("SS", 4), c("DUM")), (lane("SS", 5), c("D256"))])
+    total(c("P0", OFF, 352), statics, stop=False)
+    total(c("P0", OFF, 352), [(lane("SS", 0), c("VALN")), (lane("SS", 5), c("R16"))], start=False)
+    act(c("DW0", 0, 352), c("P0", 0, 352), 1.0 / 1024)
+    ts(c("GL0", OFF), c("GLI"), float(OFF), A.add)
+    act(c("GL1", OFF), c("GL0", OFF))
+    for n in ("DW1", "ST"):
+        act(c(n, 0, OFF), c("DW0", 0, OFF))
+
+    def entries(par, win, queues, keys):
+        for j, q in enumerate(queues):
+            n = 160 // len(queues)
+            lo = 160 * par + n * j
+            fetch(q, c("SG", 16 * lo, 16 * (lo + n)), c(win, 0, 352), c("AOU", lo, lo + n))
+            if keys:
+                nb = 16 // len(queues)
+                total(keys, ([(ID, c("K512"))] if j == 0 else []) + blocks("WM", "SG", 2560 * par, 160, range(nb * j, nb * j + nb)), j == 0, j == len(queues) - 1)
+
+    PK = (c("P2", 192, 352), c("P3", 320, 480))
+    for par in (0, 1):
+        entries(par, "DW0", FIRST[4 * par:4 * par + 4], PK[par])
+        scan(half("R1", par), c("FL"), PK[par], A.mult, A.max)
+        cp(c("KB0", par, 20, 2), c("R1", 160 * par + 15, 160 * par + 160, 16))
+    for par in (0, 1):
+        act(half("AB", par), PK[par], 1.0, 262144.0, F.Abs)
+        scan(half("R2", par), c("DR"), half("AB", par), A.max, A.min)
+        ts(c("KB1", par, 20, 2), c("R2", 160 * par + 15, 160 * par + 160, 16), -1.0, A.mult, 262144.0, A.add)
+
+    NBP = c("P4", 0, 320)
+    cp(c("NBH"), c("NBI"))
+    mms([(c("P4", b, 320, 16), ID, c("NBH", 20 * b, 20 * b + 20), True, True) for b in range(16)])
+    cp(c("XB", 60, 80), c("VAI"))
+    act(c("GDI"), c("XB", 60, 80))
+    send(rank - 1, rank + 1, c("GH0"), c("GDI"), "ag0")
+    ts(c("th64"), c("THI"), 64.0, A.mult)
+    act(c("thr"), c("th64"), 1.0, 15.0)
+    act(c("Z0", OFF, 352, 2), c("ZL"))
+    total(c("P6", 416, 436), blocks("WN", "VALN", 0, 20))
+    act(c("BASE", 0, 20, 2), c("P6", 416, 436, 2), 1.0, 7680.0 - 524288.0)
+    act(c("BASE", 1, 20, 2), c("P6", 417, 436, 2), 1.0, 7680.0)
+    for par in (0, 1):
+        act(half("APR", par), lists(par), 32.0, -432.0)
 
     def prep(t):
         par = t & 1
         cur[0] = par
-        ts(c("E1"), c("KB", 20 * par, 20 * par + 20), 160.0, A.add)
-        ts(c("EI"), c("E1"), 255, A.bitwise_and)
-        cp(c("EU"), c("EI"))
-        tt(c("EQ"), at(c("GL1", 168 * par, 168 * par + 168), c("EU")), c("MA1"), A.is_equal)
-        tt(c("W3", 0, 320), c("EQ"), NHP, A.mult)
-        tt(c("W3", 320, 640), c("EQ"), NLP, A.mult)
-        act(c("W3", 640, 960), c("EQ"), c("LK1"))
-        gather_lanes(c("P6", 0, 60), "W3", 0, 60)
-        ts(c("X1"), c("EI"), 4.0, A.mult, 2.0 * par + 1.0, A.add)
-        tt(c("X2"), c("AC"), c("X1"), A.mult)
-        ts(c("XS"), c("X2"), 4, A.arith_shift_right)
-        ts(c("MM2", 0, 20), c("EI"), 4.0, A.mult, 2.0 * par + 613.0, A.add)
-        tt(c("BB2", 0, 20), c("XS"), c("AC"), A.add)
-        ts(c("X6"), c("EI"), 16.0, A.mult, -1.0, A.add)
-        ts(c("E3"), c("EI"), 15, A.bitwise_and)
-        ts(c("E4"), c("EI"), 4, A.arith_shift_right)
-        ts(c("X7"), c("E3"), 160.0, A.mult, -1.0, A.add)
-        ts(c("X4"), c("E4"), 16.0, A.mult)
-        tt(c("X7"), c("X7"), c("X4"), A.add)
-        ts(c("A3"), c("P6", 0, 60), 1.0 / 64, A.mult)
-        tt(c("OF"), c("A3", 0, 20), c("A3", 20, 40), A.add)
-        cp(c("CI"), c("OF"))
-        ts(c("X3"), c("OF"), 320.0, A.is_ge, 352.0, A.mult)
-        ts(c("E2"), c("CI"), 1, A.bitwise_and)
-        ts(c("CS1"), c("CI"), 1, A.arith_shift_right)
-        ts(c("X5"), c("E2"), 160.0, A.mult)
-        tt(c("X8"), c("X3"), c("CS1"), A.add)
-        tt(c("X8"), c("X8"), c("X5"), A.add)
-        cp(c("OU"), c("X8"))
-        tt(c("Y2"), c("OF"), c("A21"), A.mult)
-        ts(c("MM2", 20, 40), c("OF"), 2.0, A.mult, 37.0, A.add)
-        ts(c("YS"), c("Y2"), 4, A.arith_shift_right)
-        tt(c("BB2", 20, 40), c("YS"), c("OF"), A.add)
-        ts(c("NM"), c("A3", 40, 60), 0.5, A.is_lt)
-        tt(c("DN"), c("NM"), c("DMP"), A.mult)
-        for j in (1, 2, 3):
-            act(c("JC", 20 * j, 20 * j + 20), c("NM"), BIG, 16.0 * j)
-        for j, x in ((0, "X6"), (20, "X7")):
-            tt(c(x), c(x), c("A3", 40, 60), A.add)
-            tt(c("PX", j, j + 20), c(x), c("DN"), A.max)
+        ts(c("EI"), c("KB%d" % t), 511, A.bitwise_and)
+        cp(c("EOU", 0, 20), c("EI"))
+        tt(c("W3", 640, 960), at(c("GL%d" % par), c("EOU", 0, 20)), c("MAJ"), A.is_equal)
+        tt(c("W3", 0, 320), c("W3", 640, 960), NBP, A.mult)
+        ts(c("W3", 320, 640), c("W3", 640, 960), c("ck"), A.mult)
+        total(c("P6", 0, 60), lanes16("SS", "W3", 0, 60))
+        po, pk, pm = c("P6", 0, 20), c("P6", 20, 40), c("P6", 40, 60)
+        cp(c("EF"), c("EI"))
+        act(c("V613"), c("EF"), 0.5, 137.25)
+        act(c("V17"), c("EF"), 2.0, -47.0)
+        act(c("X6"), c("EF"), 0.125, (63.0 - 8 * par) / 64)
+        tt(c("BB", 0, 20), c("AC"), c("V17"), A.mult)
+        ts(c("EOU", 20, 40), po, 1.0 / 64, A.mult, float(OFF), A.add)
+        tt(c("MM", 60, 80), pm, c("V613"), A.mult)
+        tt(c("BB", 20, 40), po, c("A17"), A.mult)
+        tt(c("pt"), pm, c("X6"), A.mult)
+        tt(c("pu"), pk, c("pt"), A.add)
+        act(c("MM", 80, 100), po, 0.5, 592.0)
+        act(c("MM", 40, 60), c("MM", 60, 80))
+        act(c("MM", 0, 40), c("MM", 40, 80))
+        tt(c("PX"), c("pu"), c("AC"), A.max)
         cp(c("PU"), c("PX"))
-        ow = "OWa%d" % par
-        mms([(c("P6", 128, 448), c("EVW"), c("W3", 0, 320), True, False), (c("P6", 128, 448), c("ODW"), c("W3", 320, 640), False, True)])
-        act(c("OEB"), c("P6", 128, 448))
-        cp(at(c(ow), c("PU", 20, 40)), c("OEB"))
-        mms([(c("P7", 320, 480), SS(b), c(ow, 160 * b, 160 * b + 160), b == 0, False) for b in range(16)]
-            + [(c("P7", 320, 480), c("ID"), c("K10"), False, True)])
-        cur[0] = 1 - par
+        total(c("P6", 64, 384), [(c("B1"), c("W3", 0, 320))])
+        act(c("OH"), c("P6", 64, 384))
+        total(c("P6", 64, 384), [(c("OD"), c("W3", 0, 320)), (c("DPM"), c("OH"))])
+        act(c("OEB"), c("P6", 64, 384), 1.0 / 512)
+        cp(at(c("OW%d" % par), c("PU")), c("OEB"))
 
     prep(0)
-    for par in (0, 1):
-        keys(par, 1)
-    elect(1)
-    cur[0] = 0
-    places(0)
-    places(1)
 
     for t in range(RO):
         par = t & 1
-        po = 160 * par
         cur[0] = par
-        zw = "Z%d" % t
-        dw = "DWa%d" % par
+        zw, dw, gw, last = "Z%d" % t, "DW%d" % par, "GW%d" % par, t == RO - 1
+        own = c(dw, OFF, 352)
+        so = c("XB", 60, 80)
         if t:
             cur[0] = 1 - par
             pn = c("PN")
             cur[0] = par
-            tt(c("SGI"), c("GH%d" % t), c("P6", 64, 84), A.add)
+            tt(c("SGI"), c("GH%d" % t), c("P5", 256, 276), A.add)
             ts(c("SGJ"), c("SGI"), 15, A.bitwise_and)
             cp(c("SGH"), c("SGJ"))
-            spread("P1", c("SGH"), 20)
-            act(c(dw, 512, 832), c("P1", 0, 320), 1.0 / 1024)
+            spread("P1", 0, c("SGH"), 20)
+            act(c(dw, 352, 672), c("P1", 0, 320))
             tt(c("SI"), pn, c("CL%d" % (t - 1)), A.add)
-            ts(c("PJM", 0, 20), c("SI"), 15, A.bitwise_and)
-            cp(c("SO"), c("PJM", 0, 20))
-            spread("P0", c("SO"), 20)
-            ts(c(dw, 0, 320), c("P0", 0, 320), 1.0 / 1024, A.mult)
+            ts(c("PJ"), c("SI"), 15, A.bitwise_and)
+            cp(so, c("PJ"))
+            spread("P0", OFF, so, 20)
+            if t == 1:
+                tt(own, c("P0", OFF, 352), c("ST", OFF, 352), A.min)
+            else:
+                act(own, c("P0", OFF, 352))
         else:
-            spread("P1", c("GH0"), 20)
-            act(c(dw, 512, 832), c("P1", 0, 320), 1.0 / 1024)
-            spread("P0", c("SO"), 20)
-        cp(c("QD", 0, 320), at(c(dw, po, po + 176), c("EU")))
-        act(c("QD", 320, 640), at(c(dw), c("OU")))
-        gather_lanes(c("P2", 0, 40), "QD", 0, 40)
+            spread("P1", 0, c("GH0"), 20)
+            act(c(dw, 352, 672), c("P1", 0, 320))
         for j in (1, 2, 3):
-            ts(c("PJ", 20 * j, 20 * j + 20), c("PJM", 0, 20), float(j), A.add)
-        ts(c("PJM", 20, 80), c("PJ", 20, 80), 15, A.bitwise_and)
-        for j in range(4):
-            tt(c("TP", 20 * j, 20 * j + 20), c("PJM", 20 * j, 20 * j + 20), c("MM2", 0, 20), A.mult)
-        tt(c("TP", 80, 100), c("PJM", 0, 20), c("MM2", 20, 40), A.mult)
-        tt(c("J2"), c("JC"), c("PJM"), A.add)
+            act(c("XB", 20 * j - 20, 20 * j), so, 1.0, float(j))
+        act(c("XB", 80, 100), so)
+        act(c("SGN"), c("XB", 0, 60), 1.0, -15.5, F.Sign)
+        mms([(c("P2", 64, 164), ID, c("XB"), True, False), (c("P2", 64, 124), c("ID8"), c("ALL1", 0, 60), False, False),
+             (c("P2", 64, 124), c("ID8"), c("SGN"), False, True)])
+        tp = lambda lo, hi: c("P4", 320 + lo, 320 + hi)
+        tt(tp(0, 100), c("P2", 64, 164), c("MM"), A.mult)
+        fetch("S", c("QD"), c(dw), c("EOU"))
+        total(c("P2", 0, 40), lanes16("WD", "QD", 0, 40))
         tt(c("U"), c("P2", 0, 40), c("CM40"), A.mult)
-        tt(c("B40"), c("BB2"), c("U"), A.add)
-        for j in range(5):
-            tt(c("T6", 20 * j, 20 * j + 20), c("TP", 20 * j, 20 * j + 20), c("B40", j // 4 * 20, j // 4 * 20 + 20), A.add)
-        ts(c("IX"), c("T6"), 4095, A.bitwise_and)
+        tt(c("B60", 20, 60), c("U"), c("BB"), A.add)
+        tt(c("B60", 0, 20), c("U", 0, 20), c("BB", 0, 20), A.add)
+        tt(c("T6", 40, 100), tp(40, 100), c("B60"), A.add)
+        tt(c("T6", 0, 40), tp(0, 40), c("B60", 0, 40), A.add)
+        ts(c("IX"), c("T6"), 4, A.arith_shift_right, 4095, A.bitwise_and)
         cp(c("IXU"), c("IX"))
-        act(c("ZE"), at(c(zw), c("EU")))
+        fetch("S", c("ZE"), c(zw), c("EOU", 0, 20))
         for j in range(4):
             tt(c("X", 320 * j, 320 * j + 320), at(c("RW", 0, 4096), c("IXU", 20 * j, 20 * j + 20)), c("ZE"), A.max)
-        gather_lanes(c("P3", 0, 80), "X", 0, 80)
-        for hf in (0, 40, 80, 120):
-            act(c("DG", 16 * hf, 16 * hf + 640), at(c(dw, 0, 320), c("AOU", po + hf, po + hf + 40)))
-        mms([(c("P4", 0, 160), SS(k), c("DG", k, 2560, 16), k == 0, k == 15) for k in range(16)])
-        tt(c("P0", 320, 480), half("M2A", par), c("P0", po, po + 160), A.mult)
-        tt(c("UC"), half("BU", par), c("P0", 320, 480), A.add)
-        tt(c("P3", 320, 480), half("M1V", par), c("P4", 0, 160), A.mult)
-        tt(c("UE"), c("UC"), c("P3", 320, 480), A.add)
-        ts(c("UF"), c("UE"), 4095, A.bitwise_and)
-        tt(c("UG"), c("UF"), half("INV", par), A.max)
-        cp(c("UI"), c("UG"))
-        gw = "Ga%d" % par
+        total(c("P3", 0, 80), lanes16("SS", "X", 0, 80) + [(ID, c("XB", 0, 80))])
         tt(c("XO"), at(c("RW", 0, 4096), c("IXU", 80, 100)), c("ZE"), A.max)
         act(c("NXO"), c("XO"), -1.0)
-        tt(c("KI"), c("P3", 0, 80), c("J2"), A.add)
-        tt(c("KJ"), c("KI", 0, 40), c("KI", 40, 80), A.min)
+        act(c("KIB"), c("P3", 40, 80))
+        tt(c("KJ"), c("P3", 0, 40), c("KIB"), A.min)
         tt(c("KK"), c("KJ", 0, 20), c("KJ", 20, 40), A.min)
         ts(c("PN"), c("KK"), 15, A.bitwise_and)
-        tt(c("PQ", 20, 40), c("PN"), c("MM2", 20, 40), A.mult)
-        tt(c("PQ", 0, 20), c("PN"), c("MM2", 0, 20), A.mult)
-        tt(c("IN"), c("PQ"), c("B40"), A.add)
-        ts(c("IM"), c("IN"), 4095, A.bitwise_and)
+        tt(c("PQ", 20, 40), c("PN"), c("MM", 80, 100), A.mult)
+        tt(c("PQ", 0, 20), c("PN"), c("MM", 60, 80), A.mult)
+        tt(c("IN"), c("PQ"), c("B60", 20, 60), A.add)
+        ts(c("IM"), c("IN"), 4, A.arith_shift_right, 4095, A.bitwise_and)
         cp(c("IXN"), c("IM"))
-        if t < RO - 1:
+        if not last:
             cp(c("GD%d" % t), c("PN"))
             send(rank - 1, rank + 1, c("GH%d" % (t + 1)), c("GD%d" % t), "ag%d" % (t + 1))
-        tt(c("XN"), at(c("RW", 0, 4096), c("IXN", 20, 40)), c("ZE"), A.max)
-        tt(at(c("DX%d" % t), c("PU", 20, 40)), c("XN"), c("NXO"), A.add)
-        mms([(c("P5", 0, 160), SS(b), c("DX%d" % t, 160 * b, 160 * b + 160), b == 0, False) for b in range(16)]
-            + [(c("P5", 0, 160), c("ID"), c("K15"), False, True)])
-        act(c("RN"), at(c("RW", 0, 4096), c("IXN", 0, 20)))
+        if t:
+            entries(par, dw, "SSSS", c("P2", 192, 352) if t == 1 else None)
+        PD, PY = c("P3", 128, 288), c("P0", 352, 512)
         for hf in (0, 80):
-            act(c(gw, 16 * hf, 16 * hf + 1280), at(c("RW"), c("UI", hf, hf + 80)))
-        scan(c("S1"), c("FL", 0, 160), c("P5", 0, 160), A.mult, A.max)
-        tt(c("QE"), c("S1"), c("P5", 0, 160), A.is_equal)
-        tt(c("QY"), c("QE"), c("P7", 320, 480), A.mult)
-        scan(c("S2"), c("FL", 0, 160), c("QY"), A.mult, A.max)
+            total(c("P3", 128 + hf, 208 + hf), [(ID, c("C185", 0, 80))] + lanes16("WD", "SG", 2560 * par + 16 * hf, 80))
+        total(PY, [(EX(5), c(dw, OFF + par, 352, 2)), (ID, c("VY", par, 320, 2))])
+        tt(c("T1"), PY, half("APR", par), A.mult)
+        tt(PD, PD, c("M1V", par, 320, 2), A.mult)
+        tt(c("UE"), PD, c("T1"), A.add)
+        ts(c("UQ"), c("UE"), 11018.5, A.add, 1.0 / 16, A.mult)
+        ts(c("UF"), c("UQ"), 4095 + 15 * 65536, A.bitwise_and)
+        ts(c("UI"), c("UF"), 4096.0, A.min)
+        for hf in (0, 80):
+            fetch("S", c(gw, 320 + 16 * hf, 1600 + 16 * hf), c("RW"), c("UI", hf, hf + 80))
+        total(c("P7", 0, 160), [(ID, c("K10"))] + blocks("SS", "OW%d" % par, 320, 160))
+        tt(c("XN"), at(c("RW", 0, 4096), c("IXN", 20, 40)), c("ZE"), A.max)
+        tt(at(c("DX%d" % t), c("PU")), c("XN"), c("NXO"), A.add)
+        P5 = c("P5", 0, 160)
+        total(P5, [(ID, c("K15"))] + blocks("SS", "DX%d" % t, 320, 160))
+        fetch("S", c("RN"), c("RW", 0, 4096), c("IXN", 0, 20))
+        scan(c("S1"), c("FL"), P5, A.mult, A.max)
+        tt(c("QE"), P5, c("S1"), A.is_equal)
+        tt(c("QY"), c("P7", 0, 160), c("QE"), A.mult)
+        scan(c("S2"), c("FL"), c("QY"), A.mult, A.max)
         tt(c("inj"), c("S1", 15, 160, 16), c("thr"), A.is_gt)
         cp(c("y"), c("S2", 15, 160, 16))
         ts(c("code"), c("y"), 1023, A.bitwise_and)
-        ts(c("gh"), c("code"), 320.0, A.is_ge)
-        if t == 1:
-            names(0)
-            keys(0, 0)
-            places(0)
-            sizes_at_entries(0)
-            elect(0)
-        tt(c("xb"), c("inj"), c("gh"), A.mult)
-        mms([(c("P5", 192, 202), c("B1"), c("xb"), True, True), (c("P5", 208, 218), c("NTRI"), c("xb"), True, True)])
-        ts(c("wi"), c("code"), 1, A.arith_shift_right, 15, A.bitwise_and)
-        ts(c("pb"), c("code"), 1, A.bitwise_and)
-        ts(c("p10"), c("pb"), 10.0, A.mult)
-        ts(c("w"), c("wi"), 1.0, A.add)
-        ts(c("h5"), c("code"), 5, A.arith_shift_right)
-        tt(c("hh"), c("h5"), c("p10"), A.add)
+        tt(c("xi"), c("code"), c("inj"), A.mult)
+        ts(c("xb"), c("xi"), 351.5, A.is_ge, 1024.0, A.mult)
+        tt(c("xj"), c("xi"), c("xb"), A.subtract)
+        if not last:
+            cp(c("CU"), c("xj"))
+            total(c("P6", 400, 410), [(c("ID32"), c("BASE", par, 20, 2))], stop=False)
+            fetch("S", c("JB"), c(dw, 0, 352), c("CU"))
+            total(c("P6", 400, 410), lanes16("WM" if par else "WP", "JB", 0, 10), start=False)
+            if t == 0:
+                tt(c("KB1", 0, 20, 2), c("P6", 400, 410), c("KB1", 0, 20, 2), A.max)
+            else:
+                scan(half("R1", 1), c("FL"), c("P2", 192, 352), A.mult, A.max)
+                entries(0, "ST", "SSSS", c("P2", 352, 512))
+                scan(half("R1", 0), c("FL"), c("P2", 352, 512), A.mult, A.max)
+                cp(c("KB2", 0, 20, 2), c("R1", 15, 160, 16))
+                tt(c("KB2", 1, 20, 2), c("P6", 400, 410), c("R1", 175, 320, 16), A.max)
+        scan(c("cs10"), c("ON10"), c("xb"), A.mult, A.add)
+        total(c("P5", 192, 193), [(c("TRI"), c("cs10", 9, 10))])
+        ts(c("wi"), c("xi"), -361.5, A.add, 0.05, A.mult)
+        ts(c("w"), c("wi"), -0.5, A.max)
+        act(c("t20"), c("w"), -20.0, -351.0)
+        tt(c("h"), c("xi"), c("t20"), A.add)
         for x in range(10):
             ts(c("LH", 128 * x, 128 * x + 128), c("BLC"), c("w", x, x + 1), A.is_equal)
-        tt(c("xh"), c("xb"), c("hh"), A.mult)
-        scan(c("cs"), c("ONF", 0, 10), c("P5", 192, 202), A.mult, A.add)
-        tt(c("pre"), c("cs"), c("P5", 208, 218), A.add)
-        ts(c("prf"), c("pre"), float(CAP), A.is_le)
-        tt(c("HF", 0, 10), c("prf"), c("xh"), A.mult)
+        ts(c("prf"), c("cs10"), c("P5", 192, 193), A.add, 1024.0 * CAP, A.is_le)
+        tt(c("HF", 0, 10), c("prf"), c("h"), A.mult)
         tt(c("RH"), at(c("HF"), c("COFF", 0, 13)), c("IOT"), A.is_equal)
-        mms([(c("P6", 64, 84), c("LH", 128 * x, 128 * x + 128), c("RH", 20 * x, 20 * x + 20), x == 0, x == 9) for x in range(10)])
-        cp(c("CN%d" % t), c("P6", 64, 84))
+        total(c("P5", 256, 276), [(c("LH", 128 * x, 128 * x + 128), c("RH", 20 * x, 20 * x + 20)) for x in range(10)])
+        act(c("CN%d" % t), c("P5", 256, 276))
         send(rank + 1, rank - 1, c("CL%d" % t), c("CN%d" % t), "ac%d" % t)
-        cp(at(c(gw), c("PU", 0, 20)), c("RN"))
-        scan(c("GS"), c("FLB"), c(gw, 0, 2560), A.mult, A.max)
-        tt(c("ZA"), c(zw, 0, 160), c("GS", 15, 2560, 16), A.add)
-        ts(c("ZB"), c("ZA"), 1, A.arith_shift_right)
-        cp(c("ZS%d" % t), c("ZB"))
-        send(rank + 1 + t, rank - 1 - t, c("Z%d" % (t + 1), 0, 160), c("ZS%d" % t), "az%d" % (t + 1))
-        l1, ns, last = lists(par), half("NS", par), t == RO - 1
-        act(c("NKA"), ns, 1.0, c("LNN"), F.Abs)
-        act(c("NK"), c("NKA"), -1.0, c("ON1"), F.Relu)
-        act(c("JB", 160, 320), ns)
-        gather_lanes(c("P2", 144, 154), "JB", 160, 10)
-        ts(c("n15"), c("P2", 144, 154), 15.5 * 1024, A.is_le)
-        ts(c("ng"), c("gh"), 0.5, A.is_lt)
-        tt(c("cc"), c("inj"), c("n15"), A.mult)
-        tt(c("cd"), c("cc"), c("ng"), A.mult)
-        ts(c("op"), c("code"), 1.0, A.add)
-        ts(c("o2"), c("code"), 1, A.arith_shift_right)
-        tt(c("xi"), c("op"), c("cd"), A.mult)
-        ts(c("jh"), c("xi"), 496, A.bitwise_and)
-        ts(c("jl"), c("xi"), 15, A.bitwise_and)
-        cp(c("JHL", 0, 10), c("jh"))
-        cp(c("JHL", 10, 20), c("jl"))
-        mms([(c("P1", b, 160, 16), EX(b), c("JHL", 10 * h, 10 * h + 10), h == 0, h == 1) for b in range(16) for h in (0, 1)])
-        tt(c("JQ"), l1, c("P1", 0, 160), A.is_equal)
-        mms([(c("P3", 128, 288), c("B1"), c("JQ"), True, True)])
+        cp(at(c(gw), c("PU")), c("RN"))
+        scan(c("GS"), c("FLB"), c(gw, 320, 2880), A.mult, A.max)
+        total(PD, [(ID, c(zw, OFF + par, 352, 2)), (ID, c("GS", 15, 2560, 16))])
+        act(c("ZF"), PD, 0.4995, ROUND)
+        act(c("ZS2") if last else c("ZS%d" % t, OFF + 1 - par, 352, 2), c("ZF"), 1.0, -ROUND)
+        send(rank + 1 + t, rank - 1 - t, c("Z%d" % (t + 1)), c("ZS%d" % t), "az%d" % (t + 1))
+        l1, val = lists(par), c("VALN", par, 320, 2)
+        P1, PJ = c("P1", 320, 480), c("P7", 160, 320)
+        spread("P1", 320, c("xj"), 10)
+        tt(c("JQ"), P1, l1, A.is_equal)
+        act(c("P1C"), P1, 1.0, c("cp"), F.Identity)
+        total(PJ, [(ID, val), (c("SHB"), val), (c("B1N"), c("JQ")), (c("ID32"), c("P1C"))])
+        tt(l1, PJ, l1, A.max)
+        if t:
+            act(c("YL", par, 320, 2), l1, 1.0, -float(OFF))
+        else:
+            cp(half("AOU", 0), l1)
+            ts(val, l1, OFF - 0.5, A.is_ge, -131072.0, A.mult)
+            act(half("APR", 0), l1, 32.0, -432.0)
+            total(c("P0", OFF, 352), statics + [(lane("SS", 5), c("C16")), (lane("SS", 0), c("VALN"))])
+            act(c("ST", OFF, 352), c("P0", OFF, 352), 1.0 / 1024)
         if not last:
-            ts(c("p16"), c("pb"), 160.0, A.mult)
-            tt(c("k1"), c("p16"), c("o2"), A.add)
-            ts(c("k1"), c("k1"), 319.0, A.min)
-            cp(c("CU"), c("k1"))
-            act(c("JB", 0, 160), at(c("NT"), c("CU")))
-        ts(c("JA"), c("P3", 128, 288), 0.5, A.is_lt)
-        jv, jw = c("P1", 160, 320), c("P1", 320, 480)
-        tt(jv, c("JA"), c("P1", 0, 160), A.mult)
-        if not last:
-            act(c("JB", 320, 480), jv, 1.0, 0.0, F.Sign)
-            gather_lanes(c("P2", 96, 126), "JB", 0, 30)
-        tt(jw, c("NK"), jv, A.mult)
-        tt(l1, l1, jw, A.add)
-        act(c("YL", par, 320, 2), l1, 1.0, -1.0)
-        if not last:
-            if t == 0:
-                tt(ns, ns, c("JB", 320, 480), A.add)
-            act(c("J3"), c("P2", 96, 126))
-            ts(c("k2"), c("J3", 10, 20), -0.25, A.mult, 3680.0, A.add)
-            ts(c("k4"), c("pb"), float(1 - par), A.is_equal, 1.0 / 1024, A.mult)
-            tt(c("k6"), c("k2"), c("J3", 0, 10), A.add)
-            tt(c("k7"), c("k6"), c("o2"), A.add)
-            tt(c("k8"), c("k4"), c("J3", 20, 30), A.mult)
-            tt(c("k9"), c("k7"), c("k8"), A.mult)
-            kb = c("KB", 20 * (1 - par) + 10 * par, 20 * (1 - par) + 10 * par + 10)
-            tt(kb, kb, c("k9"), A.max)
-            mms([(c("P5", 224, 234), c("ALL1"), c("inj"), True, True)])
-            o, i = c("CC", 0, 1), c("P5", 224, 234)
-            vec(lambda o=o, i=i: g.vector.tensor_reduce(ap(o), ap(i), AxisListType.X, A.add), o, [i], 10)
-            cp(c("CCI"), o)
+            total(c("P5", 224, 234), [(c("ALL1", 0, 128), c("inj"))])
+            act(c("jk"), c("P5", 224, 234), total=c("CC", 0, 1))
+            cp(c("CCI"), c("CC", 0, 1))
             ts(c("CCJ"), c("CCI"), 31, A.bitwise_and)
             ts(c("CC", 1, 2), c("CCJ"), 64.0, A.mult, 15.0, A.add)
             inc = c("CC", 1, 2)
             cur[0] = 1 - par
-            ts(c("thr"), c("th64"), inc, A.add)
+            act(c("thr"), c("th64"), 1.0, inc, F.Identity)
             prep(t + 1)
-            if t == 0:
-                cur[0] = 0
-                ts(c("NT", 0, 160), c("NS", 0, 160), 4.0, A.mult, 4.0, A.add)
 
     cur[0] = (RO - 1) & 1
     pn = c("PN")
-    dma("Y", T.yl[:, :], ap(c("YL")), "d_yl", [c("YL")], [], 2.2)
+    dma("Y", T.yl[:, :], ap(c("YL")), "d_yl", [c("YL")], [], 1.8)
     cur[0] = RO & 1
     tt(c("SI"), pn, c("CL%d" % (RO - 1)), A.add)
-    ts(c("PJM", 0, 20), c("SI"), 15, A.bitwise_and)
-    cp(c("SO"), c("PJM", 0, 20))
-    spread("P0", c("SO"), 20)
-    for par in (0, 1):
-        cp(c("YD", par, 320, 2), c("P0", 160 * par, 160 * par + 160))
-    dma("S", T.yd[:, :], T["YD"][0:128:16, :], "d_yd", [c("YD")], [], 2.0)
-    dma("Y", T.yz[:, :], ap(c("Z%d" % RO, 0, 160)), "d_yz", [c("Z%d" % RO, 0, 160)], [], 2.2)
+    ts(c("PJ"), c("SI"), 15, A.bitwise_and)
+    cp(c("YD"), c("PJ"))
+    dma("S", T.yd[:, :], ap(c("YD")), "d_yd", [c("YD")], [], 1.6)
+    dma("Y", T.yz[:, :], ap(c("Z3")), "d_yz", [c("Z3")], [], 1.6)
 
     succ = [[] for _ in ops]
     for k, d in enumerate(ops):
@@ -649,7 +588,7 @@ def rank_program(g, core, T, topo):
     prio = [0.0] * len(ops)
     for k in range(len(ops) - 1, -1, -1):
         d = ops[k]
-        prio[k] = d["cost"] + d["lat"] + max([prio[s] + 0.06 for s in succ[k]], default=0.0)
+        prio[k] = d["cost"] + d["lat"] + max([prio[s] + GAP for s in succ[k]], default=0.0)
     left = [len(d["preds"]) for d in ops]
     ready = [0.0] * len(ops)
     pool = {q: [] for q in "VSTGYA"}
@@ -683,8 +622,7 @@ def rank_program(g, core, T, topo):
         end = s + d["cost"] + d["lat"]
         order.append(k)
         for x in succ[k]:
-            gap = 0.06 if ops[x]["preds"][k] else 0.0
-            ready[x] = max(ready[x], end + gap)
+            ready[x] = max(ready[x], end + (GAP if ops[x]["preds"][k] else 0.0))
             left[x] -= 1
             if not left[x]:
                 pool[ops[x]["q"]].append(x)

@@ -1,3 +1,4 @@
+import numpy as np
 from concourse.mybir import AluOpType as A, AxisListType, ActivationFunctionType as F
 
 N, RO, CAP = 8, 3, 28
@@ -25,23 +26,24 @@ def _put(name, width, kind):
 
 _CONST = (("b", (("SS", 144), ("IDW", 144), ("WM", 144), ("WP", 144), ("WD", 144), ("WN", 144), ("B1", 128), ("B1N", 128), ("OD", 128), ("DPM", 128), ("ID8", 128),
                  ("SHB", 128), ("BLC", 128), ("TRA", 128), ("TRI", 128), ("ALL1", 512), ("HI", 320), ("LO", 320), ("PI", 320), ("C16", 320), ("DUM", 32), ("D256", 32),
-                 ("R16", 320), ("VALN", 320), ("FL", 160), ("DR", 160), ("K512", 160), ("K15", 160), ("C185", 160), ("ST", 352))),
+                 ("R16", 320), ("VALN", 320), ("FL", 160), ("DR", 160), ("K512", 160), ("K15", 160), ("C185", 80), ("K10", 160), ("DR4", 80), ("ST", 672),
+                 ("C75", 320), ("CN75", 20), ("JK", 80), ("JC", 100))),
           ("f", (("WI", 144), ("BI", 128), ("ID32", 128), ("PF", 1), ("LN", 1), ("LG", 1), ("LG20", 1), ("cu", 1), ("c3", 1), ("c4", 1), ("cd", 1), ("cn", 1), ("cs", 1),
                  ("ck", 1), ("cj", 1), ("cp", 1), ("TI", 20), ("AC", 20), ("A17", 20), ("CM40", 40), ("MAJ", 320), ("M1V", 320), ("IOT", 208), ("CJF", 14), ("APR", 320),
                  ("R1", 320), ("AB", 320), ("R2", 320), ("BASE", 20), ("th64", 10), ("ON10", 10), ("YL", 320))),
           ("i", (("PI32", 1), ("LI", 1), ("LGI", 1), ("CJ", 14), ("KB0", 20), ("KB1", 20), ("KB2", 20))),
           ("u", (("AOU", 320), ("COFF", 14))),
-          ("h", (("NBH", 320), ("K10", 160), ("VY", 320))))
+          ("h", (("NBH", 320), ("VY", 320))))
 for _k, _l in _CONST:
     for _n, _w in _l:
         _put(_n, _w, _k)
 LOCAL = set()
-for _k, _l in (("f", (("EF", 20), ("V613", 20), ("V17", 20), ("X6", 20), ("MM", 100), ("BB", 40), ("pt", 20), ("pu", 20), ("PX", 20), ("U", 40), ("B60", 60), ("KIB", 40),
+for _k, _l in (("f", (("EF", 20), ("V613", 20), ("V17", 20), ("X6", 20), ("MM", 100), ("BB", 100), ("pt", 20), ("pu", 20), ("PX", 20), ("U", 60), ("B40", 40), ("KS", 80), ("NQ", 160),
                       ("PQ", 40), ("T1", 160), ("UE", 160), ("S1", 160), ("QE", 160), ("QY", 160), ("S2", 160), ("ZF", 160), ("P1C", 160), ("HF", 16), ("thr", 10),
-                      ("xi", 10), ("w", 10), ("t20", 10), ("h", 10), ("prf", 10), ("jk", 10), ("CC", 2))),
-                ("i", (("EI", 20), ("SI", 20), ("PJ", 20), ("SGI", 20), ("SGJ", 20), ("T6", 100), ("IX", 100), ("KJ", 40), ("KK", 20), ("PN", 20), ("IN", 40), ("IM", 40),
-                       ("UQ", 160), ("UF", 160), ("y", 10), ("code", 10), ("wi", 10), ("CCI", 1), ("CCJ", 1))),
-                ("b", (("XB", 100), ("SGN", 60), ("SGH", 20), ("QD", 640), ("ZE", 320), ("X", 1280), ("XO", 320), ("NXO", 320), ("XN", 320), ("RN", 320), ("OH", 320),
+                      ("SGR", 20), ("xi", 10), ("w", 10), ("t20", 10), ("h", 10), ("prf", 10), ("jk", 10), ("CC", 2))),
+                ("i", (("EI", 20), ("T6", 100), ("IX", 100), ("KK", 20), ("PN", 20), ("IN", 40), ("IM", 40),
+                       ("UQ", 160), ("UF", 160), ("wi", 10), ("CCI", 1), ("CCJ", 1))),
+                ("b", (("SGN", 60), ("QD", 640), ("ZE", 320), ("X", 1280), ("XO", 320), ("NXO", 320), ("XN", 320), ("RN", 320), ("OH", 320),
                        ("OEB", 320), ("RH", 208), ("LH", 1280), ("JQ", 160), ("JB", 160), ("inj", 10), ("xb", 10), ("cs10", 10))),
                 ("h", (("W3", 960), ("xj", 10))),
                 ("u", (("EOU", 40), ("PU", 20), ("IXU", 100), ("IXN", 40), ("UI", 160), ("CU", 10)))):
@@ -53,10 +55,10 @@ for _i in (0, 1):
     _own("DW%d" % _i, 672, "b")
     _own("GL%d" % _i, 352, "f")
     _own("GW%d" % _i, 2880, "b")
-    _own("OW%d" % _i, 2880, "b")
     _own("ZS%d" % _i, 352, "b")
-for _n, _w, _k in (("GLI", 320, "i"), ("NBI", 320, "i"), ("V5", 320, "i"), ("VAI", 20, "i"), ("THI", 10, "i"), ("ZL", 160, "b"), ("RW", 4112, "b"), ("EX", 2048, "b"),
-                   ("FLB", 2560, "b"), ("SG", 5120, "b"), ("GS", 2560, "b"), ("YD", 20, "f"), ("GDI", 20, "b"), ("ZS2", 160, "b"), ("Z3", 160, "b")):
+for _n, _w, _k in (("OW", 2880, "b"), ("GLI", 320, "i"), ("NBI", 320, "i"), ("V5", 320, "i"), ("VAI", 20, "i"), ("THI", 10, "i"), ("ZL", 160, "b"), ("RW", 4112, "b"), ("EX", 2048, "b"),
+                   ("FLB", 640, "b"), ("SG", 5120, "b"), ("GS", 2560, "b"), ("YD", 20, "f"), ("GDI", 20, "b"), ("SO0", 20, "b"), ("GH3", 20, "b"),
+                   ("ZS2", 160, "b"), ("Z3", 160, "b")):
     _own(_n, _w, _k)
 for _t in range(RO):
     _own("DX%d" % _t, 2880, "b")
@@ -66,11 +68,65 @@ for _t in range(RO):
 for _t in range(8):
     SCRATCH["P%d" % _t] = ("psum", [128, 512], "float32")
     VIEW["P%d" % _t] = ("P%d" % _t, 0, 512)
-SEMAPHORES = ["sV", "sS", "sT", "sG", "loc", "ac0", "ac1", "ac2", "ag0", "ag1", "ag2", "az1", "az2", "az3",
-              "d_gl", "d_v5", "d_va", "d_th", "d_nb", "d_zl", "d_rec", "d_a", "d_b", "d_x1", "d_x2", "d_o0", "d_o1", "d_yl", "d_yd", "d_yz"]
+SEMAPHORES = ["sV", "sS", "sT", "sG", "loc", "ac0", "ac1", "ac2", "ag0", "ag1", "ag2", "ag3", "az1", "az2", "az3",
+              "d_gl", "d_v5", "d_va", "d_th", "d_nb", "d_zl", "d_rec", "d_yl", "d_yd", "d_yz"] + ["d_z%d" % _t for _t in range(7)]
 
-CYC, PE, GAP, HOP = 0.00095, 0.00065, 0.09, 1.5
-FIRST = "VSSVSVSS"
+CYC, PE, GAP, HOP = 0.00088, 0.0005, 0.17, 1.7
+FIRST = ("VSVS", "SVSV")
+PIECE = 8
+
+
+ORDER = []
+PASSES, LEAN, SHAKE = 400, 1.0, 2.0
+
+
+def schedule(ops):
+    n = len(ops)
+    cost = [d["cost"] + (0.012 if d["q"] in "VSEGY" else 0.0) for d in ops]
+    before = [[(p, ops[p]["lat"] + (GAP if hard else 0.0)) for p, hard in d["preds"].items()] for d in ops]
+    after = [[] for _ in ops]
+    for k in range(n):
+        for p, lag in before[k]:
+            after[p].append((k, lag))
+
+    def lay(turn, needs, tail):
+        busy = {q: [] for q in "VSTGY"}
+        start, place = [0.0] * n, [d["q"] for d in ops]
+        for k in turn:
+            first = max([start[p] + cost[p] + lag for p, lag in needs[k]] + [tail[k]])
+            if place[k] == "A":
+                start[k] = first
+                continue
+            gaps = []
+            for q, late in ((("S", 0.0), ("V", LEAN)) if place[k] == "E" else ((place[k], 0.0),)):
+                line, s, j = busy[q], first, len(busy[q])
+                while j and line[j - 1][1] > s:
+                    j -= 1
+                while j < len(line) and line[j][0] < s + cost[k] - 1e-9:
+                    s = max(s, line[j][1])
+                    j += 1
+                gaps.append((s + late, s, j, q))
+            _, start[k], j, place[k] = min(gaps)
+            busy[place[k]].insert(j, (start[k], start[k] + cost[k]))
+        return start, place
+
+    lat = [d["lat"] for d in ops]
+    way = [0.0] * n
+    for k in range(n - 1, -1, -1):
+        way[k] = cost[k] + max([lag + way[s] for s, lag in after[k]] + [lat[k]])
+    turn, best = sorted(range(n), key=lambda k: (-way[k], k)), None
+    shake = np.random.default_rng(0)
+    for _ in range(PASSES):
+        fore, place = lay(turn, before, [0.0] * n)
+        end = max(fore[k] + cost[k] + lat[k] for k in range(n))
+        if best is None or end <= best[0]:
+            best = (end, fore, place)
+        key = [best[1][k] + cost[k] + x for k, x in enumerate((SHAKE * shake.random(n) ** 4).tolist())]
+        for k in range(n):
+            key[k] = max([key[k]] + [key[p] for p, _ in before[k]])
+        back = lay(sorted(range(n), key=lambda k: (-key[k], -k)), after, lat)[0]
+        turn = sorted(range(n), key=lambda k: (-back[k] - cost[k], k))
+    return [(k, best[2][k]) for k in sorted(range(n), key=lambda k: (best[1][k], k))]
 
 
 def rank_program(g, core, T, topo):
@@ -183,7 +239,11 @@ def rank_program(g, core, T, topo):
             node("S", [lambda: g.scalar.activation(opnd(out), opnd(a), func, bias=bias, scale=scale, accum_out=ap(total))], [out, total], [a], cost + 0.02)
 
     def fetch(q, out, win, off):
-        (cp if q == "V" else act)(out, at(win, off))
+        a = at(win, off)
+        if q != "E":
+            return (cp if q == "V" else act)(out, a)
+        node("E", {"V": lambda: g.vector.tensor_copy(opnd(out), opnd(a)), "S": lambda: g.scalar.activation(opnd(out), opnd(a), F.Copy)},
+             [out], [a], (70 + 1.56 * width(out)) * CYC)
 
     def scan(out, d0, d1, op0, op1):
         vec(lambda: g.vector.tensor_tensor_scan(ap(out), ap(d0), ap(d1), 0.0, op0, op1), out, [d0, d1], cyc(out, [d0, d1]))
@@ -238,8 +298,10 @@ def rank_program(g, core, T, topo):
     def blocks(w, src, lo, n, bs=range(16)):
         return [(lane(w, b), c(src, lo + n * b, lo + n * b + n)) for b in bs]
 
-    def spread(bank, lo, src, n):
-        mms([(c(bank, lo + n * b, lo + n * b + n), EX(b), src, True, True) for b in range(16)])
+    def spread(bank, lo, src, n, plus=None):
+        if plus:
+            total(c(bank, lo, lo + 16 * n), [(ID, plus)], stop=False)
+        mms([(c(bank, lo + n * b, lo + n * b + n), EX(b), src, not plus, not plus or b == 15) for b in range(16)])
 
     def half(n, par):
         return c(n, 160 * par, 160 * par + 160)
@@ -275,17 +337,19 @@ def rank_program(g, core, T, topo):
     for i in (0, 1):
         const(c("GL%d" % i, 0, OFF), -5)
     const(c("RW", 4096, 4112), 0)
-    const(c("DX0", 0, 960), 0)
-    for j, s in ((1, "d_a"), (2, "d_b")):
-        dma("Y", ap(c("DX0", 960 * j, 960 * j + 960)), ap(c("DX0", 0, 960)), s, [c("DX0", 0, 960)], [c("DX0", 960 * j, 960 * j + 960)], 2.2)
-    for n, s in (("OW0", "d_o0"), ("OW1", "d_o1"), ("DX1", "d_x1"), ("DX2", "d_x2")):
-        dma("Y", ap(c(n)), ap(c("DX0")), s, [c("DX0")], [c(n)], 4.0)
+    zero = c("DX2", 320, 1600)
+    fill(zero, 0.0)
+    for j, (n, lo) in enumerate((("OW", 320), ("OW", 1600), ("DX0", 320), ("DX0", 1600), ("DX1", 320), ("DX1", 1600), ("DX2", 1600))):
+        dma("Y", ap(c(n, lo, lo + 1280)), ap(zero), "d_z%d" % j, [zero], [c(n, lo, lo + 1280)], 3.0 + j)
     for n in ("Z0", "ZS0", "ZS1", "OD"):
         const(c(n), 0)
     const(c("ON10"), 1)
     const(c("C16"), 16)
     const(c("FLB"), 1)
-    const(c("FLB", 0, 2560, 16), 0)
+    const(c("FLB", 0, 640, 16), 0)
+    const(c("DR4"), 0)
+    const(c("DR4", 0, 80, 4), 262144)
+    const(c("K10"), OFF)
     for i in (1, 0):
         cur[0] = i
         const(c("HF"), 0)
@@ -334,7 +398,6 @@ def rank_program(g, core, T, topo):
     act(c("A17"), c("AC"), 2.0 / 64, 17.0 / 64)
     act(c("CM40", 0, 20), c("AC"), 2.0, 37.0)
     act(c("CM40", 20, 40), c("AC"), 2.0, 613.0)
-    ts(c("K10"), c("LO", 0, 160), -1024.0, A.mult, float(OFF), A.add)
     ts(c("VY"), c("M1V"), -596.0, A.add, 1.0 / 32, A.mult)
     ts(c("cj"), c("LN"), -9.5, A.add)
     ts(c("CJ"), c("CJF"), c("cj"), A.add, 0.05, A.mult)
@@ -353,6 +416,14 @@ def rank_program(g, core, T, topo):
     act(c("GL1", OFF), c("GL0", OFF))
     for n in ("DW1", "ST"):
         act(c(n, 0, OFF), c("DW0", 0, OFF))
+    total(c("P1", 0, 320), [(lane("SS", 4), c("C16"))])
+    act(c("ST", 352, 672), c("P1", 0, 320), -64.0)
+    for j, x in enumerate((1, 2, 3, 0)):
+        act(c("JK", 20 * j, 20 * j + 20), c("DUM", 0, 20), 0.0, x + 7.5)
+        act(c("JC", 20 * j, 20 * j + 20), c("DUM", 0, 20), 0.0, x - 0.5 if x else 7.5)
+    act(c("JC", 80, 100), c("DUM", 0, 20), 0.0, 7.5)
+    act(c("CN75"), c("DUM", 0, 20), 0.0, -7.5)
+    act(c("C75"), c("C16"), 7.5 / 16)
 
     def entries(par, win, queues, keys):
         for j, q in enumerate(queues):
@@ -363,9 +434,9 @@ def rank_program(g, core, T, topo):
                 nb = 16 // len(queues)
                 total(keys, ([(ID, c("K512"))] if j == 0 else []) + blocks("WM", "SG", 2560 * par, 160, range(nb * j, nb * j + nb)), j == 0, j == len(queues) - 1)
 
-    PK = (c("P2", 192, 352), c("P3", 320, 480))
+    PK = (c("P7", 320, 480), c("P3", 160, 320))
     for par in (0, 1):
-        entries(par, "DW0", FIRST[4 * par:4 * par + 4], PK[par])
+        entries(par, "DW0", FIRST[par], PK[par])
         scan(half("R1", par), c("FL"), PK[par], A.mult, A.max)
         cp(c("KB0", par, 20, 2), c("R1", 160 * par + 15, 160 * par + 160, 16))
     for par in (0, 1):
@@ -376,8 +447,8 @@ def rank_program(g, core, T, topo):
     NBP = c("P4", 0, 320)
     cp(c("NBH"), c("NBI"))
     mms([(c("P4", b, 320, 16), ID, c("NBH", 20 * b, 20 * b + 20), True, True) for b in range(16)])
-    cp(c("XB", 60, 80), c("VAI"))
-    act(c("GDI"), c("XB", 60, 80))
+    ts(c("SO0"), c("VAI"), -7.5, A.add)
+    act(c("GDI"), c("SO0"), 1.0, 7.5)
     send(rank - 1, rank + 1, c("GH0"), c("GDI"), "ag0")
     ts(c("th64"), c("THI"), 64.0, A.mult)
     act(c("thr"), c("th64"), 1.0, 15.0)
@@ -402,22 +473,26 @@ def rank_program(g, core, T, topo):
         act(c("V613"), c("EF"), 0.5, 137.25)
         act(c("V17"), c("EF"), 2.0, -47.0)
         act(c("X6"), c("EF"), 0.125, (63.0 - 8 * par) / 64)
-        tt(c("BB", 0, 20), c("AC"), c("V17"), A.mult)
+        tt(c("BB", 60, 80), c("AC"), c("V17"), A.mult)
         ts(c("EOU", 20, 40), po, 1.0 / 64, A.mult, float(OFF), A.add)
         tt(c("MM", 60, 80), pm, c("V613"), A.mult)
-        tt(c("BB", 20, 40), po, c("A17"), A.mult)
+        tt(c("BB", 80, 100), po, c("A17"), A.mult)
         tt(c("pt"), pm, c("X6"), A.mult)
         tt(c("pu"), pk, c("pt"), A.add)
         act(c("MM", 80, 100), po, 0.5, 592.0)
         act(c("MM", 40, 60), c("MM", 60, 80))
         act(c("MM", 0, 40), c("MM", 40, 80))
+        act(c("BB", 40, 60), c("BB", 60, 80))
+        act(c("BB", 0, 40), c("BB", 40, 80))
         tt(c("PX"), c("pu"), c("AC"), A.max)
         cp(c("PU"), c("PX"))
         total(c("P6", 64, 384), [(c("B1"), c("W3", 0, 320))])
         act(c("OH"), c("P6", 64, 384))
         total(c("P6", 64, 384), [(c("OD"), c("W3", 0, 320)), (c("DPM"), c("OH"))])
         act(c("OEB"), c("P6", 64, 384), 1.0 / 512)
-        cp(at(c("OW%d" % par), c("PU")), c("OEB"))
+        for h in (0, 10):
+            cp(at(c("OW"), c("PU", h, h + 10)), c("OEB", 16 * h, 16 * h + 160))
+        total(c("P7", 0, 160), [(ID, c("K10"))] + blocks("SS", "OW", 320, 160))
 
     prep(0)
 
@@ -426,20 +501,11 @@ def rank_program(g, core, T, topo):
         cur[0] = par
         zw, dw, gw, last = "Z%d" % t, "DW%d" % par, "GW%d" % par, t == RO - 1
         own = c(dw, OFF, 352)
-        so = c("XB", 60, 80)
+        so = c("CL%d" % (t - 1)) if t else c("SO0")
         if t:
-            cur[0] = 1 - par
-            pn = c("PN")
-            cur[0] = par
-            tt(c("SGI"), c("GH%d" % t), c("P5", 256, 276), A.add)
-            ts(c("SGJ"), c("SGI"), 15, A.bitwise_and)
-            cp(c("SGH"), c("SGJ"))
-            spread("P1", 0, c("SGH"), 20)
+            spread("P1", 0, c("CN%d" % (t - 1)), 20, c("C75"))
             act(c(dw, 352, 672), c("P1", 0, 320))
-            tt(c("SI"), pn, c("CL%d" % (t - 1)), A.add)
-            ts(c("PJ"), c("SI"), 15, A.bitwise_and)
-            cp(so, c("PJ"))
-            spread("P0", OFF, so, 20)
+            spread("P0", OFF, so, 20, c("C75"))
             if t == 1:
                 tt(own, c("P0", OFF, 352), c("ST", OFF, 352), A.min)
             else:
@@ -448,55 +514,58 @@ def rank_program(g, core, T, topo):
             spread("P1", 0, c("GH0"), 20)
             act(c(dw, 352, 672), c("P1", 0, 320))
         for j in (1, 2, 3):
-            act(c("XB", 20 * j - 20, 20 * j), so, 1.0, float(j))
-        act(c("XB", 80, 100), so)
-        act(c("SGN"), c("XB", 0, 60), 1.0, -15.5, F.Sign)
-        mms([(c("P2", 64, 164), ID, c("XB"), True, False), (c("P2", 64, 124), c("ID8"), c("ALL1", 0, 60), False, False),
-             (c("P2", 64, 124), c("ID8"), c("SGN"), False, True)])
+            act(c("SGN", 20 * j - 20, 20 * j), so, 1.0, j - 8.0, F.Sign)
+        mms([(c("P2", 64, 164), ID, c("JC"), True, False)] + [(c("P2", 64 + 20 * j, 84 + 20 * j), ID, so, False, False) for j in range(5)])
+        total(c("P2", 64, 124), [(c("ID8"), c("SGN"))], start=False)
         tp = lambda lo, hi: c("P4", 320 + lo, 320 + hi)
         tt(tp(0, 100), c("P2", 64, 164), c("MM"), A.mult)
-        fetch("S", c("QD"), c(dw), c("EOU"))
+        tt(tp(0, 100), tp(0, 100), c("BB"), A.add)
+        fetch("V", c("QD", 0, 320), c(dw, 0, 352), c("EOU", 0, 20))
+        fetch("S", c("QD", 320, 640), c(dw), c("EOU", 20, 40))
         total(c("P2", 0, 40), lanes16("WD", "QD", 0, 40))
-        tt(c("U"), c("P2", 0, 40), c("CM40"), A.mult)
-        tt(c("B60", 20, 60), c("U"), c("BB"), A.add)
-        tt(c("B60", 0, 20), c("U", 0, 20), c("BB", 0, 20), A.add)
-        tt(c("T6", 40, 100), tp(40, 100), c("B60"), A.add)
-        tt(c("T6", 0, 40), tp(0, 40), c("B60", 0, 40), A.add)
+        tt(c("U", 20, 60), c("P2", 0, 40), c("CM40"), A.mult)
+        tt(c("U", 0, 20), c("P2", 0, 20), c("CM40", 0, 20), A.mult)
+        tt(c("T6", 40, 100), tp(40, 100), c("U"), A.add)
+        tt(c("T6", 0, 40), tp(0, 40), c("U", 0, 40), A.add)
         ts(c("IX"), c("T6"), 4, A.arith_shift_right, 4095, A.bitwise_and)
         cp(c("IXU"), c("IX"))
+        tt(c("B40"), c("U", 20, 60), c("BB", 60, 100), A.add)
+        if t:
+            entries(par, dw, "E" * PIECE, None)
+        PD, PY = c("P3", 0, 160), c("P0", 352, 512)
+        total(PY, [(EX(5), c(dw, OFF + par, 352, 2)), (ID, c("VY", par, 320, 2))])
+        tt(c("T1"), PY, half("APR", par), A.mult)
+        for lo, hi in (((0, 80), (80, 160)) if t else ((0, 160),)):
+            pd = c("P3", lo, hi)
+            for hf in range(lo, hi, 80):
+                total(c("P3", hf, 80 + hf), [(ID, c("C185"))] + lanes16("WD", "SG", 2560 * par + 16 * hf, 80))
+            tt(pd, pd, c("M1V", par + 2 * lo, 2 * hi, 2), A.mult)
+            tt(c("UE", lo, hi), pd, c("T1", lo, hi), A.add)
+            ts(c("UQ", lo, hi), c("UE", lo, hi), 11018.5, A.add, 1.0 / 16, A.mult)
+            ts(c("UF", lo, hi), c("UQ", lo, hi), 4095 + 15 * 65536, A.bitwise_and)
+            ts(c("UI", lo, hi), c("UF", lo, hi), 4096.0, A.min)
+        n = 160 // PIECE
+        for lo in range(0, 160, n):
+            fetch("E", c(gw, 320 + 16 * lo, 320 + 16 * (lo + n)), c("RW"), c("UI", lo, lo + n))
+        if t == 1:
+            total(PK[1], [(ID, c("K512"))] + blocks("WM", "SG", 2560, 160))
+            scan(half("R1", 1), c("FL"), PK[1], A.mult, A.max)
         fetch("S", c("ZE"), c(zw), c("EOU", 0, 20))
         for j in range(4):
             tt(c("X", 320 * j, 320 * j + 320), at(c("RW", 0, 4096), c("IXU", 20 * j, 20 * j + 20)), c("ZE"), A.max)
-        total(c("P3", 0, 80), lanes16("SS", "X", 0, 80) + [(ID, c("XB", 0, 80))])
+            total(c("P2", 192 + j, 272, 4), [(ID, c("JK", 20 * j, 20 * j + 20)), (ID, so)] + lanes16("SS", "X", 320 * j, 20))
         tt(c("XO"), at(c("RW", 0, 4096), c("IXU", 80, 100)), c("ZE"), A.max)
         act(c("NXO"), c("XO"), -1.0)
-        act(c("KIB"), c("P3", 40, 80))
-        tt(c("KJ"), c("P3", 0, 40), c("KIB"), A.min)
-        tt(c("KK"), c("KJ", 0, 20), c("KJ", 20, 40), A.min)
+        scan(c("KS"), c("DR4"), c("P2", 192, 272), A.max, A.min)
+        cp(c("KK"), c("KS", 3, 80, 4))
         ts(c("PN"), c("KK"), 15, A.bitwise_and)
         tt(c("PQ", 20, 40), c("PN"), c("MM", 80, 100), A.mult)
         tt(c("PQ", 0, 20), c("PN"), c("MM", 60, 80), A.mult)
-        tt(c("IN"), c("PQ"), c("B60", 20, 60), A.add)
+        tt(c("IN"), c("PQ"), c("B40"), A.add)
         ts(c("IM"), c("IN"), 4, A.arith_shift_right, 4095, A.bitwise_and)
         cp(c("IXN"), c("IM"))
-        if not last:
-            cp(c("GD%d" % t), c("PN"))
-            send(rank - 1, rank + 1, c("GH%d" % (t + 1)), c("GD%d" % t), "ag%d" % (t + 1))
-        if t:
-            entries(par, dw, "SSSS", c("P2", 192, 352) if t == 1 else None)
-        PD, PY = c("P3", 128, 288), c("P0", 352, 512)
-        for hf in (0, 80):
-            total(c("P3", 128 + hf, 208 + hf), [(ID, c("C185", 0, 80))] + lanes16("WD", "SG", 2560 * par + 16 * hf, 80))
-        total(PY, [(EX(5), c(dw, OFF + par, 352, 2)), (ID, c("VY", par, 320, 2))])
-        tt(c("T1"), PY, half("APR", par), A.mult)
-        tt(PD, PD, c("M1V", par, 320, 2), A.mult)
-        tt(c("UE"), PD, c("T1"), A.add)
-        ts(c("UQ"), c("UE"), 11018.5, A.add, 1.0 / 16, A.mult)
-        ts(c("UF"), c("UQ"), 4095 + 15 * 65536, A.bitwise_and)
-        ts(c("UI"), c("UF"), 4096.0, A.min)
-        for hf in (0, 80):
-            fetch("S", c(gw, 320 + 16 * hf, 1600 + 16 * hf), c("RW"), c("UI", hf, hf + 80))
-        total(c("P7", 0, 160), [(ID, c("K10"))] + blocks("SS", "OW%d" % par, 320, 160))
+        cp(c("GD%d" % t), c("PN"))
+        send(rank - 1, rank + 1, c("GH%d" % (t + 1)), c("GD%d" % t), "ag%d" % (t + 1))
         tt(c("XN"), at(c("RW", 0, 4096), c("IXN", 20, 40)), c("ZE"), A.max)
         tt(at(c("DX%d" % t), c("PU")), c("XN"), c("NXO"), A.add)
         P5 = c("P5", 0, 160)
@@ -504,26 +573,25 @@ def rank_program(g, core, T, topo):
         fetch("S", c("RN"), c("RW", 0, 4096), c("IXN", 0, 20))
         scan(c("S1"), c("FL"), P5, A.mult, A.max)
         tt(c("QE"), P5, c("S1"), A.is_equal)
+        tt(c("NQ"), P5, c("S1"), A.not_equal)
         tt(c("QY"), c("P7", 0, 160), c("QE"), A.mult)
-        scan(c("S2"), c("FL"), c("QY"), A.mult, A.max)
+        scan(c("S2"), c("NQ"), c("QY"), A.mult, A.add)
         tt(c("inj"), c("S1", 15, 160, 16), c("thr"), A.is_gt)
-        cp(c("y"), c("S2", 15, 160, 16))
-        ts(c("code"), c("y"), 1023, A.bitwise_and)
-        tt(c("xi"), c("code"), c("inj"), A.mult)
+        tt(c("xi"), c("S2", 15, 160, 16), c("inj"), A.mult)
         ts(c("xb"), c("xi"), 351.5, A.is_ge, 1024.0, A.mult)
         tt(c("xj"), c("xi"), c("xb"), A.subtract)
         if not last:
-            cp(c("CU"), c("xj"))
+            if t == 1:
+                entries(0, "ST", "E" * PIECE, c("P6", 64, 224))
+                scan(half("R1", 0), c("FL"), c("P6", 64, 224), A.mult, A.max)
+                cp(c("KB2", 0, 20, 2), c("R1", 15, 160, 16))
+            cp(c("CU"), c("xi"))
             total(c("P6", 400, 410), [(c("ID32"), c("BASE", par, 20, 2))], stop=False)
-            fetch("S", c("JB"), c(dw, 0, 352), c("CU"))
+            fetch("S", c("JB"), c("ST" if par else dw), c("CU"))
             total(c("P6", 400, 410), lanes16("WM" if par else "WP", "JB", 0, 10), start=False)
             if t == 0:
                 tt(c("KB1", 0, 20, 2), c("P6", 400, 410), c("KB1", 0, 20, 2), A.max)
             else:
-                scan(half("R1", 1), c("FL"), c("P2", 192, 352), A.mult, A.max)
-                entries(0, "ST", "SSSS", c("P2", 352, 512))
-                scan(half("R1", 0), c("FL"), c("P2", 352, 512), A.mult, A.max)
-                cp(c("KB2", 0, 20, 2), c("R1", 15, 160, 16))
                 tt(c("KB2", 1, 20, 2), c("P6", 400, 410), c("R1", 175, 320, 16), A.max)
         scan(c("cs10"), c("ON10"), c("xb"), A.mult, A.add)
         total(c("P5", 192, 193), [(c("TRI"), c("cs10", 9, 10))])
@@ -536,11 +604,15 @@ def rank_program(g, core, T, topo):
         ts(c("prf"), c("cs10"), c("P5", 192, 193), A.add, 1024.0 * CAP, A.is_le)
         tt(c("HF", 0, 10), c("prf"), c("h"), A.mult)
         tt(c("RH"), at(c("HF"), c("COFF", 0, 13)), c("IOT"), A.is_equal)
-        total(c("P5", 256, 276), [(c("LH", 128 * x, 128 * x + 128), c("RH", 20 * x, 20 * x + 20)) for x in range(10)])
-        act(c("CN%d" % t), c("P5", 256, 276))
+        new = c("P5", 256, 276)
+        total(new, [(ID, c("CN75")), (ID, c("GH%d" % (t + 1)))] + [(c("LH", 128 * x, 128 * x + 128), c("RH", 20 * x, 20 * x + 20)) for x in range(10)])
+        ts(c("SGR"), new, 16 * ROUND, A.add, -16 * ROUND, A.add)
+        tt(c("CN%d" % t), new, c("SGR"), A.subtract)
         send(rank + 1, rank - 1, c("CL%d" % t), c("CN%d" % t), "ac%d" % t)
-        cp(at(c(gw), c("PU")), c("RN"))
-        scan(c("GS"), c("FLB"), c(gw, 320, 2880), A.mult, A.max)
+        for h in (0, 10):
+            cp(at(c(gw), c("PU", h, h + 10)), c("RN", 16 * h, 16 * h + 160))
+        for lo in range(0, 2560, 640):
+            scan(c("GS", lo, lo + 640), c("FLB"), c(gw, 320 + lo, 960 + lo), A.mult, A.max)
         total(PD, [(ID, c(zw, OFF + par, 352, 2)), (ID, c("GS", 15, 2560, 16))])
         act(c("ZF"), PD, 0.4995, ROUND)
         act(c("ZS2") if last else c("ZS%d" % t, OFF + 1 - par, 352, 2), c("ZF"), 1.0, -ROUND)
@@ -571,69 +643,23 @@ def rank_program(g, core, T, topo):
             act(c("thr"), c("th64"), 1.0, inc, F.Identity)
             prep(t + 1)
 
-    cur[0] = (RO - 1) & 1
-    pn = c("PN")
     dma("Y", T.yl[:, :], ap(c("YL")), "d_yl", [c("YL")], [], 1.8)
-    cur[0] = RO & 1
-    tt(c("SI"), pn, c("CL%d" % (RO - 1)), A.add)
-    ts(c("PJ"), c("SI"), 15, A.bitwise_and)
-    cp(c("YD"), c("PJ"))
+    act(c("YD"), c("CL%d" % (RO - 1)), 1.0, 7.5)
     dma("S", T.yd[:, :], ap(c("YD")), "d_yd", [c("YD")], [], 1.6)
     dma("Y", T.yz[:, :], ap(c("Z3")), "d_yz", [c("Z3")], [], 1.6)
 
-    succ = [[] for _ in ops]
-    for k, d in enumerate(ops):
-        for p in d["preds"]:
-            succ[p].append(k)
-    prio = [0.0] * len(ops)
-    for k in range(len(ops) - 1, -1, -1):
-        d = ops[k]
-        prio[k] = d["cost"] + d["lat"] + max([prio[s] + GAP for s in succ[k]], default=0.0)
-    left = [len(d["preds"]) for d in ops]
-    ready = [0.0] * len(ops)
-    pool = {q: [] for q in "VSTGYA"}
-    for k, d in enumerate(ops):
-        if not left[k]:
-            pool[d["q"]].append(k)
-    free = {q: 0.0 for q in pool}
-    order = []
-    while len(order) < len(ops):
-        best = None
-        for q in pool:
-            if not pool[q]:
-                continue
-            start = lambda k: ready[k] if q == "A" else max(free[q], ready[k])
-            k = min(pool[q], key=lambda k: (start(k), -prio[k], k))
-            for _ in range(6):
-                s = start(k)
-                up = [j for j in pool[q] if prio[j] > prio[k] and s < start(j) < s + 0.6 * ops[k]["cost"]]
-                if q == "A" or not up:
-                    break
-                j = max(up, key=lambda j: (prio[j], -j))
-                fit = [i for i in pool[q] if i != k and start(i) + ops[i]["cost"] <= start(j)]
-                k = max(fit, key=lambda i: (prio[i], -i)) if fit else j
-            key = (start(k), -prio[k], k)
-            if best is None or key < best[0]:
-                best = (key, q, k)
-        (s, _, k), q, _ = best
-        pool[q].remove(k)
-        d = ops[k]
-        free[q] = s + d["cost"] + 0.012
-        end = s + d["cost"] + d["lat"]
-        order.append(k)
-        for x in succ[k]:
-            ready[x] = max(ready[x], end + (GAP if ops[x]["preds"][k] else 0.0))
-            left[x] -= 1
-            if not left[x]:
-                pool[ops[x]["q"]].append(x)
+    if not ORDER:
+        ORDER.extend(schedule(ops))
+    order = ORDER
 
     count = {q: 0 for q in "VSTG"}
     clock = {q: {} for q in "VSTGY"}
     token = [None] * len(ops)
     sent = 0
-    for k in order:
+    for k, q in order:
         d = ops[k]
-        q = d["q"]
+        if d["q"] == "E":
+            d["calls"] = [d["calls"][q]]
         if q == "A":
             token[k] = (d["sem"], d["amount"], {d["sem"]: d["amount"]})
             continue

@@ -24,29 +24,29 @@ def _put(name, width, kind):
     SCRATCH[tag] = ("sbuf", [128, _fill[tag]], _TYPES[kind])
 
 
-_CONST = (("b", (("SS", 144), ("IDW", 144), ("WM", 144), ("WP", 144), ("WD", 144), ("WN", 144), ("B1", 128), ("B1N", 128), ("OD", 128), ("DPM", 128), ("ID8", 128),
+_CONST = (("b", (("SS", 144), ("IDW", 144), ("WM", 144), ("WP", 144), ("WD", 144), ("WN", 144), ("B1", 128), ("B1N", 128), ("OD", 128), ("DPM", 128), ("ID8", 128), ("IDN", 128), ("IDH", 128), ("CNH", 160),
                  ("SHB", 128), ("BLC", 128), ("TRA", 128), ("TRI", 128), ("ALL1", 512), ("HI", 320), ("LO", 320), ("PI", 320), ("C16", 320), ("DUM", 32), ("D256", 32),
                  ("R16", 320), ("VALN", 320), ("FL", 160), ("DR", 160), ("K512", 160), ("K15", 160), ("C185", 80), ("K10", 160), ("DR4", 80), ("ST", 672),
-                 ("C75", 320), ("CN75", 20), ("JK", 80), ("JC", 100))),
-          ("f", (("WI", 144), ("BI", 128), ("ID32", 128), ("PF", 1), ("LN", 1), ("LG", 1), ("LG20", 1), ("cu", 1), ("c3", 1), ("c4", 1), ("cd", 1), ("cn", 1), ("cs", 1),
-                 ("ck", 1), ("cj", 1), ("cp", 1), ("TI", 20), ("AC", 20), ("A17", 20), ("CM40", 40), ("MAJ", 320), ("M1V", 320), ("IOT", 208), ("CJF", 14), ("APR", 320),
+                 ("W1", 144), ("WO", 144), ("D6", 128), ("S6", 128), ("EX5", 2048), ("CN75", 20), ("JK", 80), ("JC", 80), ("C72", 20), ("X16", 20), ("LX", 352))),
+          ("f", (("WI", 144), ("VY", 320), ("ID32", 128), ("PF", 1), ("LN", 1), ("LG", 1), ("LG20", 1), ("cu", 1), ("c3", 1), ("c4", 1), ("cd", 1), ("cn", 1), ("cs", 1),
+                 ("ck", 1), ("c75", 1), ("c6", 1), ("c6n", 1), ("co", 1), ("cj", 1), ("cp", 1), ("TI", 20), ("AC", 20), ("A17", 20), ("AC4", 80), ("CM4", 20), ("CM40", 40), ("MAJ", 320), ("M1V", 320), ("IOT", 208), ("CJF", 14), ("APR", 320),
                  ("R1", 320), ("AB", 320), ("R2", 320), ("BASE", 20), ("th64", 10), ("ON10", 10), ("YL", 320))),
           ("i", (("PI32", 1), ("LI", 1), ("LGI", 1), ("CJ", 14), ("KB0", 20), ("KB1", 20), ("KB2", 20))),
           ("u", (("AOU", 320), ("COFF", 14))),
-          ("h", (("NBH", 320), ("VY", 320))))
+          ("h", (("NBH", 320),)))
 for _k, _l in _CONST:
     for _n, _w in _l:
         _put(_n, _w, _k)
 LOCAL = set()
-for _k, _l in (("f", (("EF", 20), ("V613", 20), ("V17", 20), ("X6", 20), ("MM", 100), ("BB", 100), ("pt", 20), ("pu", 20), ("PX", 20), ("U", 60), ("B40", 40), ("KS", 80), ("NQ", 160),
+for _k, _l in (("f", (("X6", 20), ("MM", 100), ("BB", 100), ("pt", 20), ("pu", 20), ("PX", 20), ("U", 60), ("B40", 40), ("KS", 80), ("NQ", 160),
                       ("PQ", 40), ("T1", 160), ("UE", 160), ("S1", 160), ("QE", 160), ("QY", 160), ("S2", 160), ("ZF", 160), ("P1C", 160), ("HF", 16), ("thr", 10),
                       ("SGR", 20), ("xi", 10), ("w", 10), ("t20", 10), ("h", 10), ("prf", 10), ("jk", 10), ("CC", 2))),
                 ("i", (("EI", 20), ("T6", 100), ("IX", 100), ("KK", 20), ("PN", 20), ("IN", 40), ("IM", 40),
                        ("UQ", 160), ("UF", 160), ("wi", 10), ("CCI", 1), ("CCJ", 1))),
-                ("b", (("SGN", 60), ("QD", 640), ("ZE", 320), ("X", 1280), ("XO", 320), ("NXO", 320), ("XN", 320), ("RN", 320), ("OH", 320),
+                ("b", (("SGN", 60), ("NMB", 20), ("LM", 320), ("XR", 320), ("QD", 640), ("ZE", 320), ("X", 1280), ("XO", 320), ("NXO", 320), ("XN", 320), ("RN", 320), ("OH", 320),
                        ("OEB", 320), ("RH", 208), ("LH", 1280), ("JQ", 160), ("JB", 160), ("inj", 10), ("xb", 10), ("cs10", 10))),
-                ("h", (("W3", 960), ("xj", 10))),
-                ("u", (("EOU", 40), ("PU", 20), ("IXU", 100), ("IXN", 40), ("UI", 160), ("CU", 10)))):
+                ("h", (("W3", 960), ("EH", 20), ("xj", 10))),
+                ("u", (("EOU", 40), ("XU", 20), ("EZU", 20), ("PU", 20), ("IXU", 100), ("IXN", 40), ("UI", 160), ("CU", 10)))):
     for _n, _w in _l:
         LOCAL.add(_n)
         for _i in (0, 1):
@@ -55,14 +55,14 @@ for _i in (0, 1):
     _own("DW%d" % _i, 672, "b")
     _own("GL%d" % _i, 352, "f")
     _own("GW%d" % _i, 2880, "b")
-    _own("ZS%d" % _i, 352, "b")
 for _n, _w, _k in (("OW", 2880, "b"), ("GLI", 320, "i"), ("NBI", 320, "i"), ("V5", 320, "i"), ("VAI", 20, "i"), ("THI", 10, "i"), ("ZL", 160, "b"), ("RW", 4112, "b"), ("EX", 2048, "b"),
-                   ("FLB", 640, "b"), ("SG", 5120, "b"), ("GS", 2560, "b"), ("YD", 20, "f"), ("GDI", 20, "b"), ("SO0", 20, "b"), ("GH3", 20, "b"),
-                   ("ZS2", 160, "b"), ("Z3", 160, "b")):
+                   ("FLB", 320, "b"), ("SG", 5120, "b"), ("GS", 2560, "b"), ("YD", 20, "f"), ("GDI", 20, "b"), ("SO0", 20, "b"), ("GH3", 20, "b"),
+                   ("Z3", 176, "b")):
     _own(_n, _w, _k)
 for _t in range(RO):
     _own("DX%d" % _t, 2880, "b")
-    _own("Z%d" % _t, 352, "b")
+    _own("Z%d" % _t, 176, "b")
+    _own("ZS%d" % _t, 160, "b")
     for _n in ("CN", "CL", "GD", "GH"):
         _own("%s%d" % (_n, _t), 20, "b")
 for _t in range(8):
@@ -73,11 +73,16 @@ SEMAPHORES = ["sV", "sS", "sT", "sG", "loc", "ac0", "ac1", "ac2", "ag0", "ag1", 
 
 CYC, PE, GAP, HOP = 0.00088, 0.0005, 0.17, 1.7
 FIRST = ("VSVS", "SVSV")
-PIECE = 8
+AID = 0
+AHEAD = 0
+OL = ()
+MASK = (1, 2)
+PIECE = 4
 
 
 ORDER = []
-PASSES, LEAN, SHAKE = 400, 1.0, 2.0
+PASSES, LEAN, SHAKE = 600, 0.3, 3.0
+MOVES = 30000
 
 
 def schedule(ops):
@@ -116,17 +121,81 @@ def schedule(ops):
         way[k] = cost[k] + max([lag + way[s] for s, lag in after[k]] + [lat[k]])
     turn, best = sorted(range(n), key=lambda k: (-way[k], k)), None
     shake = np.random.default_rng(0)
-    for _ in range(PASSES):
+    held = None
+    for it in range(PASSES):
         fore, place = lay(turn, before, [0.0] * n)
         end = max(fore[k] + cost[k] + lat[k] for k in range(n))
         if best is None or end <= best[0]:
             best = (end, fore, place)
-        key = [best[1][k] + cost[k] + x for k, x in enumerate((SHAKE * shake.random(n) ** 4).tolist())]
+        if held is None or end <= held[0] + 0.2 * (1 - it / PASSES) * shake.exponential():
+            held = (end, fore)
+        done = np.array(held[1]) + np.array(cost)
+        key = (done + np.where(np.abs(done - shake.random() * held[0]) < 5, SHAKE * shake.random(n) ** 3, 0.0)).tolist()
         for k in range(n):
             key[k] = max([key[k]] + [key[p] for p, _ in before[k]])
         back = lay(sorted(range(n), key=lambda k: (-key[k], -k)), after, lat)[0]
         turn = sorted(range(n), key=lambda k: (-back[k] - cost[k], k))
-    return [(k, best[2][k]) for k in sorted(range(n), key=lambda k: (best[1][k], k))]
+    def clock(seq, place):
+        fin, why, last = [0.0] * n, [-1] * n, {}
+        for k in seq:
+            s, w = 0.0, -1
+            for p, lag in before[k]:
+                if fin[p] + lag > s:
+                    s, w = fin[p] + lag, p
+            q = place[k]
+            if q != "A":
+                j = last.get(q)
+                if j is not None and fin[j] > s:
+                    s, w = fin[j], j
+                last[q] = k
+            fin[k], why[k] = s + cost[k], w
+        e = max(range(n), key=lambda k: fin[k] + lat[k])
+        return fin[e] + lat[e], fin, why, e
+
+    def closure(k, links, inside):
+        found, stack = {k}, [k]
+        while stack:
+            for x, _ in links[stack.pop()]:
+                if inside(x) and x not in found:
+                    found.add(x)
+                    stack.append(x)
+        return found
+
+    seq, place = sorted(range(n), key=lambda k: (best[1][k], k)), best[2]
+    held = clock(seq, place)
+    best = (held[0], seq, place)
+    for it in range(MOVES):
+        pairs, k = [], held[3]
+        while held[2][k] >= 0:
+            if held[2][k] not in ops[k]["preds"]:
+                pairs.append((held[2][k], k))
+            k = held[2][k]
+        if not pairs:
+            break
+        a, b = pairs[int(shake.random() * len(pairs))]
+        pos = {k: i for i, k in enumerate(seq)}
+        i, j, far, kind = pos[a], pos[b], int(shake.random() ** 3 * 30), shake.random()
+        seq2, place2 = list(seq), place
+        free = [x for x in (a, b) if ops[x]["q"] == "E"]
+        if kind < 0.15 and free:
+            x = free[int(shake.random() * len(free))]
+            place2 = list(place)
+            place2[x] = "V" if place[x] == "S" else "S"
+        elif kind < 0.55:
+            i = max(0, i - far)
+            go = closure(b, before, lambda x: pos[x] >= i)
+            seq2[i:j + 1] = [k for k in seq[i:j + 1] if k in go] + [k for k in seq[i:j + 1] if k not in go]
+        else:
+            j = min(n - 1, j + far)
+            go = closure(a, after, lambda x: pos[x] <= j)
+            seq2[i:j + 1] = [k for k in seq[i:j + 1] if k not in go] + [k for k in seq[i:j + 1] if k in go]
+        new = clock(seq2, place2)
+        if new[0] <= held[0] + 0.08 * (1 - it / MOVES) * shake.exponential():
+            held, place = new, place2
+            seq = sorted(seq2, key=lambda k: new[1][k] - cost[k]) if it % 20 == 0 else seq2
+            if new[0] < best[0]:
+                best = (new[0], seq2, place2)
+    return [(k, best[2][k]) for k in best[1]]
 
 
 def rank_program(g, core, T, topo):
@@ -137,6 +206,7 @@ def rank_program(g, core, T, topo):
     queue = {"V": g.vector, "S": g.scalar, "T": g.tensor, "G": g, "Y": g.sync}
     cur = [0]
     ops = []
+    first = []
     acc = {}
 
     def c(name, lo=0, hi=None, step=1):
@@ -179,6 +249,8 @@ def rank_program(g, core, T, topo):
             acc[name].append([lo, hi, step, 1, k])
         for (name, lo, hi, step) in r:
             acc.setdefault(name, []).append([lo, hi, step, 0, k])
+        for p in first:
+            preds.setdefault(p, False)
         d = {"q": q, "calls": calls, "preds": preds, "cost": cost, "lat": lat}
         d.update(kw)
         ops.append(d)
@@ -265,10 +337,11 @@ def rank_program(g, core, T, topo):
         else:
             gps(lambda: g.iota(ap(v), pattern, base, cm), v, [], 0.15)
 
-    def const(v, x):
-        for lo in range(v[1], v[2], 480 * v[3]):
-            p = (v[0], lo, min(v[2], lo + 480 * v[3]), v[3])
-            iota(p, [[0, width(p)]], x, 0)
+    def const(v, x, q="S"):
+        if q == "G":
+            iota(v, [[0, width(v)]], x, 0)
+        else:
+            act(v, c("ALL1", 0, width(v)), float(x))
 
     def select(out, a, pattern, op, base, cm):
         gps(lambda: g.affine_select(ap(out), ap(a), pattern, op, 0.0, base, cm), out, [a], 0.2)
@@ -284,7 +357,7 @@ def rank_program(g, core, T, topo):
                  sent=len(topo.engines(core, dst)))
         n = len(topo.engines(cores[src_rank % N], core))
         ops.append({"q": "A", "calls": [], "preds": {k: False}, "cost": 0.0, "lat": HOP, "sem": sem, "amount": n})
-        acc[out_v[0]] = [[out_v[1], out_v[2], 1, 1, len(ops) - 1]]
+        acc.setdefault(out_v[0], []).append([out_v[1], out_v[2], 1, 1, len(ops) - 1])
 
     def lane(w, b):
         return c(w, 15 - b, 143 - b)
@@ -303,6 +376,8 @@ def rank_program(g, core, T, topo):
             total(c(bank, lo, lo + 16 * n), [(ID, plus)], stop=False)
         mms([(c(bank, lo + n * b, lo + n * b + n), EX(b), src, not plus, not plus or b == 15) for b in range(16)])
 
+    FL = c("FLB", 0, 160)
+
     def half(n, par):
         return c(n, 160 * par, 160 * par + 160)
 
@@ -315,44 +390,46 @@ def rank_program(g, core, T, topo):
     dma("S", ap(c("VAI")), T.val[:, :], "d_va", [], [c("VAI")], 1.6)
     dma("Y", ap(c("NBI")), T.nb[:, :], "d_nb", [], [c("NBI")], 2.0)
     dma("Y", ap(c("THI")), T.th[:, :], "d_th", [], [c("THI")], 1.8)
-    dma("Y", ap(c("ZL")), T.zl[:, :], "d_zl", [], [c("ZL")], 2.0)
+    dma("Y", ap(c("Z0", 16, 176)), T.zl[:, :], "d_zl", [], [c("Z0", 16, 176)], 2.0)
     dma("Y", ap(c("RW", 0, 4096)), T.rec[:, :], "d_rec", [], [c("RW", 0, 4096)], 6.0)
 
     iota(c("PI32"), [[0, 1]], 0, 1)
     iota(c("WI"), [[1, 144]], -15, 0)
     iota(c("HI"), [[-16, 20], [0, 16]], -OFF, 0)
     iota(c("LO"), [[0, 20], [-1, 16]], 0, 0)
-    iota(c("K512"), [[0, 10], [-512, 16]], 7680, 0)
+    fill(c("ALL1"), 1.0)
+    act(c("K512"), c("LO", 0, 160), 512.0, 7680.0)
     iota(c("TI"), [[1, 20]], 0, 20)
-    iota(c("BI"), [[16, 8], [0, 16]], 0, 0)
     iota(c("MAJ"), [[1, 20], [20, 16]], OFF, 0)
     iota(c("M1V"), [[2, 320]], 613, 0)
-    iota(c("K15"), [[0, 10], [-1, 16]], 15, 0)
+    act(c("K15"), c("LO", 0, 160), 1.0, 15.0)
     iota(c("IOT", 0, 200), [[0, 10], [1, 20]], 1, 0)
-    const(c("IOT", 200, 208), -1)
+    const(c("IOT", 200, 208), -1, "G")
     iota(c("CJF"), [[16, 14]], 0, 0)
-    const(c("ALL1"), 1)
     for b in range(0, 16, 4):
         select(c("EX", 128 * b, 128 * b + 512), c("ALL1"), [[-1, 4], [-16, 8], [0, 16]], A.is_equal, -b, 1)
     for i in (0, 1):
         const(c("GL%d" % i, 0, OFF), -5)
-    const(c("RW", 4096, 4112), 0)
+    const(c("RW", 4096, 4112), 0, "G")
     zero = c("DX2", 320, 1600)
-    fill(zero, 0.0)
+    for lo in (320, 960):
+        iota(c("DX2", lo, lo + 640), [[0, 640]], 0, 0)
     for j, (n, lo) in enumerate((("OW", 320), ("OW", 1600), ("DX0", 320), ("DX0", 1600), ("DX1", 320), ("DX1", 1600), ("DX2", 1600))):
         dma("Y", ap(c(n, lo, lo + 1280)), ap(zero), "d_z%d" % j, [zero], [c(n, lo, lo + 1280)], 3.0 + j)
-    for n in ("Z0", "ZS0", "ZS1", "OD"):
-        const(c(n), 0)
-    const(c("ON10"), 1)
-    const(c("C16"), 16)
+    for t in range(RO):
+        const(c("Z%d" % t, 0, 16), 0, "G")
+    const(c("OD"), 0, "G")
+    const(c("CNH"), -0.5)
+    const(c("ON10"), 1, "G")
+    const(c("C16"), 16, "G")
     const(c("FLB"), 1)
-    const(c("FLB", 0, 640, 16), 0)
+    const(c("FLB", 0, 320, 16), 0)
     const(c("DR4"), 0)
-    const(c("DR4", 0, 80, 4), 262144)
-    const(c("K10"), OFF)
+    const(c("DR4", 0, 80, 4), 1048576)
+    const(c("K10"), OFF, "G")
     for i in (1, 0):
         cur[0] = i
-        const(c("HF"), 0)
+        const(c("HF"), 0, "G")
 
     ts(c("LI"), c("PI32"), 15, A.bitwise_and)
     ts(c("LGI"), c("PI32"), 112, A.bitwise_and)
@@ -361,14 +438,12 @@ def rank_program(g, core, T, topo):
     cp(c("PF"), c("PI32"))
     ts(c("SS"), c("WI"), c("LG"), A.is_equal, 64.0, A.mult)
     ts(c("IDW"), c("WI"), c("PF"), A.is_equal)
-    fill(c("PI", 0, 320, 2), 0.0)
-    fill(c("PI", 1, 320, 2), -524288.0)
-    fill(c("DUM"), -1048576.0)
-    fill(c("D256", 0, 31), 0.0)
-    fill(c("D256", 31, 32), 256.0)
-    fill(c("FL"), 1.0)
-    fill(c("FL", 0, 160, 16), 0.0)
-    fill(c("C185"), -18.5)
+    const(c("PI", 0, 320, 2), 0.0)
+    const(c("PI", 1, 320, 2), -524288.0)
+    const(c("DUM"), -1048576.0)
+    const(c("D256", 0, 31), 0.0)
+    const(c("D256", 31, 32), 256.0)
+    const(c("C185"), -18.5)
     ts(c("cu"), c("LN"), 4.5, A.is_le, 1.0 / 32, A.mult)
     for n, col, lim in (("WM", "c3", 2.5), ("WP", "c4", 3.5)):
         ts(c(col), c("LN"), lim, A.is_ge, 0.5, A.subtract)
@@ -378,27 +453,32 @@ def rank_program(g, core, T, topo):
     ts(c("cn"), c("LN"), 15.0, A.is_equal, 1.0 / 32, A.mult)
     ts(c("cn"), c("cn"), 1.0 / 16384, A.max)
     act(c("WN"), c("SS"), c("cn"))
-    ts(c("B1"), c("BI"), c("LG"), A.is_equal)
+    select(c("TRA"), c("ALL1", 0, 128), [[16, 8], [0, 16]], A.is_ge, 15, -1)
+    select(c("B1"), c("TRA"), [[-16, 8], [0, 16]], A.is_ge, 0, 1)
+    select(c("TRI"), c("B1"), [[1, 128]], A.is_gt, 0, -1)
     ts(c("BLC"), c("WI", 15, 143), c("LG"), A.subtract)
-    ts(c("TRA"), c("BLC"), c("LN"), A.is_gt)
-    tt(c("TRI"), c("TRA"), c("B1"), A.mult)
     act(c("B1N"), c("B1"), -1024.0)
     act(c("OD", 1, 128, 2), c("B1", 1, 128, 2))
     act(c("DPM", 0, 128, 2), c("IDW", 15, 143, 2))
     act(c("DPM", 1, 128, 2), c("IDW", 16, 143, 2), -1.0)
     act(c("ID8"), ID, -8.0)
     act(c("ID32"), ID)
+    act(c("IDN"), ID, -1.0)
+    act(c("IDH"), ID, 0.5)
     ts(c("cs"), c("LN"), 15.0, A.not_equal, -1.0, A.mult)
     act(c("SHB"), c("IDW", 14, 142), c("cs"))
     ts(c("cp"), c("LN"), 0.5, A.is_ge, -131072.0, A.mult)
     ts(c("ck"), c("LN"), 1.0, A.add, 1.0 / 64, A.mult)
-    act(c("DR"), c("FL"), -262144.0, 262144.0)
+    act(c("DR"), FL, -262144.0, 262144.0)
     ts(c("LG20"), c("LG"), -20.0, A.mult)
     ts(c("AC"), c("TI"), c("LG20"), A.add)
     act(c("A17"), c("AC"), 2.0 / 64, 17.0 / 64)
+    for j in range(4):
+        act(c("AC4", 20 * j, 20 * j + 20), c("AC"))
     act(c("CM40", 0, 20), c("AC"), 2.0, 37.0)
     act(c("CM40", 20, 40), c("AC"), 2.0, 613.0)
-    ts(c("VY"), c("M1V"), -596.0, A.add, 1.0 / 32, A.mult)
+    act(c("CM4"), c("AC"), 0.5, 9.25)
+    act(c("VY"), c("M1V"), 1.0 / 32, -596.0 / 32)
     ts(c("cj"), c("LN"), -9.5, A.add)
     ts(c("CJ"), c("CJF"), c("cj"), A.add, 0.05, A.mult)
     cp(c("COFF"), c("CJ"))
@@ -419,11 +499,24 @@ def rank_program(g, core, T, topo):
     total(c("P1", 0, 320), [(lane("SS", 4), c("C16"))])
     act(c("ST", 352, 672), c("P1", 0, 320), -64.0)
     for j, x in enumerate((1, 2, 3, 0)):
-        act(c("JK", 20 * j, 20 * j + 20), c("DUM", 0, 20), 0.0, x + 7.5)
+        act(c("JK", j, 80, 4), c("DUM", 0, 20), 0.0, x + 7.5)
         act(c("JC", 20 * j, 20 * j + 20), c("DUM", 0, 20), 0.0, x - 0.5 if x else 7.5)
-    act(c("JC", 80, 100), c("DUM", 0, 20), 0.0, 7.5)
+    act(c("C72"), c("DUM", 0, 20), 0.0, -7200.0)
+    iota(c("X16"), [[1, 20]], 16, 0)
+    mms([(c("P1", 20 * b, 20 * b + 20), lane("SS", b), c("X16"), True, True) for b in range(16)])
+    act(c("LX", OFF, 352), c("P1", 0, 320), -1.0 / 1024, 8.0)
+    const(c("LX", 0, OFF), 8, "G")
     act(c("CN75"), c("DUM", 0, 20), 0.0, -7.5)
-    act(c("C75"), c("C16"), 7.5 / 16)
+    for lo in range(0, 2048, 512):
+        select(c("EX5", lo, lo + 512), c("EX", lo, lo + 512), [[0, 32], [1, 16]], A.is_equal, -5, 0)
+    act(c("W1"), c("SS"), 1.0 / 64)
+    ts(c("c75"), c("LN"), 5.0, A.is_equal, 7.5, A.mult)
+    ts(c("c6"), c("LN"), 6.0, A.is_equal)
+    ts(c("c6n"), c("LN"), 6.0, A.is_equal, -1.0, A.mult)
+    ts(c("co"), c("LN"), 7.0, A.is_equal, c("c6"), A.add)
+    act(c("D6"), ID, c("c6"))
+    act(c("S6"), c("IDW", 14, 142), c("c6n"))
+    act(c("WO"), c("W1"), c("co"))
 
     def entries(par, win, queues, keys):
         for j, q in enumerate(queues):
@@ -437,7 +530,7 @@ def rank_program(g, core, T, topo):
     PK = (c("P7", 320, 480), c("P3", 160, 320))
     for par in (0, 1):
         entries(par, "DW0", FIRST[par], PK[par])
-        scan(half("R1", par), c("FL"), PK[par], A.mult, A.max)
+        scan(half("R1", par), FL, PK[par], A.mult, A.max)
         cp(c("KB0", par, 20, 2), c("R1", 160 * par + 15, 160 * par + 160, 16))
     for par in (0, 1):
         act(half("AB", par), PK[par], 1.0, 262144.0, F.Abs)
@@ -452,7 +545,6 @@ def rank_program(g, core, T, topo):
     send(rank - 1, rank + 1, c("GH0"), c("GDI"), "ag0")
     ts(c("th64"), c("THI"), 64.0, A.mult)
     act(c("thr"), c("th64"), 1.0, 15.0)
-    act(c("Z0", OFF, 352, 2), c("ZL"))
     total(c("P6", 416, 436), blocks("WN", "VALN", 0, 20))
     act(c("BASE", 0, 20, 2), c("P6", 416, 436, 2), 1.0, 7680.0 - 524288.0)
     act(c("BASE", 1, 20, 2), c("P6", 417, 436, 2), 1.0, 7680.0)
@@ -464,28 +556,34 @@ def rank_program(g, core, T, topo):
         cur[0] = par
         ts(c("EI"), c("KB%d" % t), 511, A.bitwise_and)
         cp(c("EOU", 0, 20), c("EI"))
+        ts(c("EZU"), c("EI"), 0.5, A.mult, -0.5 * par, A.add)
+        ts(c("EH"), c("EI"), 2.0, A.mult, -47.0, A.add)
+        v17 = c("P6", 416, 496)
+        mms([(c("P6", 416 + 20 * j, 436 + 20 * j), ID, c("EH"), True, True) for j in range(4)])
+        act(c("MM", 0, 80), v17, 16.0, 9536.0)
+        act(c("X6"), c("P6", 416, 436), 0.0625, (251.0 - 8 * par) / 64)
+        tt(c("BB", 0, 80), v17, c("AC4"), A.mult)
+        if t in MASK:
+            fetch("S", c("LM"), c("LX"), c("EOU", 0, 20))
+            total(c("P6", 64, 84), lanes16("SS", "LM", 0, 20))
+            ts(c("XU"), c("P6", 64, 84), -1.0 / 64, A.mult, 112.0, A.add)
         tt(c("W3", 640, 960), at(c("GL%d" % par), c("EOU", 0, 20)), c("MAJ"), A.is_equal)
         tt(c("W3", 0, 320), c("W3", 640, 960), NBP, A.mult)
         ts(c("W3", 320, 640), c("W3", 640, 960), c("ck"), A.mult)
         total(c("P6", 0, 60), lanes16("SS", "W3", 0, 60))
         po, pk, pm = c("P6", 0, 20), c("P6", 20, 40), c("P6", 40, 60)
-        cp(c("EF"), c("EI"))
-        act(c("V613"), c("EF"), 0.5, 137.25)
-        act(c("V17"), c("EF"), 2.0, -47.0)
-        act(c("X6"), c("EF"), 0.125, (63.0 - 8 * par) / 64)
-        tt(c("BB", 60, 80), c("AC"), c("V17"), A.mult)
         ts(c("EOU", 20, 40), po, 1.0 / 64, A.mult, float(OFF), A.add)
-        tt(c("MM", 60, 80), pm, c("V613"), A.mult)
         tt(c("BB", 80, 100), po, c("A17"), A.mult)
         tt(c("pt"), pm, c("X6"), A.mult)
         tt(c("pu"), pk, c("pt"), A.add)
         act(c("MM", 80, 100), po, 0.5, 592.0)
-        act(c("MM", 40, 60), c("MM", 60, 80))
-        act(c("MM", 0, 40), c("MM", 40, 80))
-        act(c("BB", 40, 60), c("BB", 60, 80))
-        act(c("BB", 0, 40), c("BB", 40, 80))
+        act(c("NMB"), pm, -4096.0, 262144.0)
         tt(c("PX"), c("pu"), c("AC"), A.max)
         cp(c("PU"), c("PX"))
+        if t in OL:
+            mms([(c("P6", 64 + 20 * b, 84 + 20 * b), lane("W1", 6), c("W3", b, 320, 16), True, True) for b in range(16)])
+            act(c("OH"), c("P6", 64, 384))
+            return
         total(c("P6", 64, 384), [(c("B1"), c("W3", 0, 320))])
         act(c("OH"), c("P6", 64, 384))
         total(c("P6", 64, 384), [(c("OD"), c("W3", 0, 320)), (c("DPM"), c("OH"))])
@@ -503,37 +601,56 @@ def rank_program(g, core, T, topo):
         own = c(dw, OFF, 352)
         so = c("CL%d" % (t - 1)) if t else c("SO0")
         if t:
-            spread("P1", 0, c("CN%d" % (t - 1)), 20, c("C75"))
-            act(c(dw, 352, 672), c("P1", 0, 320))
-            spread("P0", OFF, so, 20, c("C75"))
-            if t == 1:
-                tt(own, c("P0", OFF, 352), c("ST", OFF, 352), A.min)
-            else:
-                act(own, c("P0", OFF, 352))
+            spread("P1", 0, c("CN%d" % (t - 1)), 20)
+            act(c(dw, 352, 672), c("P1", 0, 320), 1.0, 7.5)
+            col = lambda b: c("P0", OFF + 20 * b, OFF + 20 * b + 20)
+            early = ([(c("D6"), c("OH")), (c("S6"), c("OH"))] if t in OL else []) + ([(ID, c("ST", OFF, 352))] if t == 1 else [])
+            if early:
+                total(c("P0", OFF, 352), early, stop=False)
+            if t in OL:
+                mms([(col(b), lane("W1", 7), c("W3", b, 320, 16), False, False) for b in range(16)])
+            mms([(col(b), c("EX5", 128 * b, 128 * b + 128), so, not early, not early or b == 15) for b in range(16)])
+            act(own, c("P0", OFF, 352), 1.0, c("c75"), F.Identity)
         else:
             spread("P1", 0, c("GH0"), 20)
             act(c(dw, 352, 672), c("P1", 0, 320))
         for j in (1, 2, 3):
             act(c("SGN", 20 * j - 20, 20 * j), so, 1.0, j - 8.0, F.Sign)
-        mms([(c("P2", 64, 164), ID, c("JC"), True, False)] + [(c("P2", 64 + 20 * j, 84 + 20 * j), ID, so, False, False) for j in range(5)])
+        mms([(c("P2", 64, 144), ID, c("JC"), True, False)] + [(c("P2", 64 + 20 * j, 84 + 20 * j), ID, so, False, False) for j in range(4)])
         total(c("P2", 64, 124), [(c("ID8"), c("SGN"))], start=False)
         tp = lambda lo, hi: c("P4", 320 + lo, 320 + hi)
-        tt(tp(0, 100), c("P2", 64, 164), c("MM"), A.mult)
-        tt(tp(0, 100), tp(0, 100), c("BB"), A.add)
-        fetch("V", c("QD", 0, 320), c(dw, 0, 352), c("EOU", 0, 20))
+        tt(tp(0, 80), c("P2", 64, 144), c("MM", 0, 80), A.mult)
+        tt(tp(0, 80), tp(0, 80), c("BB", 0, 80), A.add)
+        if t in MASK:
+            tt(c("QD", 0, 320), at(so, c("XU")), c("LM"), A.max)
+            total(c("P2", 0, 20), [(ID, c("C72"))] + lanes16("SS", "QD", 0, 20))
+        else:
+            fetch("E", c("QD", 0, 320), c(dw, 0, 352), c("EOU", 0, 20))
+            total(c("P2", 0, 20), lanes16("WD", "QD", 0, 20))
+        for h in (0, 20):
+            tt(c("U", h, h + 20), c("P2", 0, 20), c("CM4") if t in MASK else c("CM40", 0, 20), A.mult)
+        for h in (0, 40):
+            tt(c("T6", h, h + 40), tp(h, h + 40), c("U", 0, 40), A.add)
+        ts(c("IX", 0, 80), c("T6", 0, 80), 4, A.arith_shift_right, 4095, A.bitwise_and)
+        cp(c("IXU", 0, 80), c("IX", 0, 80))
+        tt(c("B40", 0, 20), c("U", 0, 20), c("BB", 0, 20), A.add)
+        total(c("P1", 320, 340), [(ID, c("JC", 60, 80)), (ID, so)])
+        tt(tp(80, 100), c("P1", 320, 340), c("MM", 80, 100), A.mult)
         fetch("S", c("QD", 320, 640), c(dw), c("EOU", 20, 40))
-        total(c("P2", 0, 40), lanes16("WD", "QD", 0, 40))
-        tt(c("U", 20, 60), c("P2", 0, 40), c("CM40"), A.mult)
-        tt(c("U", 0, 20), c("P2", 0, 20), c("CM40", 0, 20), A.mult)
-        tt(c("T6", 40, 100), tp(40, 100), c("U"), A.add)
-        tt(c("T6", 0, 40), tp(0, 40), c("U", 0, 40), A.add)
-        ts(c("IX"), c("T6"), 4, A.arith_shift_right, 4095, A.bitwise_and)
-        cp(c("IXU"), c("IX"))
-        tt(c("B40"), c("U", 20, 60), c("BB", 60, 100), A.add)
+        total(c("P1", 352, 372), lanes16("WD", "QD", 320, 20))
+        tt(c("U", 40, 60), c("P1", 352, 372), c("CM40", 20, 40), A.mult)
+        tt(c("B40", 20, 40), c("U", 40, 60), c("BB", 80, 100), A.add)
+        tt(c("T6", 80, 100), tp(80, 100), c("B40", 20, 40), A.add)
+        ts(c("IX", 80, 100), c("T6", 80, 100), 4, A.arith_shift_right, 4095, A.bitwise_and)
+        cp(c("IXU", 80, 100), c("IX", 80, 100))
         if t:
             entries(par, dw, "E" * PIECE, None)
+        if t in OL:
+            total(c("P7", 0, 160), [(ID, c("K10"))] + blocks("WO", "SG", 2560 * par, 160, range(8)), stop=False)
+            total(c("P7", 0, 160), blocks("WO", "SG", 2560 * par, 160, range(8, 16)), start=False)
         PD, PY = c("P3", 0, 160), c("P0", 352, 512)
-        total(PY, [(EX(5), c(dw, OFF + par, 352, 2)), (ID, c("VY", par, 320, 2))])
+        total(PY, [(c("ID32"), c("VY", par, 320, 2))], stop=False)
+        total(PY, [(EX(5), c(dw, OFF + par, 352, 2))], start=False)
         tt(c("T1"), PY, half("APR", par), A.mult)
         for lo, hi in (((0, 80), (80, 160)) if t else ((0, 160),)):
             pd = c("P3", lo, hi)
@@ -547,13 +664,24 @@ def rank_program(g, core, T, topo):
         n = 160 // PIECE
         for lo in range(0, 160, n):
             fetch("E", c(gw, 320 + 16 * lo, 320 + 16 * (lo + n)), c("RW"), c("UI", lo, lo + n))
+        records = range(len(ops) - PIECE, len(ops))
         if t == 1:
             total(PK[1], [(ID, c("K512"))] + blocks("WM", "SG", 2560, 160))
-            scan(half("R1", 1), c("FL"), PK[1], A.mult, A.max)
-        fetch("S", c("ZE"), c(zw), c("EOU", 0, 20))
-        for j in range(4):
-            tt(c("X", 320 * j, 320 * j + 320), at(c("RW", 0, 4096), c("IXU", 20 * j, 20 * j + 20)), c("ZE"), A.max)
-            total(c("P2", 192 + j, 272, 4), [(ID, c("JK", 20 * j, 20 * j + 20)), (ID, so)] + lanes16("SS", "X", 320 * j, 20))
+            scan(half("R1", 1), FL, PK[1], A.mult, A.max)
+        fetch("S", c("ZE"), c(zw), c("EZU"))
+        key = lambda j: c("P2", 192 + j, 272, 4)
+        mms([(c("P2", 192, 272), ID, c("JK"), True, False)] + [(key(j), ID, so, False, False) for j in range(4)]
+            + [(key(j), ID, c("NMB"), False, False) for j in range(3)])
+        for j in range(AID):
+            total(key(j), lanes16("SS", "ZE", 0, 20), False, False)
+        for j in range(AID):
+            fetch("S", c("XR"), c("RW", 0, 4096), c("IXU", 20 * j, 20 * j + 20))
+            total(c("P0", 0, 320), [(c("IDN"), c("ZE")), (ID, c("XR"))])
+            act(c("X", 320 * j, 320 * j + 320), c("P0", 0, 320), 1.0, 0.0, F.Relu)
+        for j in range(3, -1, -1):
+            if j >= AID:
+                tt(c("X", 320 * j, 320 * j + 320), at(c("RW", 0, 4096), c("IXU", 20 * j, 20 * j + 20)), c("ZE"), A.max)
+            total(key(j), lanes16("SS", "X", 320 * j, 20), False, j == 0)
         tt(c("XO"), at(c("RW", 0, 4096), c("IXU", 80, 100)), c("ZE"), A.max)
         act(c("NXO"), c("XO"), -1.0)
         scan(c("KS"), c("DR4"), c("P2", 192, 272), A.max, A.min)
@@ -571,7 +699,7 @@ def rank_program(g, core, T, topo):
         P5 = c("P5", 0, 160)
         total(P5, [(ID, c("K15"))] + blocks("SS", "DX%d" % t, 320, 160))
         fetch("S", c("RN"), c("RW", 0, 4096), c("IXN", 0, 20))
-        scan(c("S1"), c("FL"), P5, A.mult, A.max)
+        scan(c("S1"), FL, P5, A.mult, A.max)
         tt(c("QE"), P5, c("S1"), A.is_equal)
         tt(c("NQ"), P5, c("S1"), A.not_equal)
         tt(c("QY"), c("P7", 0, 160), c("QE"), A.mult)
@@ -582,8 +710,10 @@ def rank_program(g, core, T, topo):
         tt(c("xj"), c("xi"), c("xb"), A.subtract)
         if not last:
             if t == 1:
+                first.extend(records[:AHEAD])
                 entries(0, "ST", "E" * PIECE, c("P6", 64, 224))
-                scan(half("R1", 0), c("FL"), c("P6", 64, 224), A.mult, A.max)
+                first.clear()
+                scan(half("R1", 0), FL, c("P6", 64, 224), A.mult, A.max)
                 cp(c("KB2", 0, 20, 2), c("R1", 15, 160, 16))
             cp(c("CU"), c("xi"))
             total(c("P6", 400, 410), [(c("ID32"), c("BASE", par, 20, 2))], stop=False)
@@ -611,12 +741,11 @@ def rank_program(g, core, T, topo):
         send(rank + 1, rank - 1, c("CL%d" % t), c("CN%d" % t), "ac%d" % t)
         for h in (0, 10):
             cp(at(c(gw), c("PU", h, h + 10)), c("RN", 16 * h, 16 * h + 160))
-        for lo in range(0, 2560, 640):
-            scan(c("GS", lo, lo + 640), c("FLB"), c(gw, 320 + lo, 960 + lo), A.mult, A.max)
-        total(PD, [(ID, c(zw, OFF + par, 352, 2)), (ID, c("GS", 15, 2560, 16))])
-        act(c("ZF"), PD, 0.4995, ROUND)
-        act(c("ZS2") if last else c("ZS%d" % t, OFF + 1 - par, 352, 2), c("ZF"), 1.0, -ROUND)
-        send(rank + 1 + t, rank - 1 - t, c("Z%d" % (t + 1)), c("ZS%d" % t), "az%d" % (t + 1))
+        for lo in range(0, 2560, 320):
+            scan(c("GS", lo, lo + 320), c("FLB"), c(gw, 320 + lo, 640 + lo), A.mult, A.max)
+        total(PD, [(c("IDH"), c("CNH")), (c("IDH"), c(zw, 16, 176)), (c("IDH"), c("GS", 15, 2560, 16))])
+        ts(c("ZS%d" % t), PD, ROUND, A.add, -ROUND, A.add)
+        send(rank + 1 + t, rank - 1 - t, c("Z%d" % (t + 1), 16, 176), c("ZS%d" % t), "az%d" % (t + 1))
         l1, val = lists(par), c("VALN", par, 320, 2)
         P1, PJ = c("P1", 320, 480), c("P7", 160, 320)
         spread("P1", 320, c("xj"), 10)
@@ -630,7 +759,7 @@ def rank_program(g, core, T, topo):
             cp(half("AOU", 0), l1)
             ts(val, l1, OFF - 0.5, A.is_ge, -131072.0, A.mult)
             act(half("APR", 0), l1, 32.0, -432.0)
-            total(c("P0", OFF, 352), statics + [(lane("SS", 5), c("C16")), (lane("SS", 0), c("VALN"))])
+            total(c("P0", OFF, 352), statics + [(lane("SS", 0), c("VALN"))])
             act(c("ST", OFF, 352), c("P0", OFF, 352), 1.0 / 1024)
         if not last:
             total(c("P5", 224, 234), [(c("ALL1", 0, 128), c("inj"))])
@@ -646,7 +775,7 @@ def rank_program(g, core, T, topo):
     dma("Y", T.yl[:, :], ap(c("YL")), "d_yl", [c("YL")], [], 1.8)
     act(c("YD"), c("CL%d" % (RO - 1)), 1.0, 7.5)
     dma("S", T.yd[:, :], ap(c("YD")), "d_yd", [c("YD")], [], 1.6)
-    dma("Y", T.yz[:, :], ap(c("Z3")), "d_yz", [c("Z3")], [], 1.6)
+    dma("Y", T.yz[:, :], ap(c("Z3", 16, 176)), "d_yz", [c("Z3", 16, 176)], [], 1.6)
 
     if not ORDER:
         ORDER.extend(schedule(ops))

@@ -24,28 +24,28 @@ def _put(name, width, kind):
     SCRATCH[tag] = ("sbuf", [128, _fill[tag]], _TYPES[kind])
 
 
-_CONST = (("b", (("SS", 144), ("IDW", 144), ("WM", 144), ("WP", 144), ("WD", 144), ("WN", 144), ("B1", 128), ("B1N", 128), ("OD", 128), ("DPM", 128), ("ID8", 128), ("IDN", 128), ("IDH", 128), ("CNH", 160),
-                 ("SHB", 128), ("BLC", 128), ("TRA", 128), ("TRI", 128), ("ALL1", 512), ("HI", 320), ("LO", 320), ("PI", 320), ("C16", 320), ("DUM", 32), ("D256", 32),
-                 ("R16", 320), ("VALN", 320), ("FL", 160), ("DR", 160), ("K512", 160), ("K15", 160), ("C185", 80), ("K10", 160), ("DR4", 80), ("ST", 672),
-                 ("W1", 144), ("WO", 144), ("D6", 128), ("S6", 128), ("EX5", 2048), ("CN75", 20), ("JK", 80), ("JC", 80), ("C72", 20), ("X16", 20), ("LX", 352))),
-          ("f", (("WI", 144), ("VY", 320), ("ID32", 128), ("PF", 1), ("LN", 1), ("LG", 1), ("LG20", 1), ("cu", 1), ("c3", 1), ("c4", 1), ("cd", 1), ("cn", 1), ("cs", 1),
-                 ("ck", 1), ("c75", 1), ("c6", 1), ("c6n", 1), ("co", 1), ("cj", 1), ("cp", 1), ("TI", 20), ("AC", 20), ("A17", 20), ("AC4", 80), ("CM4", 20), ("CM40", 40), ("MAJ", 320), ("M1V", 320), ("IOT", 208), ("CJF", 14), ("APR", 320),
-                 ("R1", 320), ("AB", 320), ("R2", 320), ("BASE", 20), ("th64", 10), ("ON10", 10), ("YL", 320))),
-          ("i", (("PI32", 1), ("LI", 1), ("LGI", 1), ("CJ", 14), ("KB0", 20), ("KB1", 20), ("KB2", 20))),
-          ("u", (("AOU", 320), ("COFF", 14))),
+_CONST = (("b", (("SS", 144), ("IDW", 144), ("WK", 144), ("WM", 144), ("WP", 144), ("WD", 144), ("WN", 144), ("B1", 128), ("B1N", 128), ("ID8", 128), ("IDN", 128), ("IDH", 128), ("CNH", 160),
+                 ("SHB", 128), ("BLC", 128), ("BLA", 128), ("BLB", 128), ("TRA", 128), ("TRI", 128), ("L8", 128), ("ALL1", 512), ("HI", 672), ("LO", 672), ("PI", 320), ("DUM", 32), ("D256", 32),
+                 ("R16", 320), ("VALN", 320), ("DR", 160), ("K512", 160), ("K8K", 160), ("K15", 160), ("KI", 160), ("KX", 160), ("C185", 80), ("DR5", 100), ("ST", 672), ("IOT", 208),
+                 ("WO0", 144), ("WO8", 144), ("WL", 144), ("ID4", 128), ("C155", 1), ("UP8", 128), ("C4K", 160), ("EX5", 2048), ("CN75", 20), ("JK", 100), ("JC", 80), ("C72", 20), ("X16", 20), ("LX", 352))),
+          ("f", (("WI", 144), ("VY", 320), ("ID32", 128), ("PF", 1), ("LN", 1), ("LG", 1), ("LG20", 1), ("cu", 1), ("c3", 1), ("c4", 1), ("cd", 1), ("cn", 1), ("cs", 1), ("c16", 1), ("wk", 1),
+                 ("ck", 1), ("c75", 1), ("co", 11), ("cj", 1), ("cp", 1), ("TI", 20), ("AC", 20), ("A17", 20), ("AC4", 80), ("AK", 40), ("AC16", 80), ("AC23", 80), ("CM4", 20), ("CM2", 20), ("CM40", 40),
+                 ("MAJ", 320), ("M1V", 320), ("M16", 320), ("CJF", 14), ("CJG", 14), ("CJH", 6), ("APR", 320), ("C0", 80), ("C1", 80), ("P44", 80), ("V4", 80),
+                 ("R1", 320), ("AB", 320), ("R2", 320), ("BASE", 20), ("th0", 10), ("th64", 10), ("ON10", 10), ("YL", 320))),
+          ("i", (("PI32", 1), ("LI", 1), ("LGI", 1), ("CJ", 14), ("KB0", 20), ("KB1", 20), ("KB2", 20), ("E16", 20), ("DV", 20))),
+          ("u", (("AOU", 320), ("COFF", 14), ("BC", 6))),
           ("h", (("NBH", 320),)))
 for _k, _l in _CONST:
     for _n, _w in _l:
         _put(_n, _w, _k)
 LOCAL = set()
-for _k, _l in (("f", (("X6", 20), ("MM", 100), ("BB", 100), ("pt", 20), ("pu", 20), ("PX", 20), ("U", 60), ("B40", 40), ("KS", 80), ("NQ", 160),
-                      ("PQ", 40), ("T1", 160), ("UE", 160), ("S1", 160), ("QE", 160), ("QY", 160), ("S2", 160), ("ZF", 160), ("P1C", 160), ("HF", 16), ("thr", 10),
-                      ("SGR", 20), ("xi", 10), ("w", 10), ("t20", 10), ("h", 10), ("prf", 10), ("jk", 10), ("CC", 2))),
-                ("i", (("EI", 20), ("T6", 100), ("IX", 100), ("KK", 20), ("PN", 20), ("IN", 40), ("IM", 40),
-                       ("UQ", 160), ("UF", 160), ("wi", 10), ("CCI", 1), ("CCJ", 1))),
-                ("b", (("SGN", 60), ("NMB", 20), ("LM", 320), ("XR", 320), ("QD", 640), ("ZE", 320), ("X", 1280), ("XO", 320), ("NXO", 320), ("XN", 320), ("RN", 320), ("OH", 320),
-                       ("OEB", 320), ("RH", 208), ("LH", 1280), ("JQ", 160), ("JB", 160), ("inj", 10), ("xb", 10), ("cs10", 10))),
-                ("h", (("W3", 960), ("EH", 20), ("xj", 10))),
+for _k, _l in (("f", (("X6", 20), ("MM", 80), ("BB", 80), ("MO", 20), ("BO", 20), ("pt", 20), ("pu", 20), ("PX", 20), ("U", 20), ("UO", 20), ("B2", 20), ("TP", 80), ("TO", 80), ("KS", 100),
+                      ("SN", 100), ("SR", 100), ("T1", 160), ("T2", 160), ("S1", 160), ("S2", 320), ("YY", 320), ("TH", 160), ("P1C", 160),
+                      ("SGR", 20), ("KM", 20), ("xk", 10), ("w", 10), ("h", 10), ("prf", 10), ("jk", 11), ("CC", 4))),
+                ("i", (("EI", 20), ("T6", 160), ("IX", 160), ("UQ", 160), ("UF", 160), ("CCI", 1), ("CCJ", 1))),
+                ("b", (("SGN", 60), ("PH", 80), ("NMB", 20), ("LM", 320), ("XR", 320), ("QD", 640), ("ZE", 320), ("X", 1280), ("XO", 320), ("NXO", 320), ("XN", 320), ("RN", 320), ("CD", 320),
+                       ("NQ", 100), ("SP", 100), ("SL", 320), ("HF", 16), ("CS", 16), ("NM", 208), ("RG", 208), ("RH", 208), ("LH", 1280), ("JQ", 160), ("JB", 160), ("inj", 10), ("xb", 10))),
+                ("h", (("W3", 960), ("EH", 20), ("xj", 10), ("H16", 160))),
                 ("u", (("EOU", 40), ("XU", 20), ("EZU", 20), ("PU", 20), ("IXU", 100), ("IXN", 40), ("UI", 160), ("CU", 10)))):
     for _n, _w in _l:
         LOCAL.add(_n)
@@ -55,8 +55,8 @@ for _i in (0, 1):
     _own("DW%d" % _i, 672, "b")
     _own("GL%d" % _i, 352, "f")
     _own("GW%d" % _i, 2880, "b")
-for _n, _w, _k in (("OW", 2880, "b"), ("GLI", 320, "i"), ("NBI", 320, "i"), ("V5", 320, "i"), ("VAI", 20, "i"), ("THI", 10, "i"), ("ZL", 160, "b"), ("RW", 4112, "b"), ("EX", 2048, "b"),
-                   ("FLB", 320, "b"), ("SG", 5120, "b"), ("GS", 2560, "b"), ("YD", 20, "f"), ("GDI", 20, "b"), ("SO0", 20, "b"), ("GH3", 20, "b"),
+for _n, _w, _k in (("GLI", 320, "i"), ("NBI", 320, "i"), ("V5", 320, "i"), ("VAI", 20, "i"), ("THI", 10, "i"), ("RW", 4112, "b"), ("EX", 2048, "b"),
+                   ("FLB", 320, "b"), ("SG", 5440, "b"), ("GS", 2560, "b"), ("YD", 20, "f"), ("GDI", 320, "b"), ("SO0", 20, "b"), ("GH3", 20, "b"),
                    ("Z3", 176, "b")):
     _own(_n, _w, _k)
 for _t in range(RO):
@@ -69,30 +69,43 @@ for _t in range(8):
     SCRATCH["P%d" % _t] = ("psum", [128, 512], "float32")
     VIEW["P%d" % _t] = ("P%d" % _t, 0, 512)
 SEMAPHORES = ["sV", "sS", "sT", "sG", "loc", "ac0", "ac1", "ac2", "ag0", "ag1", "ag2", "ag3", "az1", "az2", "az3",
-              "d_gl", "d_v5", "d_va", "d_th", "d_nb", "d_zl", "d_rec", "d_yl", "d_yd", "d_yz"] + ["d_z%d" % _t for _t in range(7)]
+              "d_gl", "d_v5", "d_va", "d_th", "d_nb", "d_zl", "d_rec", "d_yl", "d_yd", "d_yz", "d_c0"] + ["d_z%d" % _t for _t in range(5)]
 
-CYC, PE, GAP, HOP = 0.00088, 0.0005, 0.17, 1.7
+CLOCKS = ((0.00088, 1.56, 3.0, 0.0005, 0.17, 1.7), (0.00116, 1.95, 5.0, 0.0006, 0.12, 1.7), (0.00085, 1.2, 2.0, 0.0005, 0.24, 2.1))
 FIRST = ("VSVS", "SVSV")
 AID = 0
-AHEAD = 0
-OL = ()
-MASK = (1, 2)
+WIDE = ()
+MASK = ()
 PIECE = 4
 
 
 ORDER = []
-PASSES, LEAN, SHAKE = 600, 0.3, 3.0
-MOVES = 30000
+PASSES, LEAN, SHAKE = 300, 1.0, 3.0
+MOVES, EARLY, ANY, FAR, HEAT = 45000, 0.2, 0.5, 40, 0.04
 
 
 def schedule(ops):
     n = len(ops)
-    cost = [d["cost"] + (0.012 if d["q"] in "VSEGY" else 0.0) for d in ops]
-    before = [[(p, ops[p]["lat"] + (GAP if hard else 0.0)) for p, hard in d["preds"].items()] for d in ops]
-    after = [[] for _ in ops]
+    costs, befores, lats = [], [], []
+    for cy, ga, sc, pe, gap, hop in CLOCKS:
+        costs.append([d["cost"][0] + cy * (d["cost"][1] + ga * d["cost"][2] + sc * d["cost"][3]) + pe * d["cost"][4] + (0.012 if d["q"] in "VSEGY" else 0.0) for d in ops])
+        lats.append([hop if d["q"] == "A" else d["lat"] for d in ops])
+        befores.append([[(p, lats[-1][p] + gap if hard else 0.0) for p, hard in d["preds"].items()] for d in ops])
+    cost, seen = costs[0], {}
+    before = [list(x) for x in befores[0]]
+    for k, d in enumerate(ops):
+        for name in d["banks"]:
+            before[k] += [(p, CLOCKS[0][4]) for q, p in seen.setdefault(name, {}).items() if q != d["q"]]
+            seen[name][d["q"]] = k
+    after, later = [[] for _ in ops], [[] for _ in ops]
     for k in range(n):
         for p, lag in before[k]:
             after[p].append((k, lag))
+        for p, lag in befores[0][k]:
+            later[p].append((k, lag))
+    banks = [[8 * int(name[1]) for name in d["banks"]] for d in ops]
+    other = [[j for j, q in enumerate("VST") if q != d["q"]] for d in ops]
+    own = ["VST".find(d["q"]) for d in ops]
 
     def lay(turn, needs, tail):
         busy = {q: [] for q in "VSTGY"}
@@ -115,7 +128,7 @@ def schedule(ops):
             busy[place[k]].insert(j, (start[k], start[k] + cost[k]))
         return start, place
 
-    lat = [d["lat"] for d in ops]
+    lat = lats[0]
     way = [0.0] * n
     for k in range(n - 1, -1, -1):
         way[k] = cost[k] + max([lag + way[s] for s, lag in after[k]] + [lat[k]])
@@ -135,22 +148,41 @@ def schedule(ops):
             key[k] = max([key[k]] + [key[p] for p, _ in before[k]])
         back = lay(sorted(range(n), key=lambda k: (-key[k], -k)), after, lat)[0]
         turn = sorted(range(n), key=lambda k: (-back[k] - cost[k], k))
-    def clock(seq, place):
-        fin, why, last = [0.0] * n, [-1] * n, {}
-        for k in seq:
-            s, w = 0.0, -1
-            for p, lag in before[k]:
-                if fin[p] + lag > s:
-                    s, w = fin[p] + lag, p
-            q = place[k]
-            if q != "A":
-                j = last.get(q)
-                if j is not None and fin[j] > s:
-                    s, w = fin[j], j
-                last[q] = k
-            fin[k], why[k] = s + cost[k], w
-        e = max(range(n), key=lambda k: fin[k] + lat[k])
-        return fin[e] + lat[e], fin, why, e
+    ends = [k for k in range(n) if not later[k]]
+
+    def clock(seq, place, lo=0, old=None):
+        last, used, rest = {}, [-1] * 64, []
+        for k in seq[:lo]:
+            last[place[k]] = k
+            for b in banks[k]:
+                used[b + own[k]] = k
+        for k in seq[lo:]:
+            q, turns = place[k], []
+            for b in banks[k]:
+                turns += [used[b + j] for j in other[k] if used[b + j] >= 0]
+                used[b + own[k]] = k
+            rest.append((k, last.get(q, -1) if q != "A" else -1, turns))
+            last[q] = k
+        runs = []
+        for m in range(len(CLOCKS)):
+            fin, why = (list(old[1][m][1]), list(old[1][m][2])) if old else ([0.0] * n, [-1] * n)
+            bef, cst, gap = befores[m], costs[m], CLOCKS[m][4]
+            for k, j, turns in rest:
+                s, w = (fin[j], j) if j >= 0 else (0.0, -1)
+                for p, lag in bef[k]:
+                    if fin[p] + lag > s:
+                        s, w = fin[p] + lag, p
+                for p in turns:
+                    if fin[p] + gap > s:
+                        s, w = fin[p] + gap, p
+                fin[k], why[k] = s + cst[k], w
+            e = max(ends, key=lambda k: fin[k] + lats[m][k])
+            runs.append((fin[e] + lats[m][e] + EARLY * sum(fin) / n, fin, why, e))
+        if not weigh:
+            weigh.extend(runs[0][0] / r[0] / len(runs) for r in runs)
+        return sum(r[0] * x for r, x in zip(runs, weigh)), runs
+
+    weigh = []
 
     def closure(k, links, inside):
         found, stack = {k}, [k]
@@ -165,16 +197,22 @@ def schedule(ops):
     held = clock(seq, place)
     best = (held[0], seq, place)
     for it in range(MOVES):
-        pairs, k = [], held[3]
-        while held[2][k] >= 0:
-            if held[2][k] not in ops[k]["preds"]:
-                pairs.append((held[2][k], k))
-            k = held[2][k]
+        _, _, why, k = held[1][it % len(CLOCKS)]
+        pairs = []
+        while why[k] >= 0:
+            if why[k] not in ops[k]["preds"]:
+                pairs.append((why[k], k))
+            k = why[k]
         if not pairs:
-            break
+            continue
         a, b = pairs[int(shake.random() * len(pairs))]
+        if shake.random() < ANY:
+            b = int(shake.random() * n)
+            a = why[b]
+            if a < 0 or a in ops[b]["preds"]:
+                continue
         pos = {k: i for i, k in enumerate(seq)}
-        i, j, far, kind = pos[a], pos[b], int(shake.random() ** 3 * 30), shake.random()
+        i, j, far, kind = pos[a], pos[b], int(shake.random() ** 3 * FAR), shake.random()
         seq2, place2 = list(seq), place
         free = [x for x in (a, b) if ops[x]["q"] == "E"]
         if kind < 0.15 and free:
@@ -183,16 +221,16 @@ def schedule(ops):
             place2[x] = "V" if place[x] == "S" else "S"
         elif kind < 0.55:
             i = max(0, i - far)
-            go = closure(b, before, lambda x: pos[x] >= i)
+            go = closure(b, befores[0], lambda x: pos[x] >= i)
             seq2[i:j + 1] = [k for k in seq[i:j + 1] if k in go] + [k for k in seq[i:j + 1] if k not in go]
         else:
             j = min(n - 1, j + far)
-            go = closure(a, after, lambda x: pos[x] <= j)
+            go = closure(a, later, lambda x: pos[x] <= j)
             seq2[i:j + 1] = [k for k in seq[i:j + 1] if k not in go] + [k for k in seq[i:j + 1] if k in go]
-        new = clock(seq2, place2)
-        if new[0] <= held[0] + 0.08 * (1 - it / MOVES) * shake.exponential():
+        new = clock(seq2, place2, i, held)
+        if new[0] <= held[0] + HEAT * (1 - it / MOVES) * shake.exponential():
             held, place = new, place2
-            seq = sorted(seq2, key=lambda k: new[1][k] - cost[k]) if it % 20 == 0 else seq2
+            seq = sorted(seq2, key=lambda k: new[1][0][1][k] - cost[k]) if it % 20 == 0 else seq2
             if new[0] < best[0]:
                 best = (new[0], seq2, place2)
     return [(k, best[2][k]) for k in best[1]]
@@ -208,6 +246,7 @@ def rank_program(g, core, T, topo):
     ops = []
     first = []
     acc = {}
+    sums = {}
 
     def c(name, lo=0, hi=None, step=1):
         buf, o, w = VIEW[name + "#%d" % cur[0] if name in LOCAL else name]
@@ -234,16 +273,16 @@ def rank_program(g, core, T, topo):
             for (name, lo, hi, step) in views:
                 psum = SCRATCH[name][0] == "psum"
                 for a in acc.get(name, []):
-                    oq = ops[a[4]]["q"]
-                    if psum and oq != q:
-                        preds[a[4]] = True
-                        continue
-                    if psum and q == "T":
-                        preds[a[4]] = preds.get(a[4], False)
-                        continue
                     if not meet(a, lo, hi, step) or (a[3] == 0 and kind == 0):
                         continue
-                    preds[a[4]] = True
+                    preds[a[4]] = preds.get(a[4], False) or not (psum and q == "T" and ops[a[4]]["q"] == "T")
+        banks = sorted({v[0] for v in r + w if SCRATCH[v[0]][0] == "psum"})
+        if q == "T":
+            for name in banks:
+                for p in sums.setdefault(name, []):
+                    if kw.get("part") or ops[p].get("part"):
+                        preds.setdefault(p, False)
+                sums[name] = ([] if kw.get("part") else sums[name]) + [k]
         for (name, lo, hi, step) in w:
             acc[name] = [a for a in acc.get(name, []) if not (lo <= a[0] and a[1] <= hi and step == 1)]
             acc[name].append([lo, hi, step, 1, k])
@@ -251,7 +290,7 @@ def rank_program(g, core, T, topo):
             acc.setdefault(name, []).append([lo, hi, step, 0, k])
         for p in first:
             preds.setdefault(p, False)
-        d = {"q": q, "calls": calls, "preds": preds, "cost": cost, "lat": lat}
+        d = {"q": q, "calls": calls, "preds": preds, "cost": cost, "lat": lat, "outs": outs, "banks": banks}
         d.update(kw)
         ops.append(d)
         return k
@@ -277,15 +316,15 @@ def rank_program(g, core, T, topo):
     def cyc(out, ins, two=False):
         n = width(out)
         if out[0] == "@":
-            return 60 + 3.0 * n
+            return (0, 60, 0, n, 0)
         if any(v[0] == "@" for v in ins):
-            return 60 + 1.56 * n
+            return (0, 60, n, 0, 0)
         if two:
-            return n * (1 if any(SCRATCH[v[0]][0] == "psum" for v in ins) else 2)
-        return n * (0.5 if all(size2(v) for v in [out] + ins) else 1)
+            return (0, max(64, n * (1 if any(SCRATCH[v[0]][0] == "psum" for v in ins) else 2)), 0, 0, 0)
+        return (0, max(64, n * (0.5 if all(size2(v) for v in [out] + ins) else 1)), 0, 0, 0)
 
     def vec(call, out, ins, cy):
-        node("V", [call], [out], ins, max(64.0, cy) * CYC)
+        node("V", [call], [out], ins, cy)
 
     def tt(out, a, b, op):
         vec(lambda: g.vector.tensor_tensor(opnd(out), opnd(a), opnd(b), op), out, [a, b], cyc(out, [a, b], True))
@@ -304,32 +343,32 @@ def rank_program(g, core, T, topo):
 
     def act(out, a, scale=1.0, bias=0.0, func=F.Copy, total=None):
         n = width(out)
-        cost = (78 + 1.56 * n if a[0] == "@" else max(64, n)) * CYC
+        cost = (0, 78, n, 0, 0) if a[0] == "@" else (0, max(64, n), 0, 0, 0)
         if total is None:
             node("S", [lambda: g.scalar.activation(opnd(out), opnd(a), func, bias=opnd(bias), scale=opnd(scale))], [out], [a, bias, scale], cost)
         else:
-            node("S", [lambda: g.scalar.activation(opnd(out), opnd(a), func, bias=bias, scale=scale, accum_out=ap(total))], [out, total], [a], cost + 0.02)
+            node("S", [lambda: g.scalar.activation(opnd(out), opnd(a), func, bias=bias, scale=scale, accum_out=ap(total))], [out, total], [a], (0.14,) + cost[1:])
 
     def fetch(q, out, win, off):
         a = at(win, off)
         if q != "E":
             return (cp if q == "V" else act)(out, a)
         node("E", {"V": lambda: g.vector.tensor_copy(opnd(out), opnd(a)), "S": lambda: g.scalar.activation(opnd(out), opnd(a), F.Copy)},
-             [out], [a], (70 + 1.56 * width(out)) * CYC)
+             [out], [a], (0, 70, width(out), 0, 0))
 
     def scan(out, d0, d1, op0, op1):
         vec(lambda: g.vector.tensor_tensor_scan(ap(out), ap(d0), ap(d1), 0.0, op0, op1), out, [d0, d1], cyc(out, [d0, d1]))
 
     def mms(lst):
         calls = [lambda o=o, l=l, r=r, s=s, e=e: g.tensor.matmul(ap(o), ap(l), ap(r), s, e) for o, l, r, s, e in lst]
-        cost = sum(max(64, width(r)) * (1 if size2(r) else 4) for o, l, r, s, e in lst) * PE
-        node("T", calls, [x[0] for x in lst], [x[1] for x in lst] + [x[2] for x in lst], cost)
+        cost = sum(max(64, width(r)) * (1 if size2(r) else 4) for o, l, r, s, e in lst)
+        node("T", calls, [x[0] for x in lst], [x[1] for x in lst] + [x[2] for x in lst], (0, 0, 0, 0, cost), part=not (lst[0][3] and lst[-1][4]))
 
     def total(out, terms, start=True, stop=True):
         mms([(out, l, r, start and j == 0, stop and j == len(terms) - 1) for j, (l, r) in enumerate(terms)])
 
     def gps(call, out, ins, base):
-        node("G", [call], [out], ins, base + width(out) * 2 * CYC)
+        node("G", [call], [out], ins, (base, width(out) * 2, 0, 0, 0))
 
     def iota(v, pattern, base, cm):
         if SCRATCH[v[0]][2] != "int32":
@@ -343,20 +382,23 @@ def rank_program(g, core, T, topo):
         else:
             act(v, c("ALL1", 0, width(v)), float(x))
 
-    def select(out, a, pattern, op, base, cm):
-        gps(lambda: g.affine_select(ap(out), ap(a), pattern, op, 0.0, base, cm), out, [a], 0.2)
+    def select(out, a, pattern, op, base, cm, other=0.0):
+        gps(lambda: g.affine_select(ap(out), ap(a), pattern, op, other, base, cm), out, [a], 0.2)
 
     def dma(q, out_ap, in_ap, sem, reads, writes, lat):
-        node(q, [lambda: queue[q].dma_start(out_ap, in_ap)], writes, reads, 0.1, lat, sem=sem)
+        return node(q, [lambda: queue[q].dma_start(out_ap, in_ap)], writes, reads, (0.1, 0, 0, 0, 0), lat, sem=sem)
+
+    def rows(v, lo, hi, step=1):
+        return T[v[0]][lo:hi:step, v[1]:v[2]]
 
     def send(dst_rank, src_rank, out_v, in_v, sem):
         dst = cores[dst_rank % N]
         m = topo.mask(core, dst)
         rid, pid, _ = topo.addr(dst)
-        k = node("G", [lambda: g.remote_dma(ap(out_v), ap(in_v), T.sem[sem], T.sem.loc, pid, rid, m)], [], [in_v], 0.3,
+        k = node("G", [lambda: g.remote_dma(ap(out_v), ap(in_v), T.sem[sem], T.sem.loc, pid, rid, m)], [], [in_v], (0.3, 0, 0, 0, 0),
                  sent=len(topo.engines(core, dst)))
         n = len(topo.engines(cores[src_rank % N], core))
-        ops.append({"q": "A", "calls": [], "preds": {k: False}, "cost": 0.0, "lat": HOP, "sem": sem, "amount": n})
+        ops.append({"q": "A", "calls": [], "preds": {k: False}, "cost": (0, 0, 0, 0, 0), "lat": 0.0, "sem": sem, "amount": n, "banks": []})
         acc.setdefault(out_v[0], []).append([out_v[1], out_v[2], 1, 1, len(ops) - 1])
 
     def lane(w, b):
@@ -385,26 +427,31 @@ def rank_program(g, core, T, topo):
         return c("GL%d" % par, OFF + par, OFF + 320, 2)
 
     dma("Y", ap(c("GLI")), T.gl[:, :], "d_gl", [], [c("GLI")], 1.8)
-    fill(c("V5"), 0)
-    dma("S", T["V5"][5:128:16, :], T.val[:, :], "d_v5", [], [c("V5")], 1.6)
-    dma("S", ap(c("VAI")), T.val[:, :], "d_va", [], [c("VAI")], 1.6)
-    dma("Y", ap(c("NBI")), T.nb[:, :], "d_nb", [], [c("NBI")], 2.0)
-    dma("Y", ap(c("THI")), T.th[:, :], "d_th", [], [c("THI")], 1.8)
-    dma("Y", ap(c("Z0", 16, 176)), T.zl[:, :], "d_zl", [], [c("Z0", 16, 176)], 2.0)
+    first.append(0)
+    first.append(dma("S", rows(c("V5"), 0, 8), T.val[:, :], "d_v5", [], [c("V5")], 1.6))
+    first.append(dma("S", ap(c("VAI")), T.val[:, :], "d_va", [], [c("VAI")], 1.6))
+    first.append(dma("Y", ap(c("NBI")), T.nb[:, :], "d_nb", [], [c("NBI")], 2.0))
+    first.append(dma("Y", ap(c("THI")), T.th[:, :], "d_th", [], [c("THI")], 1.8))
+    first.append(dma("Y", ap(c("Z0", 16, 176)), T.zl[:, :], "d_zl", [], [c("Z0", 16, 176)], 2.0))
     dma("Y", ap(c("RW", 0, 4096)), T.rec[:, :], "d_rec", [], [c("RW", 0, 4096)], 6.0)
+    first.clear()
 
     iota(c("PI32"), [[0, 1]], 0, 1)
     iota(c("WI"), [[1, 144]], -15, 0)
-    iota(c("HI"), [[-16, 20], [0, 16]], -OFF, 0)
-    iota(c("LO"), [[0, 20], [-1, 16]], 0, 0)
+    iota(c("HI", 0, 352), [[-16, 22], [0, 16]], 0, 0)
+    iota(c("LO", 0, 352), [[0, 22], [-1, 16]], 0, 0)
+    iota(c("HI", 352, 672), [[64, 16], [0, 20]], 64, 0)
+    iota(c("LO", 352, 672), [[0, 16], [2, 20]], -19, 0)
     fill(c("ALL1"), 1.0)
     act(c("K512"), c("LO", 0, 160), 512.0, 7680.0)
+    act(c("K8K"), c("LO", 0, 160), 8192.0, 122880.0)
     iota(c("TI"), [[1, 20]], 0, 20)
     iota(c("MAJ"), [[1, 20], [20, 16]], OFF, 0)
     iota(c("M1V"), [[2, 320]], 613, 0)
     act(c("K15"), c("LO", 0, 160), 1.0, 15.0)
-    iota(c("IOT", 0, 200), [[0, 10], [1, 20]], 1, 0)
-    const(c("IOT", 200, 208), -1, "G")
+    act(c("KX"), c("HI", 0, 160), -32768.0)
+    iota(c("IOT", 0, 200), [[0, 10], [-2, 20]], 19, 0)
+    const(c("IOT", 200, 208), 99, "G")
     iota(c("CJF"), [[16, 14]], 0, 0)
     for b in range(0, 16, 4):
         select(c("EX", 128 * b, 128 * b + 512), c("ALL1"), [[-1, 4], [-16, 8], [0, 16]], A.is_equal, -b, 1)
@@ -412,24 +459,24 @@ def rank_program(g, core, T, topo):
         const(c("GL%d" % i, 0, OFF), -5)
     const(c("RW", 4096, 4112), 0, "G")
     zero = c("DX2", 320, 1600)
-    for lo in (320, 960):
-        iota(c("DX2", lo, lo + 640), [[0, 640]], 0, 0)
-    for j, (n, lo) in enumerate((("OW", 320), ("OW", 1600), ("DX0", 320), ("DX0", 1600), ("DX1", 320), ("DX1", 1600), ("DX2", 1600))):
-        dma("Y", ap(c(n, lo, lo + 1280)), ap(zero), "d_z%d" % j, [zero], [c(n, lo, lo + 1280)], 3.0 + j)
+    for lo in range(320, 1600, 320):
+        const(c("DX2", lo, lo + 320), 0.0)
+    for j, (n, lo) in enumerate((("DX0", 320), ("DX0", 1600), ("DX1", 320), ("DX1", 1600), ("DX2", 1600))):
+        dma("Y", ap(c(n, lo, lo + 1280)), ap(zero), "d_z%d" % j, [zero, c("RW", 0, 4096)], [c(n, lo, lo + 1280)], 3.0 + j)
     for t in range(RO):
         const(c("Z%d" % t, 0, 16), 0, "G")
-    const(c("OD"), 0, "G")
     const(c("CNH"), -0.5)
     const(c("ON10"), 1, "G")
-    const(c("C16"), 16, "G")
     const(c("FLB"), 1)
     const(c("FLB", 0, 320, 16), 0)
-    const(c("DR4"), 0)
-    const(c("DR4", 0, 80, 4), 1048576)
-    const(c("K10"), OFF, "G")
+    const(c("DR5"), 0)
+    const(c("DR5", 0, 100, 5), 1048576)
     for i in (1, 0):
         cur[0] = i
-        const(c("HF"), 0, "G")
+        for n in ("HF", "CS", "TH"):
+            const(c(n), 0, "G")
+        const(c("SL", 0, 320, 2), 1, "G")
+        const(c("SL", 0, 320, 32), 0, "G")
 
     ts(c("LI"), c("PI32"), 15, A.bitwise_and)
     ts(c("LGI"), c("PI32"), 112, A.bitwise_and)
@@ -445,22 +492,26 @@ def rank_program(g, core, T, topo):
     const(c("D256", 31, 32), 256.0)
     const(c("C185"), -18.5)
     ts(c("cu"), c("LN"), 4.5, A.is_le, 1.0 / 32, A.mult)
-    for n, col, lim in (("WM", "c3", 2.5), ("WP", "c4", 3.5)):
-        ts(c(col), c("LN"), lim, A.is_ge, 0.5, A.subtract)
-        ts(c(n), c("SS"), c(col), A.mult, c("cu"), A.mult)
+    ts(c("c3"), c("LN"), 2.5, A.is_ge, 0.5, A.subtract)
+    ts(c("WM"), c("SS"), c("c3"), A.mult, c("cu"), A.mult)
+    const(c("C4K"), -4096.0)
     ts(c("cd"), c("LN"), 5.0, A.is_equal, 0.25, A.mult)
     act(c("WD"), c("SS"), c("cd"))
+    ts(c("wk"), c("c3"), c("cu"), A.mult, 256.0, A.mult)
+    ts(c("wk"), c("wk"), c("cd"), A.add, 1.0 / 16, A.mult)
+    ts(c("WK"), c("SS"), c("wk"), A.mult)
+    ts(c("c16"), c("PF"), 16.0, A.mult, 5.0, A.add)
+    ts(c("L8"), c("WI", 15, 143), c("c16"), A.is_equal, 64.0, A.mult)
     ts(c("cn"), c("LN"), 15.0, A.is_equal, 1.0 / 32, A.mult)
     ts(c("cn"), c("cn"), 1.0 / 16384, A.max)
     act(c("WN"), c("SS"), c("cn"))
     select(c("TRA"), c("ALL1", 0, 128), [[16, 8], [0, 16]], A.is_ge, 15, -1)
     select(c("B1"), c("TRA"), [[-16, 8], [0, 16]], A.is_ge, 0, 1)
     select(c("TRI"), c("B1"), [[1, 128]], A.is_gt, 0, -1)
-    ts(c("BLC"), c("WI", 15, 143), c("LG"), A.subtract)
+    iota(c("BLA"), [[0, 8], [-64, 16]], -64, 0)
+    select(c("BLB"), c("BLA"), [[16, 8], [0, 16]], A.is_ge, 15, -1, 1.0)
+    select(c("BLC"), c("BLB"), [[-16, 8], [0, 16]], A.is_ge, 0, 1, 1.0)
     act(c("B1N"), c("B1"), -1024.0)
-    act(c("OD", 1, 128, 2), c("B1", 1, 128, 2))
-    act(c("DPM", 0, 128, 2), c("IDW", 15, 143, 2))
-    act(c("DPM", 1, 128, 2), c("IDW", 16, 143, 2), -1.0)
     act(c("ID8"), ID, -8.0)
     act(c("ID32"), ID)
     act(c("IDN"), ID, -1.0)
@@ -468,129 +519,148 @@ def rank_program(g, core, T, topo):
     ts(c("cs"), c("LN"), 15.0, A.not_equal, -1.0, A.mult)
     act(c("SHB"), c("IDW", 14, 142), c("cs"))
     ts(c("cp"), c("LN"), 0.5, A.is_ge, -131072.0, A.mult)
-    ts(c("ck"), c("LN"), 1.0, A.add, 1.0 / 64, A.mult)
-    act(c("DR"), FL, -262144.0, 262144.0)
+    ts(c("ck"), c("LN"), 1.0 / 64, A.mult)
+    act(c("WL"), c("SS"), c("ck"))
+    act(c("ID4"), ID, 4.0)
+    act(c("DR"), FL, -4194304.0, 4194304.0)
     ts(c("LG20"), c("LG"), -20.0, A.mult)
     ts(c("AC"), c("TI"), c("LG20"), A.add)
     act(c("A17"), c("AC"), 2.0 / 64, 17.0 / 64)
     for j in range(4):
         act(c("AC4", 20 * j, 20 * j + 20), c("AC"))
-    act(c("CM40", 0, 20), c("AC"), 2.0, 37.0)
+    for par in (0, 1):
+        act(c("AK", 20 * par, 20 * par + 20), c("AC"), 1.0, 8.0 * par - 252)
+    act(c("AC16"), c("AC4"), 1.0 / 16)
+    act(c("AC23"), c("AC4"), -23.5, -0.25)
+    act(c("CM40", 0, 20), c("AC"), 16.0, 296.0)
     act(c("CM40", 20, 40), c("AC"), 2.0, 613.0)
-    act(c("CM4"), c("AC"), 0.5, 9.25)
+    if MASK:
+        act(c("CM4"), c("AC"), 0.5, 9.25)
+    if len(MASK) < 2:
+        act(c("CM2"), c("AC"), 2.0, 37.0)
     act(c("VY"), c("M1V"), 1.0 / 32, -596.0 / 32)
     ts(c("cj"), c("LN"), -9.5, A.add)
     ts(c("CJ"), c("CJF"), c("cj"), A.add, 0.05, A.mult)
     cp(c("COFF"), c("CJ"))
+    ts(c("CJG"), c("CJ"), -20.0, A.mult, c("LN"), A.add)
+    tt(c("CJH"), c("CJG", 0, 6), c("CJF", 0, 6), A.add)
+    cp(c("BC"), c("CJH"))
+    four = lambda v: at(v, c("BC", 0, 5))
 
     ts(c("VALN"), c("GLI"), 0.0, A.is_ge, -131072.0, A.mult)
     for par in (0, 1):
         ts(half("AOU", par), c("GLI", par, 320, 2), float(OFF), A.add)
-    ts(c("R16"), c("V5"), 16.0, A.mult)
-    statics = [(lane("SS", 1), c("HI")), (lane("SS", 2), c("LO")), (lane("SS", 3), c("PI"))]
+    vec(lambda: g.vector.tensor_scalar(rows(c("R16"), 0, 8), rows(c("V5"), 0, 8), 16.0, None, A.mult), c("R16"), [c("V5")], cyc(c("R16"), [c("V5")]))
+    statics = [(lane("SS", 1), c("HI", OFF, 352)), (lane("SS", 2), c("LO", OFF, 352)), (lane("SS", 3), c("PI"))]
     total(c("P0", 0, OFF), [(lane("SS", 4), c("DUM")), (lane("SS", 5), c("D256"))])
+
+    def values(out, stop):
+        node("T", [lambda: g.tensor.matmul(ap(out), rows(c("L8"), 0, 8), rows(c("R16"), 0, 8), False, stop)], [out], [c("L8"), c("R16")], (0, 0, 0, 0, 320), part=True)
+
+    def sizes(par):
+        seventh = c("P0", OFF + par, 352, 2)
+        mms([(seventh, lane("SS", 7), c("VALN", par, 320, 2), False, False), (c("P0", OFF, 352), lane("SS", 0), c("VALN"), False, True)])
+
     total(c("P0", OFF, 352), statics, stop=False)
-    total(c("P0", OFF, 352), [(lane("SS", 0), c("VALN")), (lane("SS", 5), c("R16"))], start=False)
+    mms([(c("P0", OFF + 1, 352, 2), lane("SS", 7), c("C4K"), False, False)])
+    values(c("P0", OFF, 352), False)
+    sizes(1)
     act(c("DW0", 0, 352), c("P0", 0, 352), 1.0 / 1024)
     ts(c("GL0", OFF), c("GLI"), float(OFF), A.add)
     act(c("GL1", OFF), c("GL0", OFF))
     for n in ("DW1", "ST"):
         act(c(n, 0, OFF), c("DW0", 0, OFF))
-    total(c("P1", 0, 320), [(lane("SS", 4), c("C16"))])
-    act(c("ST", 352, 672), c("P1", 0, 320), -64.0)
     for j, x in enumerate((1, 2, 3, 0)):
-        act(c("JK", j, 80, 4), c("DUM", 0, 20), 0.0, x + 7.5)
+        act(c("JK", j, 100, 5), c("DUM", 0, 20), 0.0, float(x))
         act(c("JC", 20 * j, 20 * j + 20), c("DUM", 0, 20), 0.0, x - 0.5 if x else 7.5)
-    act(c("C72"), c("DUM", 0, 20), 0.0, -7200.0)
-    iota(c("X16"), [[1, 20]], 16, 0)
-    mms([(c("P1", 20 * b, 20 * b + 20), lane("SS", b), c("X16"), True, True) for b in range(16)])
-    act(c("LX", OFF, 352), c("P1", 0, 320), -1.0 / 1024, 8.0)
-    const(c("LX", 0, OFF), 8, "G")
+    act(c("JK", 4, 100, 5), c("DUM", 0, 20), -1.0)
+    if MASK:
+        act(c("C72"), c("DUM", 0, 20), 0.0, -7200.0)
+        iota(c("X16"), [[1, 20]], 16, 0)
+        mms([(c("P1", 20 * b, 20 * b + 20), lane("SS", b), c("X16"), True, True) for b in range(16)])
+        act(c("LX", OFF, 352), c("P1", 0, 320), -1.0 / 1024, 8.0)
+        const(c("LX", 0, OFF), 8, "G")
     act(c("CN75"), c("DUM", 0, 20), 0.0, -7.5)
     for lo in range(0, 2048, 512):
         select(c("EX5", lo, lo + 512), c("EX", lo, lo + 512), [[0, 32], [1, 16]], A.is_equal, -5, 0)
-    act(c("W1"), c("SS"), 1.0 / 64)
     ts(c("c75"), c("LN"), 5.0, A.is_equal, 7.5, A.mult)
-    ts(c("c6"), c("LN"), 6.0, A.is_equal)
-    ts(c("c6n"), c("LN"), 6.0, A.is_equal, -1.0, A.mult)
-    ts(c("co"), c("LN"), 7.0, A.is_equal, c("c6"), A.add)
-    act(c("D6"), ID, c("c6"))
-    act(c("S6"), c("IDW", 14, 142), c("c6n"))
-    act(c("WO"), c("W1"), c("co"))
+    for up in (0, 8):
+        col = lambda j: c("co", up + j, up + j + 1)
+        ts(col(0), c("LN"), up + 1.0, A.is_equal)
+        ts(col(1), c("LN"), up + 2.0, A.is_equal, col(0), A.add)
+        ts(col(2), c("LN"), up + 7.0, A.is_equal, col(1), A.add)
+        ts(c("WO%d" % up), c("SS"), col(2), A.mult, -1.0 / 64, A.mult)
+    act(c("UP8"), c("IDW", 7, 135), c("co", 2, 3))
 
-    def entries(par, win, queues, keys):
+    def entries(par, win, queues, keys, w="WM", slot="K512"):
         for j, q in enumerate(queues):
             n = 160 // len(queues)
-            lo = 160 * par + n * j
-            fetch(q, c("SG", 16 * lo, 16 * (lo + n)), c(win, 0, 352), c("AOU", lo, lo + n))
+            lo = 2880 * par + 16 * n * j
+            fetch(q, c("SG", lo, lo + 16 * n), c(win, 0, 352), c("AOU", 160 * par + n * j, 160 * par + n * j + n))
             if keys:
                 nb = 16 // len(queues)
-                total(keys, ([(ID, c("K512"))] if j == 0 else []) + blocks("WM", "SG", 2560 * par, 160, range(nb * j, nb * j + nb)), j == 0, j == len(queues) - 1)
+                total(keys, ([(ID, c(slot))] if j == 0 else []) + blocks(w, "SG", 2880 * par, 160, range(nb * j, nb * j + nb)), j == 0, j == len(queues) - 1)
 
     PK = (c("P7", 320, 480), c("P3", 160, 320))
     for par in (0, 1):
-        entries(par, "DW0", FIRST[par], PK[par])
+        entries(par, "DW0", FIRST[par], PK[par], "WK", "K8K")
         scan(half("R1", par), FL, PK[par], A.mult, A.max)
         cp(c("KB0", par, 20, 2), c("R1", 160 * par + 15, 160 * par + 160, 16))
     for par in (0, 1):
-        act(half("AB", par), PK[par], 1.0, 262144.0, F.Abs)
+        act(half("AB", par), PK[par], 1.0, 4194304.0, F.Abs)
         scan(half("R2", par), c("DR"), half("AB", par), A.max, A.min)
-        ts(c("KB1", par, 20, 2), c("R2", 160 * par + 15, 160 * par + 160, 16), -1.0, A.mult, 262144.0, A.add)
+        ts(c("KB1", par, 20, 2), c("R2", 160 * par + 15, 160 * par + 160, 16), -1.0 / 16, A.mult, 262143.53125, A.add)
 
     NBP = c("P4", 0, 320)
     cp(c("NBH"), c("NBI"))
     mms([(c("P4", b, 320, 16), ID, c("NBH", 20 * b, 20 * b + 20), True, True) for b in range(16)])
     ts(c("SO0"), c("VAI"), -7.5, A.add)
-    act(c("GDI"), c("SO0"), 1.0, 7.5)
-    send(rank - 1, rank + 1, c("GH0"), c("GDI"), "ag0")
-    ts(c("th64"), c("THI"), 64.0, A.mult)
-    act(c("thr"), c("th64"), 1.0, 15.0)
+    total(c("P1", 0, 320), [(lane("SS", 1), c("HI", 352, 672)), (lane("SS", 2), c("LO", 352, 672))], stop=False)
+    values(c("P1", 0, 320), True)
+    act(c("GDI"), c("P1", 0, 320), 1.0 / 1024)
+    send(rank - 1, rank + 1, c("DW0", 352, 672), c("GDI"), "ag0")
+    dma("Y", ap(c("ST", 352, 672)), ap(c("GDI")), "d_c0", [c("GDI")], [c("ST", 352, 672)], 2.0)
+    ts(c("th0"), c("THI"), 64.0, A.mult, 16.0 + 992.0, A.add)
+    tt(c("th64"), c("th0"), c("KX", 0, 160, 16), A.add)
+    act(c("TH", 0, 160, 16), c("th64"), 1.0, -992.0)
+    const(c("C155"), -15.5)
     total(c("P6", 416, 436), blocks("WN", "VALN", 0, 20))
-    act(c("BASE", 0, 20, 2), c("P6", 416, 436, 2), 1.0, 7680.0 - 524288.0)
-    act(c("BASE", 1, 20, 2), c("P6", 417, 436, 2), 1.0, 7680.0)
+    act(c("BASE"), c("P6", 416, 436), -1.0, 4096.0 - 7680.0)
     for par in (0, 1):
         act(half("APR", par), lists(par), 32.0, -432.0)
 
     def prep(t):
         par = t & 1
         cur[0] = par
-        ts(c("EI"), c("KB%d" % t), 511, A.bitwise_and)
+        if t:
+            ts(c("EI"), c("KB%d" % t), 511, A.bitwise_and)
+        else:
+            ts(c("EI"), c("KB0"), 4, A.arith_shift_right, 511, A.bitwise_and)
         cp(c("EOU", 0, 20), c("EI"))
         ts(c("EZU"), c("EI"), 0.5, A.mult, -0.5 * par, A.add)
         ts(c("EH"), c("EI"), 2.0, A.mult, -47.0, A.add)
-        v17 = c("P6", 416, 496)
-        mms([(c("P6", 416 + 20 * j, 436 + 20 * j), ID, c("EH"), True, True) for j in range(4)])
-        act(c("MM", 0, 80), v17, 16.0, 9536.0)
-        act(c("X6"), c("P6", 416, 436), 0.0625, (251.0 - 8 * par) / 64)
-        tt(c("BB", 0, 80), v17, c("AC4"), A.mult)
+        if t:
+            v17 = c("P6", 416, 496)
+            mms([(c("P6", 416 + 20 * j, 436 + 20 * j), ID, c("EH"), True, True) for j in range(4)])
+            act(c("MM"), v17, 16.0, 9536.0)
+            tt(c("BB"), v17, c("AC4"), A.mult)
         if t in MASK:
             fetch("S", c("LM"), c("LX"), c("EOU", 0, 20))
             total(c("P6", 64, 84), lanes16("SS", "LM", 0, 20))
             ts(c("XU"), c("P6", 64, 84), -1.0 / 64, A.mult, 112.0, A.add)
-        tt(c("W3", 640, 960), at(c("GL%d" % par), c("EOU", 0, 20)), c("MAJ"), A.is_equal)
-        tt(c("W3", 0, 320), c("W3", 640, 960), NBP, A.mult)
-        ts(c("W3", 320, 640), c("W3", 640, 960), c("ck"), A.mult)
-        total(c("P6", 0, 60), lanes16("SS", "W3", 0, 60))
-        po, pk, pm = c("P6", 0, 20), c("P6", 20, 40), c("P6", 40, 60)
+        tt(c("W3", 320, 640), at(c("GL%d" % par), c("EOU", 0, 20)), c("MAJ"), A.is_equal)
+        tt(c("W3", 0, 320), c("W3", 320, 640), NBP, A.mult)
+        total(c("P6", 0, 40), lanes16("SS", "W3", 0, 40))
+        po, pm, pk = c("P6", 0, 20), c("P6", 20, 40), c("P6", 40, 60)
         ts(c("EOU", 20, 40), po, 1.0 / 64, A.mult, float(OFF), A.add)
-        tt(c("BB", 80, 100), po, c("A17"), A.mult)
-        tt(c("pt"), pm, c("X6"), A.mult)
-        tt(c("pu"), pk, c("pt"), A.add)
-        act(c("MM", 80, 100), po, 0.5, 592.0)
+        tt(c("BO"), po, c("A17"), A.mult)
+        act(c("MO"), po, 0.5, 592.0)
         act(c("NMB"), pm, -4096.0, 262144.0)
-        tt(c("PX"), c("pu"), c("AC"), A.max)
-        cp(c("PU"), c("PX"))
-        if t in OL:
-            mms([(c("P6", 64 + 20 * b, 84 + 20 * b), lane("W1", 6), c("W3", b, 320, 16), True, True) for b in range(16)])
-            act(c("OH"), c("P6", 64, 384))
-            return
-        total(c("P6", 64, 384), [(c("B1"), c("W3", 0, 320))])
-        act(c("OH"), c("P6", 64, 384))
-        total(c("P6", 64, 384), [(c("OD"), c("W3", 0, 320)), (c("DPM"), c("OH"))])
-        act(c("OEB"), c("P6", 64, 384), 1.0 / 512)
-        for h in (0, 10):
-            cp(at(c("OW"), c("PU", h, h + 10)), c("OEB", 16 * h, 16 * h + 160))
-        total(c("P7", 0, 160), [(ID, c("K10"))] + blocks("SS", "OW", 320, 160))
+        total(pk, lanes16("WL", "W3", 320, 20) + [(c("ID4"), c("EH")), (c("IDN"), c("NMB"))])
+        tt(c("PX"), pk, c("AK", 20 * par, 20 * par + 20), A.max)
+        ts(c("PU"), c("PX"), 252.0 - 8 * par, A.add)
+        if t:
+            fetch("E", c("CD"), c("ST"), c("EOU", 20, 40))
 
     prep(0)
 
@@ -604,74 +674,94 @@ def rank_program(g, core, T, topo):
             spread("P1", 0, c("CN%d" % (t - 1)), 20)
             act(c(dw, 352, 672), c("P1", 0, 320), 1.0, 7.5)
             col = lambda b: c("P0", OFF + 20 * b, OFF + 20 * b + 20)
-            early = ([(c("D6"), c("OH")), (c("S6"), c("OH"))] if t in OL else []) + ([(ID, c("ST", OFF, 352))] if t == 1 else [])
-            if early:
-                total(c("P0", OFF, 352), early, stop=False)
-            if t in OL:
-                mms([(col(b), lane("W1", 7), c("W3", b, 320, 16), False, False) for b in range(16)])
-            mms([(col(b), c("EX5", 128 * b, 128 * b + 128), so, not early, not early or b == 15) for b in range(16)])
+            total(c("P0", OFF, 352), [(ID, c("ST", OFF, 352))], stop=False)
+            mms([(col(b), c("UP8"), c("CD", b, 320, 16), False, False) for b in range(16)])
+            mms([(col(b), c("EX5", 128 * b, 128 * b + 128), so, False, b == 15) for b in range(16)])
             act(own, c("P0", OFF, 352), 1.0, c("c75"), F.Identity)
-        else:
-            spread("P1", 0, c("GH0"), 20)
-            act(c(dw, 352, 672), c("P1", 0, 320))
         for j in (1, 2, 3):
             act(c("SGN", 20 * j - 20, 20 * j), so, 1.0, j - 8.0, F.Sign)
         mms([(c("P2", 64, 144), ID, c("JC"), True, False)] + [(c("P2", 64 + 20 * j, 84 + 20 * j), ID, so, False, False) for j in range(4)])
         total(c("P2", 64, 124), [(c("ID8"), c("SGN"))], start=False)
-        tp = lambda lo, hi: c("P4", 320 + lo, 320 + hi)
-        tt(tp(0, 80), c("P2", 64, 144), c("MM", 0, 80), A.mult)
-        tt(tp(0, 80), tp(0, 80), c("BB", 0, 80), A.add)
-        if t in MASK:
-            tt(c("QD", 0, 320), at(so, c("XU")), c("LM"), A.max)
-            total(c("P2", 0, 20), [(ID, c("C72"))] + lanes16("SS", "QD", 0, 20))
+        p4 = c("P2", 64, 144)
+        if t:
+            tt(c("P4", 320, 400), p4, c("MM"), A.mult)
+            act(c("PH"), p4)
+            tt(c("TP"), c("P4", 320, 400), c("BB"), A.add)
+            if t in MASK:
+                tt(c("QD", 0, 320), at(so, c("XU")), c("LM"), A.max)
+                total(c("P1", 320, 340), [(ID, c("C72"))], stop=False)
+                total(c("P1", 320, 340), lanes16("SS", "QD", 0, 20), start=False)
+                tt(c("U"), c("P1", 320, 340), c("CM4"), A.mult)
+            else:
+                fetch("E", c("QD", 0, 320), c(dw, 0, 352), c("EOU", 0, 20))
+                total(c("P1", 320, 340), lanes16("WD", "QD", 0, 20))
+                tt(c("U"), c("P1", 320, 340), c("CM2"), A.mult)
+            tt(c("T6", 0, 80), four(c("U")), c("TP"), A.add)
         else:
-            fetch("E", c("QD", 0, 320), c(dw, 0, 352), c("EOU", 0, 20))
-            total(c("P2", 0, 20), lanes16("WD", "QD", 0, 20))
-        for h in (0, 20):
-            tt(c("U", h, h + 20), c("P2", 0, 20), c("CM4") if t in MASK else c("CM40", 0, 20), A.mult)
-        for h in (0, 40):
-            tt(c("T6", h, h + 40), tp(h, h + 40), c("U", 0, 40), A.add)
-        ts(c("IX", 0, 80), c("T6", 0, 80), 4, A.arith_shift_right, 4095, A.bitwise_and)
+            tt(c("C1"), p4, c("AC16"), A.add)
+            act(c("P44"), p4, 4392.0)
+            act(c("PH"), p4)
+            tt(c("C0"), c("P44"), c("AC23"), A.add)
+            ts(c("DV"), c("KB0"), 15, A.bitwise_and)
+            ts(c("E16"), c("KB0"), 511 * 16, A.bitwise_and)
+            tt(c("U"), c("DV"), c("CM40", 0, 20), A.mult)
+            tt(c("V4"), four(c("E16")), c("C1"), A.mult)
+            tt(c("TP"), four(c("U")), c("C0"), A.add)
+            tt(c("T6", 0, 80), c("V4"), c("TP"), A.add)
+        ts(c("IX", 0, 80), c("T6", 0, 80), 4 if t else 3, A.arith_shift_right, 4095, A.bitwise_and)
         cp(c("IXU", 0, 80), c("IX", 0, 80))
-        tt(c("B40", 0, 20), c("U", 0, 20), c("BB", 0, 20), A.add)
-        total(c("P1", 320, 340), [(ID, c("JC", 60, 80)), (ID, so)])
-        tt(tp(80, 100), c("P1", 320, 340), c("MM", 80, 100), A.mult)
         fetch("S", c("QD", 320, 640), c(dw), c("EOU", 20, 40))
         total(c("P1", 352, 372), lanes16("WD", "QD", 320, 20))
-        tt(c("U", 40, 60), c("P1", 352, 372), c("CM40", 20, 40), A.mult)
-        tt(c("B40", 20, 40), c("U", 40, 60), c("BB", 80, 100), A.add)
-        tt(c("T6", 80, 100), tp(80, 100), c("B40", 20, 40), A.add)
-        ts(c("IX", 80, 100), c("T6", 80, 100), 4, A.arith_shift_right, 4095, A.bitwise_and)
-        cp(c("IXU", 80, 100), c("IX", 80, 100))
+        tt(c("TO"), four(c("MO")), c("PH"), A.mult)
+        tt(c("UO"), c("P1", 352, 372), c("CM40", 20, 40), A.mult)
+        tt(c("B2"), c("UO"), c("BO"), A.add)
+        tt(c("T6", 80, 160), four(c("B2")), c("TO"), A.add)
+        ts(c("IX", 80, 160), c("T6", 80, 160), 4, A.arith_shift_right, 4095, A.bitwise_and)
+        cp(c("IXU", 80, 100), c("IX", 140, 160))
+        ts(c("H16"), c("IX"), -2048.0, A.add)
+
+        def steps(bank, lo, src, at0):
+            blk = lambda j: c(src, at0 + 20 * j, at0 + 20 * j + 20)
+            lst = []
+            for j in range(5):
+                terms = ([(ID, blk(j - 1))] if j else []) + ([(c("IDN"), blk(j))] if j < 4 else [])
+                lst += [(c(bank, lo + j, lo + 100, 5), l, r, i == 0, i == len(terms) - 1) for i, (l, r) in enumerate(terms)]
+            mms(lst)
+            return c(bank, lo, lo + 100)
+
+        dn, dr, dp = steps("P5", 288, "H16", 80), steps("P5", 388, "H16", 0), steps("P4", 400, "PH", 0)
         if t:
             entries(par, dw, "E" * PIECE, None)
-        if t in OL:
-            total(c("P7", 0, 160), [(ID, c("K10"))] + blocks("WO", "SG", 2560 * par, 160, range(8)), stop=False)
-            total(c("P7", 0, 160), blocks("WO", "SG", 2560 * par, 160, range(8, 16)), start=False)
         PD, PY = c("P3", 0, 160), c("P0", 352, 512)
         total(PY, [(c("ID32"), c("VY", par, 320, 2))], stop=False)
         total(PY, [(EX(5), c(dw, OFF + par, 352, 2))], start=False)
         tt(c("T1"), PY, half("APR", par), A.mult)
+        act(c("T2"), c("T1"), 1.0, 11026.0)
         for lo, hi in (((0, 80), (80, 160)) if t else ((0, 160),)):
             pd = c("P3", lo, hi)
             for hf in range(lo, hi, 80):
-                total(c("P3", hf, 80 + hf), [(ID, c("C185"))] + lanes16("WD", "SG", 2560 * par + 16 * hf, 80))
+                total(c("P3", hf, 80 + hf), [(ID, c("C185"))] + lanes16("WD", "SG", 2880 * par + 16 * hf, 80))
             tt(pd, pd, c("M1V", par + 2 * lo, 2 * hi, 2), A.mult)
-            tt(c("UE", lo, hi), pd, c("T1", lo, hi), A.add)
-            ts(c("UQ", lo, hi), c("UE", lo, hi), 11018.5, A.add, 1.0 / 16, A.mult)
-            ts(c("UF", lo, hi), c("UQ", lo, hi), 4095 + 15 * 65536, A.bitwise_and)
+            tt(c("UQ", lo, hi), pd, c("T2", lo, hi), A.add)
+            ts(c("UF", lo, hi), c("UQ", lo, hi), 4, A.arith_shift_right, 4095 + 15 * 65536, A.bitwise_and)
             ts(c("UI", lo, hi), c("UF", lo, hi), 4096.0, A.min)
         n = 160 // PIECE
         for lo in range(0, 160, n):
             fetch("E", c(gw, 320 + 16 * lo, 320 + 16 * (lo + n)), c("RW"), c("UI", lo, lo + n))
-        records = range(len(ops) - PIECE, len(ops))
         if t == 1:
-            total(PK[1], [(ID, c("K512"))] + blocks("WM", "SG", 2560, 160))
+            total(PK[1], [(ID, c("K512"))] + blocks("WM", "SG", 2880, 160))
             scan(half("R1", 1), FL, PK[1], A.mult, A.max)
+        if t == 0:
+            for h in (0, 10):
+                cp(at(c("SG", 2560, 5440), c("PU", h, h + 10)), c("QD", 320 + 16 * h, 480 + 16 * h))
+        for h in (0, 8):
+            total(c("P7", 0, 160), blocks("WO8" if t else "WO0", "SG", 2880 * par if t else 2880, 160, range(h, h + 8)), h == 0, h == 8)
+        act(c("YY", 0, 320, 2), c("P7", 0, 160), -1.0)
+        act(c("YY", 1, 320, 2), c("P7", 0, 160))
         fetch("S", c("ZE"), c(zw), c("EZU"))
-        key = lambda j: c("P2", 192 + j, 272, 4)
-        mms([(c("P2", 192, 272), ID, c("JK"), True, False)] + [(key(j), ID, so, False, False) for j in range(4)]
-            + [(key(j), ID, c("NMB"), False, False) for j in range(3)])
+        keys = c("P2", 192, 292)
+        key = lambda j: c("P2", 192 + j, 292, 5)
+        mms([(keys, ID, c("JK"), True, False)] + [(key(j), ID, c("NMB"), False, False) for j in range(3)])
         for j in range(AID):
             total(key(j), lanes16("SS", "ZE", 0, 20), False, False)
         for j in range(AID):
@@ -684,56 +774,52 @@ def rank_program(g, core, T, topo):
             total(key(j), lanes16("SS", "X", 320 * j, 20), False, j == 0)
         tt(c("XO"), at(c("RW", 0, 4096), c("IXU", 80, 100)), c("ZE"), A.max)
         act(c("NXO"), c("XO"), -1.0)
-        scan(c("KS"), c("DR4"), c("P2", 192, 272), A.max, A.min)
-        cp(c("KK"), c("KS", 3, 80, 4))
-        ts(c("PN"), c("KK"), 15, A.bitwise_and)
-        tt(c("PQ", 20, 40), c("PN"), c("MM", 80, 100), A.mult)
-        tt(c("PQ", 0, 20), c("PN"), c("MM", 60, 80), A.mult)
-        tt(c("IN"), c("PQ"), c("B40"), A.add)
-        ts(c("IM"), c("IN"), 4, A.arith_shift_right, 4095, A.bitwise_and)
-        cp(c("IXN"), c("IM"))
-        cp(c("GD%d" % t), c("PN"))
+        scan(c("KS"), c("DR5"), keys, A.max, A.min)
+        tt(c("NQ"), keys, c("KS"), A.not_equal)
+        scan(c("SN"), dn, c("NQ"), A.add, A.mult)
+        ts(c("IXN", 20, 40), c("SN", 4, 100, 5), 2048.0, A.add)
+        scan(c("SR"), dr, c("NQ"), A.add, A.mult)
+        ts(c("IXN", 0, 20), c("SR", 4, 100, 5), 2048.0, A.add)
+        scan(c("SP"), dp, c("NQ"), A.add, A.mult)
+        act(c("GD%d" % t), c("SP", 4, 100, 5))
         send(rank - 1, rank + 1, c("GH%d" % (t + 1)), c("GD%d" % t), "ag%d" % (t + 1))
         tt(c("XN"), at(c("RW", 0, 4096), c("IXN", 20, 40)), c("ZE"), A.max)
         tt(at(c("DX%d" % t), c("PU")), c("XN"), c("NXO"), A.add)
         P5 = c("P5", 0, 160)
-        total(P5, [(ID, c("K15"))] + blocks("SS", "DX%d" % t, 320, 160))
+        total(P5, [(ID, c("K15")), (ID, c("KX"))], stop=False)
+        total(P5, blocks("SS", "DX%d" % t, 320, 160), start=False)
         fetch("S", c("RN"), c("RW", 0, 4096), c("IXN", 0, 20))
-        scan(c("S1"), FL, P5, A.mult, A.max)
-        tt(c("QE"), P5, c("S1"), A.is_equal)
-        tt(c("NQ"), P5, c("S1"), A.not_equal)
-        tt(c("QY"), c("P7", 0, 160), c("QE"), A.mult)
-        scan(c("S2"), c("NQ"), c("QY"), A.mult, A.add)
-        tt(c("inj"), c("S1", 15, 160, 16), c("thr"), A.is_gt)
-        tt(c("xi"), c("S2", 15, 160, 16), c("inj"), A.mult)
-        ts(c("xb"), c("xi"), 351.5, A.is_ge, 1024.0, A.mult)
-        tt(c("xj"), c("xi"), c("xb"), A.subtract)
+        scan(c("S1"), c("TH"), P5, A.max, A.max)
+        tt(c("SL", 1, 320, 2), P5, c("S1"), A.not_equal)
+        scan(c("S2"), c("SL"), c("YY"), A.mult, A.add)
+        y = c("S2", 31, 320, 32)
+        ts(c("xb"), y, 0.0, A.is_lt, 1.0 / 64, A.mult)
+        ts(c("w"), y, 64 * ROUND, A.add, -64 * ROUND, A.add)
+        ts(c("xk"), y, 4096 * ROUND, A.add, -4096 * ROUND, A.add)
+        tt(c("xj"), y, c("xk"), A.subtract)
         if not last:
             if t == 1:
-                first.extend(records[:AHEAD])
                 entries(0, "ST", "E" * PIECE, c("P6", 64, 224))
-                first.clear()
                 scan(half("R1", 0), FL, c("P6", 64, 224), A.mult, A.max)
                 cp(c("KB2", 0, 20, 2), c("R1", 15, 160, 16))
-            cp(c("CU"), c("xi"))
-            total(c("P6", 400, 410), [(c("ID32"), c("BASE", par, 20, 2))], stop=False)
-            fetch("S", c("JB"), c("ST" if par else dw), c("CU"))
-            total(c("P6", 400, 410), lanes16("WM" if par else "WP", "JB", 0, 10), start=False)
-            if t == 0:
-                tt(c("KB1", 0, 20, 2), c("P6", 400, 410), c("KB1", 0, 20, 2), A.max)
-            else:
-                tt(c("KB2", 1, 20, 2), c("P6", 400, 410), c("R1", 175, 320, 16), A.max)
-        scan(c("cs10"), c("ON10"), c("xb"), A.mult, A.add)
-        total(c("P5", 192, 193), [(c("TRI"), c("cs10", 9, 10))])
-        ts(c("wi"), c("xi"), -361.5, A.add, 0.05, A.mult)
-        ts(c("w"), c("wi"), -0.5, A.max)
-        act(c("t20"), c("w"), -20.0, -351.0)
-        tt(c("h"), c("xi"), c("t20"), A.add)
+            ts(c("inj"), y, 0.0, A.not_equal)
+            tt(c("KM", 0, 10), c("R1", 175, 320, 16) if t else c("KB1", 0, 20, 2), c("BASE", par, 20, 2), A.add)
+            ts(c("KM", 10, 20), c("KM", 0, 10), 4096.0, A.max)
+            tt(c("KB%d" % (t + 1), par, 20, 2), c("KM", 10, 20), y, A.max)
+        scan(c("CS", 0, 10), c("ON10"), c("xb"), A.mult, A.add)
+        total(c("P5", 192, 193), [(c("TRI"), c("CS", 9, 10))])
         for x in range(10):
             ts(c("LH", 128 * x, 128 * x + 128), c("BLC"), c("w", x, x + 1), A.is_equal)
-        ts(c("prf"), c("cs10"), c("P5", 192, 193), A.add, 1024.0 * CAP, A.is_le)
-        tt(c("HF", 0, 10), c("prf"), c("h"), A.mult)
-        tt(c("RH"), at(c("HF"), c("COFF", 0, 13)), c("IOT"), A.is_equal)
+        if t in WIDE:
+            tt(c("HF", 0, 10), y, c("w"), A.subtract)
+            tt(c("NM"), at(c("HF"), c("COFF", 0, 13)), c("IOT"), A.not_equal)
+            tt(c("RG"), at(c("CS"), c("COFF", 0, 13)), c("NM"), A.add)
+            ts(c("RH", 0, 200), c("RG", 0, 200), c("P5", 192, 193), A.add, CAP / 64, A.is_le)
+        else:
+            tt(c("h"), y, c("w"), A.subtract)
+            ts(c("prf"), c("CS", 0, 10), c("P5", 192, 193), A.add, CAP / 64, A.is_gt)
+            tt(c("HF", 0, 10), c("prf"), c("h"), A.add)
+            tt(c("RH"), at(c("HF"), c("COFF", 0, 13)), c("IOT"), A.is_equal)
         new = c("P5", 256, 276)
         total(new, [(ID, c("CN75")), (ID, c("GH%d" % (t + 1)))] + [(c("LH", 128 * x, 128 * x + 128), c("RH", 20 * x, 20 * x + 20)) for x in range(10)])
         ts(c("SGR"), new, 16 * ROUND, A.add, -16 * ROUND, A.add)
@@ -759,17 +845,19 @@ def rank_program(g, core, T, topo):
             cp(half("AOU", 0), l1)
             ts(val, l1, OFF - 0.5, A.is_ge, -131072.0, A.mult)
             act(half("APR", 0), l1, 32.0, -432.0)
-            total(c("P0", OFF, 352), statics + [(lane("SS", 0), c("VALN"))])
+            total(c("P0", OFF, 352), statics, stop=False)
+            mms([(c("P0", OFF, 352, 2), lane("SS", 7), c("C4K"), False, False)])
+            sizes(0)
             act(c("ST", OFF, 352), c("P0", OFF, 352), 1.0 / 1024)
         if not last:
-            total(c("P5", 224, 234), [(c("ALL1", 0, 128), c("inj"))])
-            act(c("jk"), c("P5", 224, 234), total=c("CC", 0, 1))
-            cp(c("CCI"), c("CC", 0, 1))
-            ts(c("CCJ"), c("CCI"), 31, A.bitwise_and)
-            ts(c("CC", 1, 2), c("CCJ"), 64.0, A.mult, 15.0, A.add)
-            inc = c("CC", 1, 2)
+            mms([(c("P5", 234, 235), ID, c("C155"), True, True), (c("P5", 224, 234), c("ALL1", 0, 128), c("inj"), True, True)])
+            act(c("jk"), c("P5", 224, 235), total=c("CC", 0, 1))
+            act(c("CC", 1, 2), c("CC", 0, 1), 1.0, 32 * ROUND)
+            act(c("CC", 2, 3), c("CC", 1, 2), -64.0, 2048 * ROUND)
+            act(c("CC", 3, 4), c("CC", 0, 1), 64.0, c("CC", 2, 3), F.Identity)
+            inc = c("CC", 3, 4)
             cur[0] = 1 - par
-            act(c("thr"), c("th64"), 1.0, inc, F.Identity)
+            act(c("TH", 0, 160, 16), c("th64"), 1.0, inc, F.Identity)
             prep(t + 1)
 
     dma("Y", T.yl[:, :], ap(c("YL")), "d_yl", [c("YL")], [], 1.8)
@@ -785,8 +873,12 @@ def rank_program(g, core, T, topo):
     clock = {q: {} for q in "VSTGY"}
     token = [None] * len(ops)
     sent = 0
+    seen = {}
     for k, q in order:
         d = ops[k]
+        for name in d["banks"]:
+            d["preds"].update({p: True for q2, p in seen.setdefault(name, {}).items() if q2 != q})
+            seen[name][q] = k
         if d["q"] == "E":
             d["calls"] = [d["calls"][q]]
         if q == "A":

import numpy as np
from concourse.mybir import AluOpType as A, AxisListType, ActivationFunctionType as F

N, RO, CAP = 8, 3, 28
OFF = 32
ROUND = 12582912.0

SCRATCH = {}
VIEW = {}
_TYPES = {"f": "float32", "i": "int32", "b": "bfloat16", "u": "uint16", "h": "float16"}
_fill = {}


def _own(name, width, kind):
    SCRATCH[name] = ("sbuf", [128, width], _TYPES[kind])
    VIEW[name] = (name, 0, width)


def _put(name, width, kind):
    tag = "ar" + kind
    o = _fill.get(tag, 0)
    VIEW[name] = (tag, o, width)
    _fill[tag] = o + (width + 15) // 16 * 16
    SCRATCH[tag] = ("sbuf", [128, _fill[tag]], _TYPES[kind])


_CONST = (("b", (("SS", 144), ("IDW", 144), ("WK", 144), ("WM", 144), ("WP", 144), ("WD", 144), ("WN", 144), ("B1", 128), ("B1N", 128), ("ID8", 128), ("IDN", 128), ("IDH", 128), ("CNH", 160),
                 ("SHB", 128), ("BLC", 128), ("BLA", 128), ("BLB", 128), ("TRA", 128), ("TRI", 128), ("L8", 128), ("ALL1", 512), ("HI", 672), ("LO", 672), ("PI", 320), ("DUM", 32), ("D256", 32),
                 ("R16", 320), ("VALN", 320), ("DR", 160), ("K512", 160), ("K8K", 160), ("K15", 160), ("KI", 160), ("KX", 160), ("C185", 80), ("DR5", 100), ("ST", 672), ("IOT", 208),
                 ("WO0", 144), ("WO8", 144), ("WL", 144), ("ID4", 128), ("C155", 1), ("UP8", 128), ("C4K", 160), ("EX5", 2048), ("CN75", 20), ("JK", 100), ("JC", 80), ("C72", 20), ("X16", 20), ("LX", 352))),
          ("f", (("WI", 144), ("VY", 320), ("ID32", 128), ("PF", 1), ("LN", 1), ("LG", 1), ("LG20", 1), ("cu", 1), ("c3", 1), ("c4", 1), ("cd", 1), ("cn", 1), ("cs", 1), ("c16", 1), ("wk", 1),
                 ("ck", 1), ("c75", 1), ("co", 11), ("cj", 1), ("cp", 1), ("TI", 20), ("AC", 20), ("A17", 20), ("AC4", 80), ("AK", 40), ("AC16", 80), ("AC23", 80), ("CM4", 20), ("CM2", 20), ("CM40", 40),
                 ("MAJ", 320), ("M1V", 320), ("M16", 320), ("CJF", 14), ("CJG", 14), ("CJH", 6), ("APR", 320), ("C0", 80), ("C1", 80), ("P44", 80), ("V4", 80),
                 ("R1", 320), ("AB", 320), ("R2", 320), ("BASE", 20), ("th0", 10), ("th64", 10), ("ON10", 10), ("YL", 320))),
          ("i", (("PI32", 1), ("LI", 1), ("LGI", 1), ("CJ", 14), ("KB0", 20), ("KB1", 20), ("KB2", 20), ("E16", 20), ("DV", 20))),
          ("u", (("AOU", 320), ("COFF", 14), ("BC", 6))),
          ("h", (("NBH", 320),)))
for _k, _l in _CONST:
    for _n, _w in _l:
        _put(_n, _w, _k)
LOCAL = set()
for _k, _l in (("f", (("X6", 20), ("MM", 80), ("BB", 80), ("MO", 20), ("BO", 20), ("pt", 20), ("pu", 20), ("PX", 20), ("U", 20), ("UO", 20), ("B2", 20), ("TP", 80), ("TO", 80), ("KS", 100),
                      ("SN", 100), ("SR", 100), ("T1", 160), ("T2", 160), ("S1", 160), ("S2", 320), ("YY", 320), ("TH", 160), ("P1C", 160),
                      ("SGR", 20), ("KM", 20), ("xk", 10), ("w", 10), ("h", 10), ("prf", 10), ("jk", 11), ("CC", 4))),
                ("i", (("EI", 20), ("T6", 160), ("IX", 160), ("UQ", 160), ("UF", 160), ("CCI", 1), ("CCJ", 1))),
                ("b", (("SGN", 60), ("PH", 80), ("NMB", 20), ("LM", 320), ("XR", 320), ("QD", 640), ("ZE", 320), ("X", 1280), ("XO", 320), ("NXO", 320), ("XN", 320), ("RN", 320), ("CD", 320),
                       ("NQ", 100), ("SP", 100), ("SL", 320), ("HF", 16), ("CS", 16), ("NM", 208), ("RG", 208), ("RH", 208), ("LH", 1280), ("JQ", 160), ("JB", 160), ("inj", 10), ("xb", 10))),
                ("h", (("W3", 960), ("EH", 20), ("xj", 10), ("H16", 160))),
                ("u", (("EOU", 40), ("XU", 20), ("EZU", 20), ("PU", 20), ("IXU", 100), ("IXN", 40), ("UI", 160), ("CU", 10)))):
    for _n, _w in _l:
        LOCAL.add(_n)
        for _i in (0, 1):
            _put(_n + "#%d" % _i, _w, _k)
for _i in (0, 1):
    _own("DW%d" % _i, 672, "b")
    _own("GL%d" % _i, 352, "f")
    _own("GW%d" % _i, 2880, "b")
for _n, _w, _k in (("GLI", 320, "i"), ("NBI", 320, "i"), ("V5", 320, "i"), ("VAI", 20, "i"), ("THI", 10, "i"), ("RW", 4112, "b"), ("EX", 2048, "b"),
                   ("FLB", 320, "b"), ("SG", 5440, "b"), ("GS", 2560, "b"), ("YD", 20, "f"), ("GDI", 320, "b"), ("SO0", 20, "b"), ("GH3", 20, "b"),
                   ("Z3", 176, "b")):
    _own(_n, _w, _k)
for _t in range(RO):
    _own("DX%d" % _t, 2880, "b")
    _own("Z%d" % _t, 176, "b")
    _own("ZS%d" % _t, 160, "b")
    for _n in ("CN", "CL", "GD", "GH"):
        _own("%s%d" % (_n, _t), 20, "b")
for _t in range(8):
    SCRATCH["P%d" % _t] = ("psum", [128, 512], "float32")
    VIEW["P%d" % _t] = ("P%d" % _t, 0, 512)
SEMAPHORES = ["sV", "sS", "sT", "sG", "loc", "ac0", "ac1", "ac2", "ag0", "ag1", "ag2", "ag3", "az1", "az2", "az3",
              "d_gl", "d_v5", "d_va", "d_th", "d_nb", "d_zl", "d_rec", "d_yl", "d_yd", "d_yz", "d_c0"] + ["d_z%d" % _t for _t in range(5)]

CLOCKS = ((0.00088, 1.56, 3.0, 0.0005, 0.17, 1.7), (0.00116, 1.95, 5.0, 0.0006, 0.12, 1.7), (0.00085, 1.2, 2.0, 0.0005, 0.24, 2.1))
FIRST = ("VSVS", "SVSV")
AID = 0
WIDE = ()
MASK = ()
PIECE = 4


ORDER = []
PASSES, LEAN, SHAKE = 300, 1.0, 3.0
MOVES, EARLY, ANY, FAR, HEAT = 45000, 0.2, 0.5, 40, 0.04


def schedule(ops):
    n = len(ops)
    costs, befores, lats = [], [], []
    for cy, ga, sc, pe, gap, hop in CLOCKS:
        costs.append([d["cost"][0] + cy * (d["cost"][1] + ga * d["cost"][2] + sc * d["cost"][3]) + pe * d["cost"][4] + (0.012 if d["q"] in "VSEGY" else 0.0) for d in ops])
        lats.append([hop if d["q"] == "A" else d["lat"] for d in ops])
        befores.append([[(p, lats[-1][p] + gap if hard else 0.0) for p, hard in d["preds"].items()] for d in ops])
    cost, seen = costs[0], {}
    before = [list(x) for x in befores[0]]
    for k, d in enumerate(ops):
        for name in d["banks"]:
            before[k] += [(p, CLOCKS[0][4]) for q, p in seen.setdefault(name, {}).items() if q != d["q"]]
            seen[name][d["q"]] = k
    after, later = [[] for _ in ops], [[] for _ in ops]
    for k in range(n):
        for p, lag in before[k]:
            after[p].append((k, lag))
        for p, lag in befores[0][k]:
            later[p].append((k, lag))
    banks = [[8 * int(name[1]) for name in d["banks"]] for d in ops]
    other = [[j for j, q in enumerate("VST") if q != d["q"]] for d in ops]
    own = ["VST".find(d["q"]) for d in ops]

    def lay(turn, needs, tail):
        busy = {q: [] for q in "VSTGY"}
        start, place = [0.0] * n, [d["q"] for d in ops]
        for k in turn:
            first = max([start[p] + cost[p] + lag for p, lag in needs[k]] + [tail[k]])
            if place[k] == "A":
                start[k] = first
                continue
            gaps = []
            for q, late in ((("S", 0.0), ("V", LEAN)) if place[k] == "E" else ((place[k], 0.0),)):
                line, s, j = busy[q], first, len(busy[q])
                while j and line[j - 1][1] > s:
                    j -= 1
                while j < len(line) and line[j][0] < s + cost[k] - 1e-9:
                    s = max(s, line[j][1])
                    j += 1
                gaps.append((s + late, s, j, q))
            _, start[k], j, place[k] = min(gaps)
            busy[place[k]].insert(j, (start[k], start[k] + cost[k]))
        return start, place

    lat = lats[0]
    way = [0.0] * n
    for k in range(n - 1, -1, -1):
        way[k] = cost[k] + max([lag + way[s] for s, lag in after[k]] + [lat[k]])
    turn, best = sorted(range(n), key=lambda k: (-way[k], k)), None
    shake = np.random.default_rng(0)
    held = None
    for it in range(PASSES):
        fore, place = lay(turn, before, [0.0] * n)
        end = max(fore[k] + cost[k] + lat[k] for k in range(n))
        if best is None or end <= best[0]:
            best = (end, fore, place)
        if held is None or end <= held[0] + 0.2 * (1 - it / PASSES) * shake.exponential():
            held = (end, fore)
        done = np.array(held[1]) + np.array(cost)
        key = (done + np.where(np.abs(done - shake.random() * held[0]) < 5, SHAKE * shake.random(n) ** 3, 0.0)).tolist()
        for k in range(n):
            key[k] = max([key[k]] + [key[p] for p, _ in before[k]])
        back = lay(sorted(range(n), key=lambda k: (-key[k], -k)), after, lat)[0]
        turn = sorted(range(n), key=lambda k: (-back[k] - cost[k], k))
    ends = [k for k in range(n) if not later[k]]

    def clock(seq, place, lo=0, old=None):
        last, used, rest = {}, [-1] * 64, []
        for k in seq[:lo]:
            last[place[k]] = k
            for b in banks[k]:
                used[b + own[k]] = k
        for k in seq[lo:]:
            q, turns = place[k], []
            for b in banks[k]:
                turns += [used[b + j] for j in other[k] if used[b + j] >= 0]
                used[b + own[k]] = k
            rest.append((k, last.get(q, -1) if q != "A" else -1, turns))
            last[q] = k
        runs = []
        for m in range(len(CLOCKS)):
            fin, why = (list(old[1][m][1]), list(old[1][m][2])) if old else ([0.0] * n, [-1] * n)
            bef, cst, gap = befores[m], costs[m], CLOCKS[m][4]
            for k, j, turns in rest:
                s, w = (fin[j], j) if j >= 0 else (0.0, -1)
                for p, lag in bef[k]:
                    if fin[p] + lag > s:
                        s, w = fin[p] + lag, p
                for p in turns:
                    if fin[p] + gap > s:
                        s, w = fin[p] + gap, p
                fin[k], why[k] = s + cst[k], w
            e = max(ends, key=lambda k: fin[k] + lats[m][k])
            runs.append((fin[e] + lats[m][e] + EARLY * sum(fin) / n, fin, why, e))
        if not weigh:
            weigh.extend(runs[0][0] / r[0] / len(runs) for r in runs)
        return sum(r[0] * x for r, x in zip(runs, weigh)), runs

    weigh = []

    def closure(k, links, inside):
        found, stack = {k}, [k]
        while stack:
            for x, _ in links[stack.pop()]:
                if inside(x) and x not in found:
                    found.add(x)
                    stack.append(x)
        return found

    seq, place = sorted(range(n), key=lambda k: (best[1][k], k)), best[2]
    held = clock(seq, place)
    best = (held[0], seq, place)
    for it in range(MOVES):
        _, _, why, k = held[1][it % len(CLOCKS)]
        pairs = []
        while why[k] >= 0:
            if why[k] not in ops[k]["preds"]:
                pairs.append((why[k], k))
            k = why[k]
        if not pairs:
            continue
        a, b = pairs[int(shake.random() * len(pairs))]
        if shake.random() < ANY:
            b = int(shake.random() * n)
            a = why[b]
            if a < 0 or a in ops[b]["preds"]:
                continue
        pos = {k: i for i, k in enumerate(seq)}
        i, j, far, kind = pos[a], pos[b], int(shake.random() ** 3 * FAR), shake.random()
        seq2, place2 = list(seq), place
        free = [x for x in (a, b) if ops[x]["q"] == "E"]
        if kind < 0.15 and free:
            x = free[int(shake.random() * len(free))]
            place2 = list(place)
            place2[x] = "V" if place[x] == "S" else "S"
        elif kind < 0.55:
            i = max(0, i - far)
            go = closure(b, befores[0], lambda x: pos[x] >= i)
            seq2[i:j + 1] = [k for k in seq[i:j + 1] if k in go] + [k for k in seq[i:j + 1] if k not in go]
        else:
            j = min(n - 1, j + far)
            go = closure(a, later, lambda x: pos[x] <= j)
            seq2[i:j + 1] = [k for k in seq[i:j + 1] if k not in go] + [k for k in seq[i:j + 1] if k in go]
        new = clock(seq2, place2, i, held)
        if new[0] <= held[0] + HEAT * (1 - it / MOVES) * shake.exponential():
            held, place = new, place2
            seq = sorted(seq2, key=lambda k: new[1][0][1][k] - cost[k]) if it % 20 == 0 else seq2
            if new[0] < best[0]:
                best = (new[0], seq2, place2)
    return [(k, best[2][k]) for k in best[1]]


def rank_program(g, core, T, topo):
    rank = T.rank_of(core)
    if rank is None:
        return
    cores = list(T.cores)
    queue = {"V": g.vector, "S": g.scalar, "T": g.tensor, "G": g, "Y": g.sync}
    cur = [0]
    ops = []
    first = []
    acc = {}
    sums = {}

    def c(name, lo=0, hi=None, step=1):
        buf, o, w = VIEW[name + "#%d" % cur[0] if name in LOCAL else name]
        return (buf, o + lo, o + (w if hi is None else hi), step)

    def meet(a, lo, hi, step):
        if a[1] <= lo or hi <= a[0]:
            return False
        return not (a[2] == step and step > 1 and a[0] % step != lo % step)

    def node(q, calls, outs, ins, cost, lat=0.0, **kw):
        r, w = [], []
        for v in ins:
            if isinstance(v, tuple):
                r += [v[1], v[2]] if v[0] == "@" else [v]
        for v in outs:
            if v[0] == "@":
                w.append(v[1])
                r.append(v[2])
            else:
                w.append(v)
        k, preds = len(ops), {}
        for kind, views in ((0, r), (1, w)):
            for (name, lo, hi, step) in views:
                psum = SCRATCH[name][0] == "psum"
                for a in acc.get(name, []):
                    if not meet(a, lo, hi, step) or (a[3] == 0 and kind == 0):
                        continue
                    preds[a[4]] = preds.get(a[4], False) or not (psum and q == "T" and ops[a[4]]["q"] == "T")
        banks = sorted({v[0] for v in r + w if SCRATCH[v[0]][0] == "psum"})
        if q == "T":
            for name in banks:
                for p in sums.setdefault(name, []):
                    if kw.get("part") or ops[p].get("part"):
                        preds.setdefault(p, False)
                sums[name] = ([] if kw.get("part") else sums[name]) + [k]
        for (name, lo, hi, step) in w:
            acc[name] = [a for a in acc.get(name, []) if not (lo <= a[0] and a[1] <= hi and step == 1)]
            acc[name].append([lo, hi, step, 1, k])
        for (name, lo, hi, step) in r:
            acc.setdefault(name, []).append([lo, hi, step, 0, k])
        for p in first:
            preds.setdefault(p, False)
        d = {"q": q, "calls": calls, "preds": preds, "cost": cost, "lat": lat, "outs": outs, "banks": banks}
        d.update(kw)
        ops.append(d)
        return k

    def ap(v):
        name, lo, hi, step = v
        return T[name][:, lo:hi:step]

    def opnd(v):
        if isinstance(v, tuple):
            return ap(v[1]).indirect(ap(v[2])) if v[0] == "@" else ap(v)
        return v

    def at(win, off):
        return ("@", win, off)

    def width(v):
        return 16 * (v[2][2] - v[2][1]) if v[0] == "@" else -(-(v[2] - v[1]) // v[3])

    def size2(v):
        return SCRATCH[(v[1] if v[0] == "@" else v)[0]][2] in ("bfloat16", "uint16", "float16")

    def cyc(out, ins, two=False):
        n = width(out)
        if out[0] == "@":
            return (0, 60, 0, n, 0)
        if any(v[0] == "@" for v in ins):
            return (0, 60, n, 0, 0)
        if two:
            return (0, max(64, n * (1 if any(SCRATCH[v[0]][0] == "psum" for v in ins) else 2)), 0, 0, 0)
        return (0, max(64, n * (0.5 if all(size2(v) for v in [out] + ins) else 1)), 0, 0, 0)

    def vec(call, out, ins, cy):
        node("V", [call], [out], ins, cy)

    def tt(out, a, b, op):
        vec(lambda: g.vector.tensor_tensor(opnd(out), opnd(a), opnd(b), op), out, [a, b], cyc(out, [a, b], True))

    def ts(out, a, s1, op0, s2=None, op1=None):
        if op1 is None:
            vec(lambda: g.vector.tensor_scalar(opnd(out), opnd(a), opnd(s1), None, op0), out, [a, s1], cyc(out, [a]))
        else:
            vec(lambda: g.vector.tensor_scalar(opnd(out), opnd(a), opnd(s1), opnd(s2), op0, op1), out, [a, s1, s2], cyc(out, [a]))

    def cp(out, a):
        vec(lambda: g.vector.tensor_copy(opnd(out), opnd(a)), out, [a], cyc(out, [a]))

    def fill(out, x):
        vec(lambda: g.vector.memset(ap(out), x), out, [], cyc(out, []))

    def act(out, a, scale=1.0, bias=0.0, func=F.Copy, total=None):
        n = width(out)
        cost = (0, 78, n, 0, 0) if a[0] == "@" else (0, max(64, n), 0, 0, 0)
        if total is None:
            node("S", [lambda: g.scalar.activation(opnd(out), opnd(a), func, bias=opnd(bias), scale=opnd(scale))], [out], [a, bias, scale], cost)
        else:
            node("S", [lambda: g.scalar.activation(opnd(out), opnd(a), func, bias=bias, scale=scale, accum_out=ap(total))], [out, total], [a], (0.14,) + cost[1:])

    def fetch(q, out, win, off):
        a = at(win, off)
        if q != "E":
            return (cp if q == "V" else act)(out, a)
        node("E", {"V": lambda: g.vector.tensor_copy(opnd(out), opnd(a)), "S": lambda: g.scalar.activation(opnd(out), opnd(a), F.Copy)},
             [out], [a], (0, 70, width(out), 0, 0))

    def scan(out, d0, d1, op0, op1):
        vec(lambda: g.vector.tensor_tensor_scan(ap(out), ap(d0), ap(d1), 0.0, op0, op1), out, [d0, d1], cyc(out, [d0, d1]))

    def mms(lst):
        calls = [lambda o=o, l=l, r=r, s=s, e=e: g.tensor.matmul(ap(o), ap(l), ap(r), s, e) for o, l, r, s, e in lst]
        cost = sum(max(64, width(r)) * (1 if size2(r) else 4) for o, l, r, s, e in lst)
        node("T", calls, [x[0] for x in lst], [x[1] for x in lst] + [x[2] for x in lst], (0, 0, 0, 0, cost), part=not (lst[0][3] and lst[-1][4]))

    def total(out, terms, start=True, stop=True):
        mms([(out, l, r, start and j == 0, stop and j == len(terms) - 1) for j, (l, r) in enumerate(terms)])

    def gps(call, out, ins, base):
        node("G", [call], [out], ins, (base, width(out) * 2, 0, 0, 0))

    def iota(v, pattern, base, cm):
        if SCRATCH[v[0]][2] != "int32":
            gps(lambda: g.iota(ap(v), pattern, base, cm, allow_small_or_imprecise_dtypes=True), v, [], 0.15)
        else:
            gps(lambda: g.iota(ap(v), pattern, base, cm), v, [], 0.15)

    def const(v, x, q="S"):
        if q == "G":
            iota(v, [[0, width(v)]], x, 0)
        else:
            act(v, c("ALL1", 0, width(v)), float(x))

    def select(out, a, pattern, op, base, cm, other=0.0):
        gps(lambda: g.affine_select(ap(out), ap(a), pattern, op, other, base, cm), out, [a], 0.2)

    def dma(q, out_ap, in_ap, sem, reads, writes, lat):
        return node(q, [lambda: queue[q].dma_start(out_ap, in_ap)], writes, reads, (0.1, 0, 0, 0, 0), lat, sem=sem)

    def rows(v, lo, hi, step=1):
        return T[v[0]][lo:hi:step, v[1]:v[2]]

    def send(dst_rank, src_rank, out_v, in_v, sem):
        dst = cores[dst_rank % N]
        m = topo.mask(core, dst)
        rid, pid, _ = topo.addr(dst)
        k = node("G", [lambda: g.remote_dma(ap(out_v), ap(in_v), T.sem[sem], T.sem.loc, pid, rid, m)], [], [in_v], (0.3, 0, 0, 0, 0),
                 sent=len(topo.engines(core, dst)))
        n = len(topo.engines(cores[src_rank % N], core))
        ops.append({"q": "A", "calls": [], "preds": {k: False}, "cost": (0, 0, 0, 0, 0), "lat": 0.0, "sem": sem, "amount": n, "banks": []})
        acc.setdefault(out_v[0], []).append([out_v[1], out_v[2], 1, 1, len(ops) - 1])

    def lane(w, b):
        return c(w, 15 - b, 143 - b)

    EX = lambda b: c("EX", 128 * b, 128 * b + 128)
    ID = c("IDW", 15, 143)

    def lanes16(w, src, lo, n):
        return [(lane(w, b), c(src, lo + b, lo + 16 * n, 16)) for b in range(16)]

    def blocks(w, src, lo, n, bs=range(16)):
        return [(lane(w, b), c(src, lo + n * b, lo + n * b + n)) for b in bs]

    def spread(bank, lo, src, n, plus=None):
        if plus:
            total(c(bank, lo, lo + 16 * n), [(ID, plus)], stop=False)
        mms([(c(bank, lo + n * b, lo + n * b + n), EX(b), src, not plus, not plus or b == 15) for b in range(16)])

    FL = c("FLB", 0, 160)

    def half(n, par):
        return c(n, 160 * par, 160 * par + 160)

    def lists(par):
        return c("GL%d" % par, OFF + par, OFF + 320, 2)

    dma("Y", ap(c("GLI")), T.gl[:, :], "d_gl", [], [c("GLI")], 1.8)
    first.append(0)
    first.append(dma("S", rows(c("V5"), 0, 8), T.val[:, :], "d_v5", [], [c("V5")], 1.6))
    first.append(dma("S", ap(c("VAI")), T.val[:, :], "d_va", [], [c("VAI")], 1.6))
    first.append(dma("Y", ap(c("NBI")), T.nb[:, :], "d_nb", [], [c("NBI")], 2.0))
    first.append(dma("Y", ap(c("THI")), T.th[:, :], "d_th", [], [c("THI")], 1.8))
    first.append(dma("Y", ap(c("Z0", 16, 176)), T.zl[:, :], "d_zl", [], [c("Z0", 16, 176)], 2.0))
    dma("Y", ap(c("RW", 0, 4096)), T.rec[:, :], "d_rec", [], [c("RW", 0, 4096)], 6.0)
    first.clear()

    iota(c("PI32"), [[0, 1]], 0, 1)
    iota(c("WI"), [[1, 144]], -15, 0)
    iota(c("HI", 0, 352), [[-16, 22], [0, 16]], 0, 0)
    iota(c("LO", 0, 352), [[0, 22], [-1, 16]], 0, 0)
    iota(c("HI", 352, 672), [[64, 16], [0, 20]], 64, 0)
    iota(c("LO", 352, 672), [[0, 16], [2, 20]], -19, 0)
    fill(c("ALL1"), 1.0)
    act(c("K512"), c("LO", 0, 160), 512.0, 7680.0)
    act(c("K8K"), c("LO", 0, 160), 8192.0, 122880.0)
    iota(c("TI"), [[1, 20]], 0, 20)
    iota(c("MAJ"), [[1, 20], [20, 16]], OFF, 0)
    iota(c("M1V"), [[2, 320]], 613, 0)
    act(c("K15"), c("LO", 0, 160), 1.0, 15.0)
    act(c("KX"), c("HI", 0, 160), -32768.0)
    iota(c("IOT", 0, 200), [[0, 10], [-2, 20]], 19, 0)
    const(c("IOT", 200, 208), 99, "G")
    iota(c("CJF"), [[16, 14]], 0, 0)
    for b in range(0, 16, 4):
        select(c("EX", 128 * b, 128 * b + 512), c("ALL1"), [[-1, 4], [-16, 8], [0, 16]], A.is_equal, -b, 1)
    for i in (0, 1):
        const(c("GL%d" % i, 0, OFF), -5)
    const(c("RW", 4096, 4112), 0, "G")
    zero = c("DX2", 320, 1600)
    for lo in range(320, 1600, 320):
        const(c("DX2", lo, lo + 320), 0.0)
    for j, (n, lo) in enumerate((("DX0", 320), ("DX0", 1600), ("DX1", 320), ("DX1", 1600), ("DX2", 1600))):
        dma("Y", ap(c(n, lo, lo + 1280)), ap(zero), "d_z%d" % j, [zero, c("RW", 0, 4096)], [c(n, lo, lo + 1280)], 3.0 + j)
    for t in range(RO):
        const(c("Z%d" % t, 0, 16), 0, "G")
    const(c("CNH"), -0.5)
    const(c("ON10"), 1, "G")
    const(c("FLB"), 1)
    const(c("FLB", 0, 320, 16), 0)
    const(c("DR5"), 0)
    const(c("DR5", 0, 100, 5), 1048576)
    for i in (1, 0):
        cur[0] = i
        for n in ("HF", "CS", "TH"):
            const(c(n), 0, "G")
        const(c("SL", 0, 320, 2), 1, "G")
        const(c("SL", 0, 320, 32), 0, "G")

    ts(c("LI"), c("PI32"), 15, A.bitwise_and)
    ts(c("LGI"), c("PI32"), 112, A.bitwise_and)
    cp(c("LG"), c("LGI"))
    cp(c("LN"), c("LI"))
    cp(c("PF"), c("PI32"))
    ts(c("SS"), c("WI"), c("LG"), A.is_equal, 64.0, A.mult)
    ts(c("IDW"), c("WI"), c("PF"), A.is_equal)
    const(c("PI", 0, 320, 2), 0.0)
    const(c("PI", 1, 320, 2), -524288.0)
    const(c("DUM"), -1048576.0)
    const(c("D256", 0, 31), 0.0)
    const(c("D256", 31, 32), 256.0)
    const(c("C185"), -18.5)
    ts(c("cu"), c("LN"), 4.5, A.is_le, 1.0 / 32, A.mult)
    ts(c("c3"), c("LN"), 2.5, A.is_ge, 0.5, A.subtract)
    ts(c("WM"), c("SS"), c("c3"), A.mult, c("cu"), A.mult)
    const(c("C4K"), -4096.0)
    ts(c("cd"), c("LN"), 5.0, A.is_equal, 0.25, A.mult)
    act(c("WD"), c("SS"), c("cd"))
    ts(c("wk"), c("c3"), c("cu"), A.mult, 256.0, A.mult)
    ts(c("wk"), c("wk"), c("cd"), A.add, 1.0 / 16, A.mult)
    ts(c("WK"), c("SS"), c("wk"), A.mult)
    ts(c("c16"), c("PF"), 16.0, A.mult, 5.0, A.add)
    ts(c("L8"), c("WI", 15, 143), c("c16"), A.is_equal, 64.0, A.mult)
    ts(c("cn"), c("LN"), 15.0, A.is_equal, 1.0 / 32, A.mult)
    ts(c("cn"), c("cn"), 1.0 / 16384, A.max)
    act(c("WN"), c("SS"), c("cn"))
    select(c("TRA"), c("ALL1", 0, 128), [[16, 8], [0, 16]], A.is_ge, 15, -1)
    select(c("B1"), c("TRA"), [[-16, 8], [0, 16]], A.is_ge, 0, 1)
    select(c("TRI"), c("B1"), [[1, 128]], A.is_gt, 0, -1)
    iota(c("BLA"), [[0, 8], [-64, 16]], -64, 0)
    select(c("BLB"), c("BLA"), [[16, 8], [0, 16]], A.is_ge, 15, -1, 1.0)
    select(c("BLC"), c("BLB"), [[-16, 8], [0, 16]], A.is_ge, 0, 1, 1.0)
    act(c("B1N"), c("B1"), -1024.0)
    act(c("ID8"), ID, -8.0)
    act(c("ID32"), ID)
    act(c("IDN"), ID, -1.0)
    act(c("IDH"), ID, 0.5)
    ts(c("cs"), c("LN"), 15.0, A.not_equal, -1.0, A.mult)
    act(c("SHB"), c("IDW", 14, 142), c("cs"))
    ts(c("cp"), c("LN"), 0.5, A.is_ge, -131072.0, A.mult)
    ts(c("ck"), c("LN"), 1.0 / 64, A.mult)
    act(c("WL"), c("SS"), c("ck"))
    act(c("ID4"), ID, 4.0)
    act(c("DR"), FL, -4194304.0, 4194304.0)
    ts(c("LG20"), c("LG"), -20.0, A.mult)
    ts(c("AC"), c("TI"), c("LG20"), A.add)
    act(c("A17"), c("AC"), 2.0 / 64, 17.0 / 64)
    for j in range(4):
        act(c("AC4", 20 * j, 20 * j + 20), c("AC"))
    for par in (0, 1):
        act(c("AK", 20 * par, 20 * par + 20), c("AC"), 1.0, 8.0 * par - 252)
    act(c("AC16"), c("AC4"), 1.0 / 16)
    act(c("AC23"), c("AC4"), -23.5, -0.25)
    act(c("CM40", 0, 20), c("AC"), 16.0, 296.0)
    act(c("CM40", 20, 40), c("AC"), 2.0, 613.0)
    if MASK:
        act(c("CM4"), c("AC"), 0.5, 9.25)
    if len(MASK) < 2:
        act(c("CM2"), c("AC"), 2.0, 37.0)
    act(c("VY"), c("M1V"), 1.0 / 32, -596.0 / 32)
    ts(c("cj"), c("LN"), -9.5, A.add)
    ts(c("CJ"), c("CJF"), c("cj"), A.add, 0.05, A.mult)
    cp(c("COFF"), c("CJ"))
    ts(c("CJG"), c("CJ"), -20.0, A.mult, c("LN"), A.add)
    tt(c("CJH"), c("CJG", 0, 6), c("CJF", 0, 6), A.add)
    cp(c("BC"), c("CJH"))
    four = lambda v: at(v, c("BC", 0, 5))

    ts(c("VALN"), c("GLI"), 0.0, A.is_ge, -131072.0, A.mult)
    for par in (0, 1):
        ts(half("AOU", par), c("GLI", par, 320, 2), float(OFF), A.add)
    vec(lambda: g.vector.tensor_scalar(rows(c("R16"), 0, 8), rows(c("V5"), 0, 8), 16.0, None, A.mult), c("R16"), [c("V5")], cyc(c("R16"), [c("V5")]))
    statics = [(lane("SS", 1), c("HI", OFF, 352)), (lane("SS", 2), c("LO", OFF, 352)), (lane("SS", 3), c("PI"))]
    total(c("P0", 0, OFF), [(lane("SS", 4), c("DUM")), (lane("SS", 5), c("D256"))])

    def values(out, stop):
        node("T", [lambda: g.tensor.matmul(ap(out), rows(c("L8"), 0, 8), rows(c("R16"), 0, 8), False, stop)], [out], [c("L8"), c("R16")], (0, 0, 0, 0, 320), part=True)

    def sizes(par):
        seventh = c("P0", OFF + par, 352, 2)
        mms([(seventh, lane("SS", 7), c("VALN", par, 320, 2), False, False), (c("P0", OFF, 352), lane("SS", 0), c("VALN"), False, True)])

    total(c("P0", OFF, 352), statics, stop=False)
    mms([(c("P0", OFF + 1, 352, 2), lane("SS", 7), c("C4K"), False, False)])
    values(c("P0", OFF, 352), False)
    sizes(1)
    act(c("DW0", 0, 352), c("P0", 0, 352), 1.0 / 1024)
    ts(c("GL0", OFF), c("GLI"), float(OFF), A.add)
    act(c("GL1", OFF), c("GL0", OFF))
    for n in ("DW1", "ST"):
        act(c(n, 0, OFF), c("DW0", 0, OFF))
    for j, x in enumerate((1, 2, 3, 0)):
        act(c("JK", j, 100, 5), c("DUM", 0, 20), 0.0, float(x))
        act(c("JC", 20 * j, 20 * j + 20), c("DUM", 0, 20), 0.0, x - 0.5 if x else 7.5)
    act(c("JK", 4, 100, 5), c("DUM", 0, 20), -1.0)
    if MASK:
        act(c("C72"), c("DUM", 0, 20), 0.0, -7200.0)
        iota(c("X16"), [[1, 20]], 16, 0)
        mms([(c("P1", 20 * b, 20 * b + 20), lane("SS", b), c("X16"), True, True) for b in range(16)])
        act(c("LX", OFF, 352), c("P1", 0, 320), -1.0 / 1024, 8.0)
        const(c("LX", 0, OFF), 8, "G")
    act(c("CN75"), c("DUM", 0, 20), 0.0, -7.5)
    for lo in range(0, 2048, 512):
        select(c("EX5", lo, lo + 512), c("EX", lo, lo + 512), [[0, 32], [1, 16]], A.is_equal, -5, 0)
    ts(c("c75"), c("LN"), 5.0, A.is_equal, 7.5, A.mult)
    for up in (0, 8):
        col = lambda j: c("co", up + j, up + j + 1)
        ts(col(0), c("LN"), up + 1.0, A.is_equal)
        ts(col(1), c("LN"), up + 2.0, A.is_equal, col(0), A.add)
        ts(col(2), c("LN"), up + 7.0, A.is_equal, col(1), A.add)
        ts(c("WO%d" % up), c("SS"), col(2), A.mult, -1.0 / 64, A.mult)
    act(c("UP8"), c("IDW", 7, 135), c("co", 2, 3))

    def entries(par, win, queues, keys, w="WM", slot="K512"):
        for j, q in enumerate(queues):
            n = 160 // len(queues)
            lo = 2880 * par + 16 * n * j
            fetch(q, c("SG", lo, lo + 16 * n), c(win, 0, 352), c("AOU", 160 * par + n * j, 160 * par + n * j + n))
            if keys:
                nb = 16 // len(queues)
                total(keys, ([(ID, c(slot))] if j == 0 else []) + blocks(w, "SG", 2880 * par, 160, range(nb * j, nb * j + nb)), j == 0, j == len(queues) - 1)

    PK = (c("P7", 320, 480), c("P3", 160, 320))
    for par in (0, 1):
        entries(par, "DW0", FIRST[par], PK[par], "WK", "K8K")
        scan(half("R1", par), FL, PK[par], A.mult, A.max)
        cp(c("KB0", par, 20, 2), c("R1", 160 * par + 15, 160 * par + 160, 16))
    for par in (0, 1):
        act(half("AB", par), PK[par], 1.0, 4194304.0, F.Abs)
        scan(half("R2", par), c("DR"), half("AB", par), A.max, A.min)
        ts(c("KB1", par, 20, 2), c("R2", 160 * par + 15, 160 * par + 160, 16), -1.0 / 16, A.mult, 262143.53125, A.add)

    NBP = c("P4", 0, 320)
    cp(c("NBH"), c("NBI"))
    mms([(c("P4", b, 320, 16), ID, c("NBH", 20 * b, 20 * b + 20), True, True) for b in range(16)])
    ts(c("SO0"), c("VAI"), -7.5, A.add)
    total(c("P1", 0, 320), [(lane("SS", 1), c("HI", 352, 672)), (lane("SS", 2), c("LO", 352, 672))], stop=False)
    values(c("P1", 0, 320), True)
    act(c("GDI"), c("P1", 0, 320), 1.0 / 1024)
    send(rank - 1, rank + 1, c("DW0", 352, 672), c("GDI"), "ag0")
    dma("Y", ap(c("ST", 352, 672)), ap(c("GDI")), "d_c0", [c("GDI")], [c("ST", 352, 672)], 2.0)
    ts(c("th0"), c("THI"), 64.0, A.mult, 16.0 + 992.0, A.add)
    tt(c("th64"), c("th0"), c("KX", 0, 160, 16), A.add)
    act(c("TH", 0, 160, 16), c("th64"), 1.0, -992.0)
    const(c("C155"), -15.5)
    total(c("P6", 416, 436), blocks("WN", "VALN", 0, 20))
    act(c("BASE"), c("P6", 416, 436), -1.0, 4096.0 - 7680.0)
    for par in (0, 1):
        act(half("APR", par), lists(par), 32.0, -432.0)

    def prep(t):
        par = t & 1
        cur[0] = par
        if t:
            ts(c("EI"), c("KB%d" % t), 511, A.bitwise_and)
        else:
            ts(c("EI"), c("KB0"), 4, A.arith_shift_right, 511, A.bitwise_and)
        cp(c("EOU", 0, 20), c("EI"))
        ts(c("EZU"), c("EI"), 0.5, A.mult, -0.5 * par, A.add)
        ts(c("EH"), c("EI"), 2.0, A.mult, -47.0, A.add)
        if t:
            v17 = c("P6", 416, 496)
            mms([(c("P6", 416 + 20 * j, 436 + 20 * j), ID, c("EH"), True, True) for j in range(4)])
            act(c("MM"), v17, 16.0, 9536.0)
            tt(c("BB"), v17, c("AC4"), A.mult)
        if t in MASK:
            fetch("S", c("LM"), c("LX"), c("EOU", 0, 20))
            total(c("P6", 64, 84), lanes16("SS", "LM", 0, 20))
            ts(c("XU"), c("P6", 64, 84), -1.0 / 64, A.mult, 112.0, A.add)
        tt(c("W3", 320, 640), at(c("GL%d" % par), c("EOU", 0, 20)), c("MAJ"), A.is_equal)
        tt(c("W3", 0, 320), c("W3", 320, 640), NBP, A.mult)
        total(c("P6", 0, 40), lanes16("SS", "W3", 0, 40))
        po, pm, pk = c("P6", 0, 20), c("P6", 20, 40), c("P6", 40, 60)
        ts(c("EOU", 20, 40), po, 1.0 / 64, A.mult, float(OFF), A.add)
        tt(c("BO"), po, c("A17"), A.mult)
        act(c("MO"), po, 0.5, 592.0)
        act(c("NMB"), pm, -4096.0, 262144.0)
        total(pk, lanes16("WL", "W3", 320, 20) + [(c("ID4"), c("EH")), (c("IDN"), c("NMB"))])
        tt(c("PX"), pk, c("AK", 20 * par, 20 * par + 20), A.max)
        ts(c("PU"), c("PX"), 252.0 - 8 * par, A.add)
        if t:
            fetch("E", c("CD"), c("ST"), c("EOU", 20, 40))

    prep(0)

    for t in range(RO):
        par = t & 1
        cur[0] = par
        zw, dw, gw, last = "Z%d" % t, "DW%d" % par, "GW%d" % par, t == RO - 1
        own = c(dw, OFF, 352)
        so = c("CL%d" % (t - 1)) if t else c("SO0")
        if t:
            spread("P1", 0, c("CN%d" % (t - 1)), 20)
            act(c(dw, 352, 672), c("P1", 0, 320), 1.0, 7.5)
            col = lambda b: c("P0", OFF + 20 * b, OFF + 20 * b + 20)
            total(c("P0", OFF, 352), [(ID, c("ST", OFF, 352))], stop=False)
            mms([(col(b), c("UP8"), c("CD", b, 320, 16), False, False) for b in range(16)])
            mms([(col(b), c("EX5", 128 * b, 128 * b + 128), so, False, b == 15) for b in range(16)])
            act(own, c("P0", OFF, 352), 1.0, c("c75"), F.Identity)
        for j in (1, 2, 3):
            act(c("SGN", 20 * j - 20, 20 * j), so, 1.0, j - 8.0, F.Sign)
        mms([(c("P2", 64, 144), ID, c("JC"), True, False)] + [(c("P2", 64 + 20 * j, 84 + 20 * j), ID, so, False, False) for j in range(4)])
        total(c("P2", 64, 124), [(c("ID8"), c("SGN"))], start=False)
        p4 = c("P2", 64, 144)
        if t:
            tt(c("P4", 320, 400), p4, c("MM"), A.mult)
            act(c("PH"), p4)
            tt(c("TP"), c("P4", 320, 400), c("BB"), A.add)
            if t in MASK:
                tt(c("QD", 0, 320), at(so, c("XU")), c("LM"), A.max)
                total(c("P1", 320, 340), [(ID, c("C72"))], stop=False)
                total(c("P1", 320, 340), lanes16("SS", "QD", 0, 20), start=False)
                tt(c("U"), c("P1", 320, 340), c("CM4"), A.mult)
            else:
                fetch("E", c("QD", 0, 320), c(dw, 0, 352), c("EOU", 0, 20))
                total(c("P1", 320, 340), lanes16("WD", "QD", 0, 20))
                tt(c("U"), c("P1", 320, 340), c("CM2"), A.mult)
            tt(c("T6", 0, 80), four(c("U")), c("TP"), A.add)
        else:
            tt(c("C1"), p4, c("AC16"), A.add)
            act(c("P44"), p4, 4392.0)
            act(c("PH"), p4)
            tt(c("C0"), c("P44"), c("AC23"), A.add)
            ts(c("DV"), c("KB0"), 15, A.bitwise_and)
            ts(c("E16"), c("KB0"), 511 * 16, A.bitwise_and)
            tt(c("U"), c("DV"), c("CM40", 0, 20), A.mult)
            tt(c("V4"), four(c("E16")), c("C1"), A.mult)
            tt(c("TP"), four(c("U")), c("C0"), A.add)
            tt(c("T6", 0, 80), c("V4"), c("TP"), A.add)
        ts(c("IX", 0, 80), c("T6", 0, 80), 4 if t else 3, A.arith_shift_right, 4095, A.bitwise_and)
        cp(c("IXU", 0, 80), c("IX", 0, 80))
        fetch("S", c("QD", 320, 640), c(dw), c("EOU", 20, 40))
        total(c("P1", 352, 372), lanes16("WD", "QD", 320, 20))
        tt(c("TO"), four(c("MO")), c("PH"), A.mult)
        tt(c("UO"), c("P1", 352, 372), c("CM40", 20, 40), A.mult)
        tt(c("B2"), c("UO"), c("BO"), A.add)
        tt(c("T6", 80, 160), four(c("B2")), c("TO"), A.add)
        ts(c("IX", 80, 160), c("T6", 80, 160), 4, A.arith_shift_right, 4095, A.bitwise_and)
        cp(c("IXU", 80, 100), c("IX", 140, 160))
        ts(c("H16"), c("IX"), -2048.0, A.add)

        def steps(bank, lo, src, at0):
            blk = lambda j: c(src, at0 + 20 * j, at0 + 20 * j + 20)
            lst = []
            for j in range(5):
                terms = ([(ID, blk(j - 1))] if j else []) + ([(c("IDN"), blk(j))] if j < 4 else [])
                lst += [(c(bank, lo + j, lo + 100, 5), l, r, i == 0, i == len(terms) - 1) for i, (l, r) in enumerate(terms)]
            mms(lst)
            return c(bank, lo, lo + 100)

        dn, dr, dp = steps("P5", 288, "H16", 80), steps("P5", 388, "H16", 0), steps("P4", 400, "PH", 0)
        if t:
            entries(par, dw, "E" * PIECE, None)
        PD, PY = c("P3", 0, 160), c("P0", 352, 512)
        total(PY, [(c("ID32"), c("VY", par, 320, 2))], stop=False)
        total(PY, [(EX(5), c(dw, OFF + par, 352, 2))], start=False)
        tt(c("T1"), PY, half("APR", par), A.mult)
        act(c("T2"), c("T1"), 1.0, 11026.0)
        for lo, hi in (((0, 80), (80, 160)) if t else ((0, 160),)):
            pd = c("P3", lo, hi)
            for hf in range(lo, hi, 80):
                total(c("P3", hf, 80 + hf), [(ID, c("C185"))] + lanes16("WD", "SG", 2880 * par + 16 * hf, 80))
            tt(pd, pd, c("M1V", par + 2 * lo, 2 * hi, 2), A.mult)
            tt(c("UQ", lo, hi), pd, c("T2", lo, hi), A.add)
            ts(c("UF", lo, hi), c("UQ", lo, hi), 4, A.arith_shift_right, 4095 + 15 * 65536, A.bitwise_and)
            ts(c("UI", lo, hi), c("UF", lo, hi), 4096.0, A.min)
        n = 160 // PIECE
        for lo in range(0, 160, n):
            fetch("E", c(gw, 320 + 16 * lo, 320 + 16 * (lo + n)), c("RW"), c("UI", lo, lo + n))
        if t == 1:
            total(PK[1], [(ID, c("K512"))] + blocks("WM", "SG", 2880, 160))
            scan(half("R1", 1), FL, PK[1], A.mult, A.max)
        if t == 0:
            for h in (0, 10):
                cp(at(c("SG", 2560, 5440), c("PU", h, h + 10)), c("QD", 320 + 16 * h, 480 + 16 * h))
        for h in (0, 8):
            total(c("P7", 0, 160), blocks("WO8" if t else "WO0", "SG", 2880 * par if t else 2880, 160, range(h, h + 8)), h == 0, h == 8)
        act(c("YY", 0, 320, 2), c("P7", 0, 160), -1.0)
        act(c("YY", 1, 320, 2), c("P7", 0, 160))
        fetch("S", c("ZE"), c(zw), c("EZU"))
        keys = c("P2", 192, 292)
        key = lambda j: c("P2", 192 + j, 292, 5)
        mms([(keys, ID, c("JK"), True, False)] + [(key(j), ID, c("NMB"), False, False) for j in range(3)])
        for j in range(AID):
            total(key(j), lanes16("SS", "ZE", 0, 20), False, False)
        for j in range(AID):
            fetch("S", c("XR"), c("RW", 0, 4096), c("IXU", 20 * j, 20 * j + 20))
            total(c("P0", 0, 320), [(c("IDN"), c("ZE")), (ID, c("XR"))])
            act(c("X", 320 * j, 320 * j + 320), c("P0", 0, 320), 1.0, 0.0, F.Relu)
        for j in range(3, -1, -1):
            if j >= AID:
                tt(c("X", 320 * j, 320 * j + 320), at(c("RW", 0, 4096), c("IXU", 20 * j, 20 * j + 20)), c("ZE"), A.max)
            total(key(j), lanes16("SS", "X", 320 * j, 20), False, j == 0)
        tt(c("XO"), at(c("RW", 0, 4096), c("IXU", 80, 100)), c("ZE"), A.max)
        act(c("NXO"), c("XO"), -1.0)
        scan(c("KS"), c("DR5"), keys, A.max, A.min)
        tt(c("NQ"), keys, c("KS"), A.not_equal)
        scan(c("SN"), dn, c("NQ"), A.add, A.mult)
        ts(c("IXN", 20, 40), c("SN", 4, 100, 5), 2048.0, A.add)
        scan(c("SR"), dr, c("NQ"), A.add, A.mult)
        ts(c("IXN", 0, 20), c("SR", 4, 100, 5), 2048.0, A.add)
        scan(c("SP"), dp, c("NQ"), A.add, A.mult)
        act(c("GD%d" % t), c("SP", 4, 100, 5))
        send(rank - 1, rank + 1, c("GH%d" % (t + 1)), c("GD%d" % t), "ag%d" % (t + 1))
        tt(c("XN"), at(c("RW", 0, 4096), c("IXN", 20, 40)), c("ZE"), A.max)
        tt(at(c("DX%d" % t), c("PU")), c("XN"), c("NXO"), A.add)
        P5 = c("P5", 0, 160)
        total(P5, [(ID, c("K15")), (ID, c("KX"))], stop=False)
        total(P5, blocks("SS", "DX%d" % t, 320, 160), start=False)
        fetch("S", c("RN"), c("RW", 0, 4096), c("IXN", 0, 20))
        scan(c("S1"), c("TH"), P5, A.max, A.max)
        tt(c("SL", 1, 320, 2), P5, c("S1"), A.not_equal)
        scan(c("S2"), c("SL"), c("YY"), A.mult, A.add)
        y = c("S2", 31, 320, 32)
        ts(c("xb"), y, 0.0, A.is_lt, 1.0 / 64, A.mult)
        ts(c("w"), y, 64 * ROUND, A.add, -64 * ROUND, A.add)
        ts(c("xk"), y, 4096 * ROUND, A.add, -4096 * ROUND, A.add)
        tt(c("xj"), y, c("xk"), A.subtract)
        if not last:
            if t == 1:
                entries(0, "ST", "E" * PIECE, c("P6", 64, 224))
                scan(half("R1", 0), FL, c("P6", 64, 224), A.mult, A.max)
                cp(c("KB2", 0, 20, 2), c("R1", 15, 160, 16))
            ts(c("inj"), y, 0.0, A.not_equal)
            tt(c("KM", 0, 10), c("R1", 175, 320, 16) if t else c("KB1", 0, 20, 2), c("BASE", par, 20, 2), A.add)
            ts(c("KM", 10, 20), c("KM", 0, 10), 4096.0, A.max)
            tt(c("KB%d" % (t + 1), par, 20, 2), c("KM", 10, 20), y, A.max)
        scan(c("CS", 0, 10), c("ON10"), c("xb"), A.mult, A.add)
        total(c("P5", 192, 193), [(c("TRI"), c("CS", 9, 10))])
        for x in range(10):
            ts(c("LH", 128 * x, 128 * x + 128), c("BLC"), c("w", x, x + 1), A.is_equal)
        if t in WIDE:
            tt(c("HF", 0, 10), y, c("w"), A.subtract)
            tt(c("NM"), at(c("HF"), c("COFF", 0, 13)), c("IOT"), A.not_equal)
            tt(c("RG"), at(c("CS"), c("COFF", 0, 13)), c("NM"), A.add)
            ts(c("RH", 0, 200), c("RG", 0, 200), c("P5", 192, 193), A.add, CAP / 64, A.is_le)
        else:
            tt(c("h"), y, c("w"), A.subtract)
            ts(c("prf"), c("CS", 0, 10), c("P5", 192, 193), A.add, CAP / 64, A.is_gt)
            tt(c("HF", 0, 10), c("prf"), c("h"), A.add)
            tt(c("RH"), at(c("HF"), c("COFF", 0, 13)), c("IOT"), A.is_equal)
        new = c("P5", 256, 276)
        total(new, [(ID, c("CN75")), (ID, c("GH%d" % (t + 1)))] + [(c("LH", 128 * x, 128 * x + 128), c("RH", 20 * x, 20 * x + 20)) for x in range(10)])
        ts(c("SGR"), new, 16 * ROUND, A.add, -16 * ROUND, A.add)
        tt(c("CN%d" % t), new, c("SGR"), A.subtract)
        send(rank + 1, rank - 1, c("CL%d" % t), c("CN%d" % t), "ac%d" % t)
        for h in (0, 10):
            cp(at(c(gw), c("PU", h, h + 10)), c("RN", 16 * h, 16 * h + 160))
        for lo in range(0, 2560, 320):
            scan(c("GS", lo, lo + 320), c("FLB"), c(gw, 320 + lo, 640 + lo), A.mult, A.max)
        total(PD, [(c("IDH"), c("CNH")), (c("IDH"), c(zw, 16, 176)), (c("IDH"), c("GS", 15, 2560, 16))])
        ts(c("ZS%d" % t), PD, ROUND, A.add, -ROUND, A.add)
        send(rank + 1 + t, rank - 1 - t, c("Z%d" % (t + 1), 16, 176), c("ZS%d" % t), "az%d" % (t + 1))
        l1, val = lists(par), c("VALN", par, 320, 2)
        P1, PJ = c("P1", 320, 480), c("P7", 160, 320)
        spread("P1", 320, c("xj"), 10)
        tt(c("JQ"), P1, l1, A.is_equal)
        act(c("P1C"), P1, 1.0, c("cp"), F.Identity)
        total(PJ, [(ID, val), (c("SHB"), val), (c("B1N"), c("JQ")), (c("ID32"), c("P1C"))])
        tt(l1, PJ, l1, A.max)
        if t:
            act(c("YL", par, 320, 2), l1, 1.0, -float(OFF))
        else:
            cp(half("AOU", 0), l1)
            ts(val, l1, OFF - 0.5, A.is_ge, -131072.0, A.mult)
            act(half("APR", 0), l1, 32.0, -432.0)
            total(c("P0", OFF, 352), statics, stop=False)
            mms([(c("P0", OFF, 352, 2), lane("SS", 7), c("C4K"), False, False)])
            sizes(0)
            act(c("ST", OFF, 352), c("P0", OFF, 352), 1.0 / 1024)
        if not last:
            mms([(c("P5", 234, 235), ID, c("C155"), True, True), (c("P5", 224, 234), c("ALL1", 0, 128), c("inj"), True, True)])
            act(c("jk"), c("P5", 224, 235), total=c("CC", 0, 1))
            act(c("CC", 1, 2), c("CC", 0, 1), 1.0, 32 * ROUND)
            act(c("CC", 2, 3), c("CC", 1, 2), -64.0, 2048 * ROUND)
            act(c("CC", 3, 4), c("CC", 0, 1), 64.0, c("CC", 2, 3), F.Identity)
            inc = c("CC", 3, 4)
            cur[0] = 1 - par
            act(c("TH", 0, 160, 16), c("th64"), 1.0, inc, F.Identity)
            prep(t + 1)

    dma("Y", T.yl[:, :], ap(c("YL")), "d_yl", [c("YL")], [], 1.8)
    act(c("YD"), c("CL%d" % (RO - 1)), 1.0, 7.5)
    dma("S", T.yd[:, :], ap(c("YD")), "d_yd", [c("YD")], [], 1.6)
    dma("Y", T.yz[:, :], ap(c("Z3", 16, 176)), "d_yz", [c("Z3", 16, 176)], [], 1.6)

    if not ORDER:
        ORDER.extend(schedule(ops))
    order = ORDER

    count = {q: 0 for q in "VSTG"}
    clock = {q: {} for q in "VSTGY"}
    token = [None] * len(ops)
    sent = 0
    seen = {}
    for k, q in order:
        d = ops[k]
        for name in d["banks"]:
            d["preds"].update({p: True for q2, p in seen.setdefault(name, {}).items() if q2 != q})
            seen[name][q] = k
        if d["q"] == "E":
            d["calls"] = [d["calls"][q]]
        if q == "A":
            token[k] = (d["sem"], d["amount"], {d["sem"]: d["amount"]})
            continue
        ck, best = clock[q], {}
        for p, hard in d["preds"].items():
            if hard:
                s, v, kk = token[p]
                if ck.get(s, 0) < v and best.get(s, (0, None))[0] < v:
                    best[s] = (v, kk)
        for s in list(best):
            v = best[s][0]
            if any(s2 != s and k2.get(s, 0) >= v for s2, (v2, k2) in best.items()):
                del best[s]
        for s, (v, kk) in best.items():
            queue[q].wait_ge(T.sem[s], v)
            for s2, v2 in kk.items():
                ck[s2] = max(ck.get(s2, 0), v2)
        for call in d["calls"]:
            if "sem" in d:
                call().then_inc(T.sem[d["sem"]], 16)
            elif "sent" in d:
                call()
                sent += d["sent"]
            else:
                count[q] += 1
                call().then_inc(T.sem["s" + q], 1)
        kk = dict(ck)
        if "sem" in d:
            kk[d["sem"]] = 16
            token[k] = (d["sem"], 16, kk)
        elif "sent" not in d:
            kk["s" + q] = count[q]
            token[k] = ("s" + q, count[q], kk)
    g.wait_ge(T.sem.loc, sent)
    for s in ("d_yl", "d_yd", "d_yz"):
        g.wait_ge(T.sem[s], 16)
    for q in "VSTG":
        if clock["G"].get("s" + q, 0) < count[q]:
            g.wait_ge(T.sem["s" + q], count[q])
